import numpy as np
import ml_dtypes


def mxq(x, axis, fmt="e4m3"):
    dtype, down = {"e4m3": (ml_dtypes.float8_e4m3fn, 7), "e5m2": (ml_dtypes.float8_e5m2, 14)}[fmt]
    v = np.moveaxis(np.asarray(x, np.float32).astype(ml_dtypes.bfloat16).astype(np.float64), axis, -1)
    blocks = v.reshape(v.shape[:-1] + (-1, 32))
    amax = np.abs(blocks).max(-1, keepdims=True)
    byte = np.maximum(np.where(amax > 0, np.frexp(amax)[1] - 1 + 127, 0) - down, 1)
    scale = np.exp2(byte - 127.0)
    codes = (blocks / scale).astype(np.float32).astype(dtype).astype(np.float64)
    return np.moveaxis((codes * scale).reshape(v.shape), -1, axis)


WIDE = False


def mx_kscale(k):
    if not WIDE:
        return np.ones(k)
    levels = np.array([10, -10, 5, -5, 0])
    if k % 512:
        return np.exp2(np.random.permutation(np.resize(levels, k // 32))).repeat(32)
    a = np.empty((k // 512, 16))
    for p in range(k // 512):
        a[p, :8] = np.random.permutation(np.resize(levels, 8))
        for g in range(8):
            far = levels[np.abs(levels - a[p, g]) >= 10]
            a[p, g + 8] = far[np.random.randint(len(far))]
    return np.exp2(a.ravel()).repeat(32)


def f64(x):
    return np.asarray(x).astype(np.float64)


def striped(idx):
    return np.tile(idx.reshape(-1, 16).T, (8, 1)).astype(np.uint16)


def unstriped(offs):
    return offs[:16].T.reshape(-1).astype(np.int64)


E2M1 = np.array([0.0, 0.5, 1.0, 1.5, 2.0, 3.0, 4.0, 6.0, -0.0, -0.5, -1.0, -1.5, -2.0, -3.0, -4.0, -6.0])


def pack_weight(w, fmt):
    k, n = w.shape
    w = f64(np.asarray(w, np.float32).astype(ml_dtypes.bfloat16)).reshape(k // 32, 32, n)
    amax = np.abs(w).max(1)
    if fmt == "e4m3":
        byte = np.frexp(amax)[1] - 1 + 127 - 7
    else:
        mant, ex = np.frexp(amax / 6.0)
        byte = np.where(mant > 0.5, ex, ex - 1) + 127
    byte = np.clip(np.where(amax > 0, byte, 1), 1, 254)
    scaled = (w * np.exp2(127.0 - byte)[:, None, :]).reshape(k, n).astype(np.float32)
    by_word = np.ascontiguousarray(scaled.reshape(k // 512, 128, 4, n).transpose(0, 1, 3, 2))
    if fmt == "e4m3":
        words = by_word.astype(ml_dtypes.float8_e4m3fn).view(np.uint8)
    else:
        c = by_word.astype(ml_dtypes.float4_e2m1fn).view(np.uint8) & 0xF
        words = (c[..., 0::2] | (c[..., 1::2] << 4)).reshape(k // 512, 128, 2 * n)
    return np.ascontiguousarray(words), np.ascontiguousarray(byte.astype(np.uint8).reshape(k // 512, 16, n))


def unpack_weight(words, scales, fmt):
    g, _, n = scales.shape
    words = np.ascontiguousarray(words).reshape(g, 128, n, -1)
    if fmt == "e4m3":
        vals = words.view(ml_dtypes.float8_e4m3fn).astype(np.float64)
    else:
        nib = np.empty((g, 128, n, 4), np.uint8)
        nib[..., 0::2] = words & 0xF
        nib[..., 1::2] = words >> 4
        vals = E2M1[nib]
    vals = vals * np.repeat(np.exp2(scales.astype(np.float64) - 127.0), 8, axis=1)[..., None]
    return vals.transpose(0, 1, 3, 2).reshape(g * 512, n)


def gelu(v):
    return 0.5 * v * (1.0 + np.tanh(np.sqrt(2.0 / np.pi) * (v + 0.044715 * v**3)))


K, H, N, T, S, P = 1024, 1024, 512, 4096, 1024, 512

def setup_inputs():
    n = np.random.standard_normal
    s = mx_kscale(K)[:, None]
    u = mx_kscale(H)[:, None]
    tab_words, tab_scales = pack_weight(n((K, T)) * s, "e4m3")
    w1_words, w1_scales = pack_weight(n((K, H)) / np.sqrt(K) / s, "e2m1")
    w2 = n((K, H)) / np.sqrt(K) / s * u.T
    w3 = 0.4 * n((H, N)) / np.sqrt(H) / u
    w4_words, w4_scales = pack_weight(0.35 * n((H, N)) / np.sqrt(H) / u, "e4m3")
    return {
        "tab_words": tab_words, "tab_scales": tab_scales,
        "offs": striped(np.random.permutation(T)[:S]),
        "pos1": striped(np.random.permutation(S)[:P]),
        "pos2": striped(np.random.permutation(S)[:P]),
        "pos3": striped(np.random.permutation(S)[:P]),
        "w1_words": w1_words, "w1_scales": w1_scales,
        "w2": w2.astype(np.float32),
        "w3": w3.astype(np.float32),
        "w4_words": w4_words, "w4_scales": w4_scales,
        "prior": (n((H, P)) * u).astype(np.float32),
    }

def reference(tab_words, tab_scales, offs, pos1, pos2, pos3, w1_words, w1_scales,
              w2, w3, w4_words, w4_scales, prior):
    v = unpack_weight(tab_words, tab_scales, "e4m3")[:, unstriped(offs)]
    w1 = unpack_weight(w1_words, w1_scales, "e2m1")
    w4 = unpack_weight(w4_words, w4_scales, "e4m3")
    x1 = w1.T @ v
    x2 = (mxq(f64(w2), 0, "e4m3").T @ v) * (1.0 / (1.0 + np.exp(-x1)))
    z = np.maximum(np.square(x1[:, unstriped(pos1)]) * x2[:, unstriped(pos2)],
                   x2[:, unstriped(pos3)])
    y = (mxq(f64(w3), 0, "e4m3").T @ mxq(z, 0, "e4m3")
              + w4.T @ mxq(f64(prior), 0, "e4m3"))
    return np.sin(y)

@@ -1,0 +1,376 @@
+from contextlib import ExitStack
+
+import concourse.mybir as mybir
+
+K, H, N, T, S, M = 1024, 1024, 512, 4096, 1024, 512
+FLOPS = 2 * (2 * K * H * S + 2 * H * N * M)
+
+F32 = mybir.dt.float32
+BF16 = mybir.dt.bfloat16
+I32 = mybir.dt.int32
+U32 = mybir.dt.uint32
+U16 = mybir.dt.uint16
+U8 = mybir.dt.uint8
+FP8X4 = mybir.dt.float8_e4m3fn_x4
+FP4X4 = mybir.dt.float4_e2m1fn_x4
+ACT = mybir.ActivationFunctionType
+ALU = mybir.AluOpType
+
+P = 128
+PASSES = 2
+BANK = 512
+ROW_TILES = 8
+CHUNK = 256
+
+
+def tile_list_layering_chain_features_kernel(
+    tc, tab_words, tab_scales, offs, pos1, pos2, pos3, w1_words, w1_scales,
+    w2, w3, w4_words, w4_scales, prior, out
+):
+    nc = tc.nc
+    with ExitStack() as ctx:
+        lists = ctx.enter_context(tc.tile_pool(name="lists", bufs=1))
+        keep = ctx.enter_context(tc.tile_pool(name="keep", bufs=1))
+        big = ctx.enter_context(tc.tile_pool(name="big", bufs=1))
+        work = ctx.enter_context(tc.tile_pool(name="work", bufs=3))
+        psum = ctx.enter_context(tc.psum_pool(name="psum", bufs=4))
+
+        KB = 1024
+        tab_s = big.tile([P, T], U8, name="tab_s", align_bytes=64, offset=53 * KB)
+        nc.vector.memset(tab_s[:].bitcast(I32), 0)
+        warm = big.tile([P, 8], F32, name="warm", align_bytes=64, offset=18 * KB)
+        nc.vector.memset(warm[:], 0.0)
+        warm_out = keep.tile([P, 8], F32, name="warm_out")
+        nc.scalar.activation(warm_out[:], warm[:], ACT.Sigmoid)
+        w1_s_raw = keep.tile([P, PASSES, H // 4], I32, name="w1_s_raw")
+        nc.gpsimd.memset(w1_s_raw[:], 0)
+        v_s1 = keep.tile([P, S], U8, name="v_s1", align_bytes=64)
+        nc.vector.memset(v_s1[:].bitcast(I32), 0)
+
+        idx = lists.tile([P, S // 16], U16, name="idx")
+        p1 = lists.tile([P, M // 16], U16, name="p1")
+        p2 = lists.tile([P, M // 16], U16, name="p2")
+        p3 = lists.tile([P, M // 16], U16, name="p3")
+        nc.sync.dma_start(idx[:], offs)
+        nc.sync.dma_start(p1[:], pos1)
+        nc.sync.dma_start(p2[:], pos2)
+        nc.sync.dma_start(p3[:], pos3)
+        for q in range(4):
+            nc.gpsimd.dma_start(
+                w1_s_raw[32 * q : 32 * q + 4, :, :],
+                w1_scales[:, 4 * q : 4 * q + 4, :].bitcast(I32).rearrange("a q n -> q a n"),
+            )
+        tab_w = []
+        for a in range(PASSES):
+            words = big.tile([P, T], I32, name="tab_w%d" % a, align_bytes=64, offset=18 * KB * a)
+            nc.sync.dma_start(words[:], tab_words[a].rearrange("p t i -> p (t i)").bitcast(I32))
+            tab_w.append(words)
+            if a == 0:
+                for q in range(4):
+                    nc.sync.dma_start(
+                        tab_s[32 * q : 32 * q + 4, :].bitcast(I32),
+                        tab_scales[0, 4 * q : 4 * q + 4, :].bitcast(I32),
+                    )
+                nc.sync.dma_start(tab_s[4:P:8, :].bitcast(I32), tab_scales[1].bitcast(I32))
+
+        v_s0 = keep.tile([P, S], U8, name="v_s0", align_bytes=64)
+        nc.vector.tensor_copy(v_s0[:], tab_s[:].indirect(idx[:]))
+        for q in range(4):
+            nc.scalar.dma_start(
+                v_s1[32 * q : 32 * q + 4, :].bitcast(I32), v_s0[32 * q + 4 : 32 * q + 32 : 8, :].bitcast(I32)
+            )
+        w1_raw = big.tile([P, PASSES, H // 2], I32, name="w1_raw", align_bytes=64, offset=50 * KB)
+        nc.sync.dma_start(w1_raw[:], w1_words.bitcast(I32).rearrange("a p c -> p a c"))
+        v_s = [v_s0, v_s1]
+        v_w = {}
+
+        def gather_words(a, h):
+            if (a, h) == (0, 1):
+                tile = big.tile([P, BANK], U32, name="v_w01", align_bytes=64, offset=56 * KB)
+            else:
+                tile = keep.tile([P, BANK], U32, name="v_w%d%d" % (a, h), align_bytes=64)
+            nc.vector.tensor_copy(tile[:], tab_w[a][:].bitcast(U32).indirect(idx[:, 32 * h : 32 * (h + 1)]))
+            v_w[a, h] = tile
+
+        w1_w, w1_s = {}, {}
+
+        def order_w1_scales(a, b):
+            tile = big.tile([P, BANK], U8, name="w1_s%d%d" % (a, b), align_bytes=64, offset=BANK * (2 * b + a))
+            nc.vector.tensor_copy(
+                tile[:].bitcast(I32).rearrange("p (t g w) -> p t g w", t=4, w=2),
+                w1_s_raw[:, a, 128 * b : 128 * (b + 1)].rearrange("p (g t w) -> p t g w", t=4, w=2),
+            )
+            w1_s[a, b] = tile
+
+        def order_w1_words(a, b):
+            tile = keep.tile([P, BANK // 2], I32, name="w1_w%d%d" % (a, b), align_bytes=64)
+            nc.vector.tensor_copy(
+                tile[:].rearrange("p (t g w) -> p t g w", t=4, w=4),
+                w1_raw[:, a, 256 * b : 256 * (b + 1)].rearrange("p (g t w) -> p t g w", t=4, w=4),
+            )
+            w1_w[a, b] = tile
+
+        w2_raw = {}
+
+        def load_w2(b):
+            for a in range(PASSES):
+                rows = big.tile(
+                    [P, 4, BANK], F32, name="w2_raw%d%d" % (b, a), align_bytes=64, offset=KB * (2 + 16 * b + 8 * a)
+                )
+                nc.sync.dma_start(
+                    rows[:],
+                    w2[512 * a : 512 * (a + 1), 512 * b : 512 * (b + 1)].rearrange("(p i) c -> p i c", i=4),
+                )
+                w2_raw[b, a] = rows
+
+        gather_words(0, 0)
+        gather_words(0, 1)
+        load_w2(0)
+        for b in range(PASSES):
+            for a in range(PASSES):
+                order_w1_scales(a, b)
+        gather_words(1, 0)
+        for a in range(PASSES):
+            order_w1_words(a, 0)
+        gather_words(1, 1)
+        load_w2(1)
+        for a in range(PASSES):
+            order_w1_words(a, 1)
+
+        w3_raw = big.tile([P, PASSES, 4, N], F32, name="w3_raw", align_bytes=64, offset=35 * KB)
+        for b in range(PASSES):
+            rows = w3[512 * b : 512 * (b + 1), :].rearrange("(g t j) n -> t g j n", t=4, j=8)
+            for t in range(4):
+                nc.sync.dma_start(w3_raw[:, b, t, :], rows[t])
+        w4_s = big.tile([P, PASSES, N], U8, name="w4_s", align_bytes=64, offset=51 * KB)
+        nc.gpsimd.memset(w4_s[:].rearrange("p a n -> p (a n)").bitcast(I32), 0)
+        w4_w = big.tile([P, PASSES, N], I32, name="w4_w", align_bytes=64, offset=52 * KB)
+        nc.sync.dma_start(
+            w4_w[:], w4_words.rearrange("a p c i -> a p (c i)").bitcast(I32).rearrange("a p c -> p a c")
+        )
+        for q in range(4):
+            nc.sync.dma_start(
+                w4_s[32 * q : 32 * q + 4, :, :].bitcast(I32),
+                w4_scales[:, 4 * q : 4 * q + 4, :].bitcast(I32).rearrange("a q n -> q a n"),
+            )
+
+        x1_ps, u_ps, sq, sig, x2, g1 = {}, {}, {}, {}, {}, {}
+        w2_bf, w2_w, w2_s = {}, {}, {}
+        a4, c4 = {}, {}
+
+        def x1_product(i):
+            b, t = divmod(i, 4)
+            for h in range(2):
+                bank = psum.tile([P, BANK], F32, name="x1", tag="x1")
+                for a in range(PASSES):
+                    nc.tensor.matmul_mx(
+                        out=bank[:],
+                        lhsT=w1_w[a, b][:, 64 * t : 64 * (t + 1)].bitcast(FP4X4),
+                        lhsT_scale=w1_s[a, b][:, 128 * t : 128 * (t + 1)],
+                        rhs=v_w[a, h][:].bitcast(FP8X4),
+                        rhs_scale=v_s[a][:, BANK * h : BANK * (h + 1)],
+                        start=(a == 0),
+                        stop=(a == PASSES - 1),
+                    )
+                x1_ps[i, h] = bank
+
+        def square(i):
+            sq[i] = work.tile([P, S], F32, name="sq")
+            for h in range(2):
+                nc.scalar.activation(sq[i][:, BANK * h : BANK * (h + 1)], x1_ps[i, h][:], ACT.Square)
+
+        def sigmoid(i):
+            sig[i] = work.tile([P, S], F32, name="sig")
+            for h in range(2):
+                nc.scalar.activation(sig[i][:, BANK * h : BANK * (h + 1)], x1_ps[i, h][:], ACT.Sigmoid)
+
+        def cast_w2(i, a, on_vector):
+            b, t = divmod(i, 4)
+            if i not in w2_bf:
+                w2_bf[i] = work.tile([P, PASSES, BANK], BF16, name="w2_bf", align_bytes=64, bufs=5)
+            dst = w2_bf[i][:, a, :].rearrange("p (g u e i) -> p g u i e", u=2, e=4, i=4)
+            src = w2_raw[b, a][:].rearrange("p i (g t u e) -> p t g u i e", t=4, u=2, e=4)[:, t]
+            if on_vector:
+                nc.vector.tensor_copy(dst, src)
+            else:
+                nc.scalar.copy(dst, src)
+
+        def quantize_w2(i):
+            w2_w[i] = work.tile([P, PASSES * P], U32, name="w2_w", align_bytes=64)
+            w2_s[i] = work.tile([P, PASSES * P], U8, name="w2_s", align_bytes=64)
+            nc.vector.quantize_mx(
+                out=w2_w[i][:].bitcast(FP8X4),
+                scales=w2_s[i][:],
+                in_=w2_bf[i][:].rearrange("p a c -> p (a c)"),
+            )
+
+        def u_product(i):
+            for h in range(2):
+                bank = psum.tile([P, BANK], F32, name="u", tag="u")
+                for a in range(PASSES):
+                    nc.tensor.matmul_mx(
+                        out=bank[:],
+                        lhsT=w2_w[i][:, P * a : P * (a + 1)].bitcast(FP8X4),
+                        lhsT_scale=w2_s[i][:, P * a : P * (a + 1)],
+                        rhs=v_w[a, h][:].bitcast(FP8X4),
+                        rhs_scale=v_s[a][:, BANK * h : BANK * (h + 1)],
+                        start=(a == 0),
+                        stop=(a == PASSES - 1),
+                    )
+                u_ps[i, h] = bank
+
+        def gate(i):
+            x2[i] = work.tile([P, S], F32, name="x2", bufs=2)
+            for h in range(2):
+                cols = slice(BANK * h, BANK * (h + 1))
+                nc.vector.tensor_tensor(x2[i][:, cols], u_ps[i, h][:], sig[i][:, cols], ALU.mult)
+
+        def pick_deposit(i):
+            g1[i] = work.tile([P, M], F32, name="g1")
+            nc.vector.tensor_copy(g1[i][:], sq[i][:].indirect(p1[:]))
+
+        def pick_hop_and_withdrawal(i, lo, hi):
+            b, t = divmod(i, 4)
+            if b not in a4:
+                a4[b] = work.tile([P, 4, M], F32, name="a4", bufs=2)
+                c4[b] = work.tile([P, 4, M], F32, name="c4", bufs=2)
+            entries = slice(lo // 16, hi // 16)
+            nc.vector.tensor_copy(c4[b][:, t, lo:hi], x2[i][:].indirect(p3[:, entries]))
+            nc.vector.tensor_tensor(
+                a4[b][:, t, lo:hi], x2[i][:].indirect(p2[:, entries]), g1[i][:, lo:hi], ALU.mult
+            )
+
+        z_bf, z_w, z_s = {}, {}, {}
+
+        def larger(b, lo, hi):
+            z_bf[b, lo] = work.tile([P, hi - lo, 4], BF16, name="z_bf", align_bytes=64, bufs=2)
+            nc.vector.tensor_tensor(
+                z_bf[b, lo][:].rearrange("p (c e) t -> p c t e", e=4),
+                a4[b][:, :, lo:hi].rearrange("p t (c e) -> p c t e", e=4),
+                c4[b][:, :, lo:hi].rearrange("p t (c e) -> p c t e", e=4),
+                ALU.max,
+            )
+
+        def quantize(name, src, width):
+            words = keep.tile([P, width], U32, name=name + "_w", align_bytes=64)
+            scales = keep.tile([P, width], U8, name=name + "_s", align_bytes=64)
+            nc.vector.quantize_mx(out=words[:].bitcast(FP8X4), scales=scales[:], in_=src)
+            return words, scales
+
+        def quantize_z(b, lo):
+            tile = z_bf[b, lo]
+            z_w[b, lo], z_s[b, lo] = quantize(
+                "z%d_%d" % (b, lo), tile[:].rearrange("p m t -> p (m t)"), tile.shape[1]
+            )
+
+        late_bf, late_q = {}, {}
+        late_raw = [w3_raw]
+
+        def load_prior():
+            prior_raw = big.tile([P, PASSES, 4, M], F32, name="prior_raw", align_bytes=64, offset=2 * KB)
+            for b in range(PASSES):
+                nc.sync.dma_start(
+                    prior_raw[:, b, :, :], prior[512 * b : 512 * (b + 1), :].rearrange("(p t) m -> p t m", t=4)
+                )
+            late_raw.append(prior_raw)
+
+        def cast_late(n, half):
+            raw = late_raw[n // 2]
+            if n not in late_bf:
+                late_bf[n] = work.tile([P, BANK, 4], BF16, name="late_bf", align_bytes=64, bufs=2)
+            cols = slice(256 * half, 256 * (half + 1))
+            nc.scalar.copy(
+                late_bf[n][:, cols, :].rearrange("p (c e) t -> p c t e", e=4),
+                raw[:, n % 2, :, cols].rearrange("p t (c e) -> p c t e", e=4),
+            )
+
+        def quantize_late(n):
+            late_q[n] = quantize("late%d" % n, late_bf[n][:].rearrange("p c t -> p (c t)"), BANK)
+
+        x1_product(0)
+        square(0)
+        x1_product(1)
+        square(1)
+        sigmoid(0)
+        for t in range(4):
+            cast_w2(t, 0, True)
+        pick_deposit(0)
+        cast_w2(0, 1, True)
+        quantize_w2(0)
+        sigmoid(1)
+        for i in range(ROW_TILES):
+            nxt = i + 1
+            u_product(i)
+            if nxt < ROW_TILES:
+                if nxt >= 4:
+                    cast_w2(nxt, 0, False)
+                cast_w2(nxt, 1, False)
+                pick_deposit(nxt)
+                quantize_w2(nxt)
+            if nxt == 3:
+                load_prior()
+            if nxt + 1 < ROW_TILES:
+                x1_product(nxt + 1)
+                square(nxt + 1)
+                sigmoid(nxt + 1)
+            gate(i)
+            if 2 <= i < 6:
+                cast_late(i - 2, 0)
+                cast_late(i - 2, 1)
+            if 3 <= i < 7:
+                quantize_late(i - 3)
+            if i < ROW_TILES - 1:
+                pick_hop_and_withdrawal(i, 0, M)
+            if i == 3:
+                larger(0, 0, M)
+            if i == 4:
+                quantize_z(0, 0)
+
+        sin_warm = keep.tile([P, 8], F32, name="sin_warm")
+        nc.scalar.activation(sin_warm[:], sig[ROW_TILES - 1][:, S - 8 : S], ACT.Sin)
+
+        y_ps = {}
+        for lo in range(0, M, CHUNK):
+            cols = slice(lo, lo + CHUNK)
+            for c in range(N // P):
+                rows = slice(P * c, P * (c + 1))
+                tag = "x1" if lo == 0 else "u"
+                bank = psum.tile([P, CHUNK], F32, name=tag, tag=tag)
+                for b in range(PASSES):
+                    nc.tensor.matmul_mx(
+                        out=bank[:],
+                        lhsT=w4_w[:, b, rows].bitcast(FP8X4),
+                        lhsT_scale=w4_s[:, b, rows],
+                        rhs=late_q[2 + b][0][:, cols].bitcast(FP8X4),
+                        rhs_scale=late_q[2 + b][1][:, cols],
+                        start=(b == 0),
+                        stop=False,
+                    )
+                nc.tensor.matmul_mx(
+                    out=bank[:],
+                    lhsT=late_q[0][0][:, rows].bitcast(FP8X4),
+                    lhsT_scale=late_q[0][1][:, rows],
+                    rhs=z_w[0, 0][:, cols].bitcast(FP8X4),
+                    rhs_scale=z_s[0, 0][:, cols],
+                    start=False,
+                    stop=False,
+                )
+                y_ps[lo, c] = bank
+        for lo in range(0, M, CHUNK):
+            pick_hop_and_withdrawal(ROW_TILES - 1, lo, lo + CHUNK)
+            larger(1, lo, lo + CHUNK)
+            quantize_z(1, lo)
+            for c in range(N // P):
+                rows = slice(P * c, P * (c + 1))
+                nc.tensor.matmul_mx(
+                    out=y_ps[lo, c][:],
+                    lhsT=late_q[1][0][:, rows].bitcast(FP8X4),
+                    lhsT_scale=late_q[1][1][:, rows],
+                    rhs=z_w[1, lo][:].bitcast(FP8X4),
+                    rhs_scale=z_s[1, lo][:],
+                    start=False,
+                    stop=True,
+                )
+                res = work.tile([P, CHUNK], F32, name="res", bufs=8)
+                nc.scalar.activation(res[:], y_ps[lo, c][:], ACT.Sin)
+                nc.sync.dma_start(out[rows, lo : lo + CHUNK], res[:])

@@ -36,9 +36,9 @@ def tile_list_layering_chain_features_kernel(
         psum = ctx.enter_context(tc.psum_pool(name="psum", bufs=4))
 
         KB = 1024
-        tab_s = big.tile([P, T], U8, name="tab_s", align_bytes=64, offset=53 * KB)
+        tab_s = big.tile([P, T], U8, name="tab_s", align_bytes=64, offset=58 * KB)
         nc.vector.memset(tab_s[:].bitcast(I32), 0)
-        warm = big.tile([P, 8], F32, name="warm", align_bytes=64, offset=18 * KB)
+        warm = big.tile([P, 8], F32, name="warm", align_bytes=64, offset=40 * KB)
         nc.vector.memset(warm[:], 0.0)
         warm_out = keep.tile([P, 8], F32, name="warm_out")
         nc.scalar.activation(warm_out[:], warm[:], ACT.Sigmoid)
@@ -62,7 +62,7 @@ def tile_list_layering_chain_features_kernel(
             )
         tab_w = []
         for a in range(PASSES):
-            words = big.tile([P, T], I32, name="tab_w%d" % a, align_bytes=64, offset=18 * KB * a)
+            words = big.tile([P, T], I32, name="tab_w%d" % a, align_bytes=64, offset=33 * KB * a)
             nc.sync.dma_start(words[:], tab_words[a].rearrange("p t i -> p (t i)").bitcast(I32))
             tab_w.append(words)
             if a == 0:
@@ -79,14 +79,14 @@ def tile_list_layering_chain_features_kernel(
             nc.scalar.dma_start(
                 v_s1[32 * q : 32 * q + 4, :].bitcast(I32), v_s0[32 * q + 4 : 32 * q + 32 : 8, :].bitcast(I32)
             )
-        w1_raw = big.tile([P, PASSES, H // 2], I32, name="w1_raw", align_bytes=64, offset=50 * KB)
+        w1_raw = big.tile([P, PASSES, H // 2], I32, name="w1_raw", align_bytes=64, offset=55 * KB)
         nc.sync.dma_start(w1_raw[:], w1_words.bitcast(I32).rearrange("a p c -> p a c"))
         v_s = [v_s0, v_s1]
         v_w = {}
 
         def gather_words(a, h):
-            if (a, h) == (0, 1):
-                tile = big.tile([P, BANK], U32, name="v_w01", align_bytes=64, offset=56 * KB)
+            if h == 1:
+                tile = big.tile([P, BANK], U32, name="v_w%d1" % a, align_bytes=64, offset=(60 - 5 * a) * KB)
             else:
                 tile = keep.tile([P, BANK], U32, name="v_w%d%d" % (a, h), align_bytes=64)
             nc.vector.tensor_copy(tile[:], tab_w[a][:].bitcast(U32).indirect(idx[:, 32 * h : 32 * (h + 1)]))
@@ -115,7 +115,7 @@ def tile_list_layering_chain_features_kernel(
         def load_w2(b):
             for a in range(PASSES):
                 rows = big.tile(
-                    [P, 4, BANK], F32, name="w2_raw%d%d" % (b, a), align_bytes=64, offset=KB * (2 + 16 * b + 8 * a)
+                    [P, 4, BANK], F32, name="w2_raw%d%d" % (b, a), align_bytes=64, offset=KB * ((2, 10), (34, 47))[b][a]
                 )
                 nc.sync.dma_start(
                     rows[:],
@@ -130,21 +130,20 @@ def tile_list_layering_chain_features_kernel(
             for a in range(PASSES):
                 order_w1_scales(a, b)
         gather_words(1, 0)
-        for a in range(PASSES):
-            order_w1_words(a, 0)
+        for b in range(PASSES):
+            for a in range(PASSES):
+                order_w1_words(a, b)
         gather_words(1, 1)
         load_w2(1)
-        for a in range(PASSES):
-            order_w1_words(a, 1)
 
-        w3_raw = big.tile([P, PASSES, 4, N], F32, name="w3_raw", align_bytes=64, offset=35 * KB)
+        w3_raw = big.tile([P, PASSES, 4, N], F32, name="w3_raw", align_bytes=64, offset=18 * KB)
         for b in range(PASSES):
             rows = w3[512 * b : 512 * (b + 1), :].rearrange("(g t j) n -> t g j n", t=4, j=8)
             for t in range(4):
                 nc.sync.dma_start(w3_raw[:, b, t, :], rows[t])
-        w4_s = big.tile([P, PASSES, N], U8, name="w4_s", align_bytes=64, offset=51 * KB)
+        w4_s = big.tile([P, PASSES, N], U8, name="w4_s", align_bytes=64, offset=42 * KB)
         nc.gpsimd.memset(w4_s[:].rearrange("p a n -> p (a n)").bitcast(I32), 0)
-        w4_w = big.tile([P, PASSES, N], I32, name="w4_w", align_bytes=64, offset=52 * KB)
+        w4_w = big.tile([P, PASSES, N], I32, name="w4_w", align_bytes=64, offset=43 * KB)
         nc.sync.dma_start(
             w4_w[:], w4_words.rearrange("a p c i -> a p (c i)").bitcast(I32).rearrange("a p c -> p a c")
         )
@@ -175,7 +174,10 @@ def tile_list_layering_chain_features_kernel(
                 x1_ps[i, h] = bank
 
         def square(i):
-            sq[i] = work.tile([P, S], F32, name="sq")
+            if i < 2:
+                sq[i] = big.tile([P, S], F32, name="sq%d" % i, align_bytes=64, offset=(62 + 4 * i) * KB)
+            else:
+                sq[i] = work.tile([P, S], F32, name="sq")
             for h in range(2):
                 nc.scalar.activation(sq[i][:, BANK * h : BANK * (h + 1)], x1_ps[i, h][:], ACT.Square)
 
@@ -186,8 +188,12 @@ def tile_list_layering_chain_features_kernel(
 
         def cast_w2(i, a, on_vector):
             b, t = divmod(i, 4)
-            if i not in w2_bf:
-                w2_bf[i] = work.tile([P, PASSES, BANK], BF16, name="w2_bf", align_bytes=64, bufs=5)
+            if a == 0 and 1 <= i <= 3:
+                w2_bf[i] = big.tile(
+                    [P, PASSES, BANK], BF16, name="w2_bf%d" % i, align_bytes=64, offset=(60 + 2 * i) * KB
+                )
+            elif a == 0:
+                w2_bf[i] = work.tile([P, PASSES, BANK], BF16, name="w2_bf", align_bytes=64)
             dst = w2_bf[i][:, a, :].rearrange("p (g u e i) -> p g u i e", u=2, e=4, i=4)
             src = w2_raw[b, a][:].rearrange("p i (g t u e) -> p t g u i e", t=4, u=2, e=4)[:, t]
             if on_vector:
@@ -229,15 +235,18 @@ def tile_list_layering_chain_features_kernel(
             g1[i] = work.tile([P, M], F32, name="g1")
             nc.vector.tensor_copy(g1[i][:], sq[i][:].indirect(p1[:]))
 
-        def pick_hop_and_withdrawal(i, lo, hi):
+        def pick_withdrawal(i, lo, hi):
+            b, t = divmod(i, 4)
+            if b not in c4:
+                c4[b] = work.tile([P, 4, M], F32, name="c4", bufs=2)
+            nc.vector.tensor_copy(c4[b][:, t, lo:hi], x2[i][:].indirect(p3[:, lo // 16 : hi // 16]))
+
+        def pick_hop(i, lo, hi):
             b, t = divmod(i, 4)
             if b not in a4:
                 a4[b] = work.tile([P, 4, M], F32, name="a4", bufs=2)
-                c4[b] = work.tile([P, 4, M], F32, name="c4", bufs=2)
-            entries = slice(lo // 16, hi // 16)
-            nc.vector.tensor_copy(c4[b][:, t, lo:hi], x2[i][:].indirect(p3[:, entries]))
             nc.vector.tensor_tensor(
-                a4[b][:, t, lo:hi], x2[i][:].indirect(p2[:, entries]), g1[i][:, lo:hi], ALU.mult
+                a4[b][:, t, lo:hi], x2[i][:].indirect(p2[:, lo // 16 : hi // 16]), g1[i][:, lo:hi], ALU.mult
             )
 
         z_bf, z_w, z_s = {}, {}, {}
@@ -245,9 +254,9 @@ def tile_list_layering_chain_features_kernel(
         def larger(b, lo, hi):
             z_bf[b, lo] = work.tile([P, hi - lo, 4], BF16, name="z_bf", align_bytes=64, bufs=2)
             nc.vector.tensor_tensor(
-                z_bf[b, lo][:].rearrange("p (c e) t -> p c t e", e=4),
-                a4[b][:, :, lo:hi].rearrange("p t (c e) -> p c t e", e=4),
-                c4[b][:, :, lo:hi].rearrange("p t (c e) -> p c t e", e=4),
+                z_bf[b, lo][:].rearrange("p (c e) t -> p c t e", e=2),
+                a4[b][:, :, lo:hi].rearrange("p t (c e) -> p c t e", e=2),
+                c4[b][:, :, lo:hi].rearrange("p t (c e) -> p c t e", e=2),
                 ALU.max,
             )
 
@@ -277,7 +286,9 @@ def tile_list_layering_chain_features_kernel(
         def cast_late(n, half):
             raw = late_raw[n // 2]
             if n not in late_bf:
-                late_bf[n] = work.tile([P, BANK, 4], BF16, name="late_bf", align_bytes=64, bufs=2)
+                late_bf[n] = big.tile(
+                    [P, BANK, 4], BF16, name="late_bf%d" % n, align_bytes=64, offset=(62 + 4 * (n % 2)) * KB
+                )
             cols = slice(256 * half, 256 * (half + 1))
             nc.scalar.copy(
                 late_bf[n][:, cols, :].rearrange("p (c e) t -> p c t e", e=4),
@@ -291,40 +302,38 @@ def tile_list_layering_chain_features_kernel(
         square(0)
         x1_product(1)
         square(1)
-        sigmoid(0)
-        for t in range(4):
-            cast_w2(t, 0, True)
+        cast_w2(0, 0, True)
         pick_deposit(0)
         cast_w2(0, 1, True)
         quantize_w2(0)
-        sigmoid(1)
+        pick_deposit(1)
         for i in range(ROW_TILES):
             nxt = i + 1
             u_product(i)
+            if i >= 2:
+                x1_product(i)
+                square(i)
+                pick_deposit(i)
+            sigmoid(i)
+            gate(i)
             if nxt < ROW_TILES:
-                if nxt >= 4:
-                    cast_w2(nxt, 0, False)
+                cast_w2(nxt, 0, False)
                 cast_w2(nxt, 1, False)
-                pick_deposit(nxt)
                 quantize_w2(nxt)
             if nxt == 3:
                 load_prior()
-            if nxt + 1 < ROW_TILES:
-                x1_product(nxt + 1)
-                square(nxt + 1)
-                sigmoid(nxt + 1)
-            gate(i)
-            if 2 <= i < 6:
-                cast_late(i - 2, 0)
-                cast_late(i - 2, 1)
-            if 3 <= i < 7:
-                quantize_late(i - 3)
-            if i < ROW_TILES - 1:
-                pick_hop_and_withdrawal(i, 0, M)
-            if i == 3:
-                larger(0, 0, M)
             if i == 4:
                 quantize_z(0, 0)
+            if 3 <= i < 7:
+                cast_late(i - 3, 0)
+                cast_late(i - 3, 1)
+            if i < ROW_TILES - 1:
+                pick_withdrawal(i, 0, M)
+                pick_hop(i, 0, M)
+            if 3 <= i < 7:
+                quantize_late(i - 3)
+            if i == 3:
+                larger(0, 0, M)
 
         sin_warm = keep.tile([P, 8], F32, name="sin_warm")
         nc.scalar.activation(sin_warm[:], sig[ROW_TILES - 1][:, S - 8 : S], ACT.Sin)
@@ -356,10 +365,16 @@ def tile_list_layering_chain_features_kernel(
                     stop=False,
                 )
                 y_ps[lo, c] = bank
+        last = ROW_TILES - 1
+        pick_withdrawal(last, 0, CHUNK)
+        pick_hop(last, 0, CHUNK)
+        pick_withdrawal(last, CHUNK, M)
+        larger(1, 0, CHUNK)
+        pick_hop(last, CHUNK, M)
+        quantize_z(1, 0)
+        larger(1, CHUNK, M)
+        quantize_z(1, CHUNK)
         for lo in range(0, M, CHUNK):
-            pick_hop_and_withdrawal(ROW_TILES - 1, lo, lo + CHUNK)
-            larger(1, lo, lo + CHUNK)
-            quantize_z(1, lo)
             for c in range(N // P):
                 rows = slice(P * c, P * (c + 1))
                 nc.tensor.matmul_mx(

@@ -21,6 +21,9 @@ PASSES = 2
 BANK = 512
 ROW_TILES = 8
 CHUNK = 256
+LATE_GATE = (3, 7)
+LATE0 = 3
+X2B = 2
 
 
 def tile_list_layering_chain_features_kernel(
@@ -36,11 +39,11 @@ def tile_list_layering_chain_features_kernel(
         psum = ctx.enter_context(tc.psum_pool(name="psum", bufs=4))
 
         KB = 1024
-        tab_s = big.tile([P, T], U8, name="tab_s", align_bytes=64, offset=58 * KB)
+        tab_s = big.tile([P, T], U8, name="tab_s", align_bytes=64, offset=60 * KB)
         nc.vector.memset(tab_s[:].bitcast(I32), 0)
-        warm = big.tile([P, 8], F32, name="warm", align_bytes=64, offset=40 * KB)
+        warm = big.tile([P, 32], F32, name="warm", align_bytes=64, offset=31 * KB - 64)
         nc.vector.memset(warm[:], 0.0)
-        warm_out = keep.tile([P, 8], F32, name="warm_out")
+        warm_out = keep.tile([P, 32], F32, name="warm_out")
         nc.scalar.activation(warm_out[:], warm[:], ACT.Sigmoid)
         w1_s_raw = keep.tile([P, PASSES, H // 4], I32, name="w1_s_raw")
         nc.gpsimd.memset(w1_s_raw[:], 0)
@@ -62,7 +65,7 @@ def tile_list_layering_chain_features_kernel(
             )
         tab_w = []
         for a in range(PASSES):
-            words = big.tile([P, T], I32, name="tab_w%d" % a, align_bytes=64, offset=33 * KB * a)
+            words = big.tile([P, T], I32, name="tab_w%d" % a, align_bytes=64, offset=31 * KB * a)
             nc.sync.dma_start(words[:], tab_words[a].rearrange("p t i -> p (t i)").bitcast(I32))
             tab_w.append(words)
             if a == 0:
@@ -72,21 +75,21 @@ def tile_list_layering_chain_features_kernel(
                         tab_scales[0, 4 * q : 4 * q + 4, :].bitcast(I32),
                     )
                 nc.sync.dma_start(tab_s[4:P:8, :].bitcast(I32), tab_scales[1].bitcast(I32))
+                w1_raw = big.tile([P, PASSES, H // 2], I32, name="w1_raw", align_bytes=64, offset=27 * KB)
+                nc.sync.dma_start(w1_raw[:], w1_words.bitcast(I32).rearrange("a p c -> p a c"))
 
         v_s0 = keep.tile([P, S], U8, name="v_s0", align_bytes=64)
         nc.vector.tensor_copy(v_s0[:], tab_s[:].indirect(idx[:]))
         for q in range(4):
-            nc.scalar.dma_start(
+            nc.sync.dma_start(
                 v_s1[32 * q : 32 * q + 4, :].bitcast(I32), v_s0[32 * q + 4 : 32 * q + 32 : 8, :].bitcast(I32)
             )
-        w1_raw = big.tile([P, PASSES, H // 2], I32, name="w1_raw", align_bytes=64, offset=55 * KB)
-        nc.sync.dma_start(w1_raw[:], w1_words.bitcast(I32).rearrange("a p c -> p a c"))
         v_s = [v_s0, v_s1]
         v_w = {}
 
         def gather_words(a, h):
-            if h == 1:
-                tile = big.tile([P, BANK], U32, name="v_w%d1" % a, align_bytes=64, offset=(60 - 5 * a) * KB)
+            if (a, h) == (0, 1):
+                tile = big.tile([P, BANK], U32, name="v_w01", align_bytes=64, offset=62 * KB)
             else:
                 tile = keep.tile([P, BANK], U32, name="v_w%d%d" % (a, h), align_bytes=64)
             nc.vector.tensor_copy(tile[:], tab_w[a][:].bitcast(U32).indirect(idx[:, 32 * h : 32 * (h + 1)]))
@@ -94,28 +97,26 @@ def tile_list_layering_chain_features_kernel(
 
         w1_w, w1_s = {}, {}
 
-        def order_w1_scales(a, b):
-            tile = big.tile([P, BANK], U8, name="w1_s%d%d" % (a, b), align_bytes=64, offset=BANK * (2 * b + a))
+        def order_w1_scales(a):
+            w1_s[a] = big.tile([P, H], U8, name="w1_s%d" % a, align_bytes=64, offset=KB * a)
             nc.vector.tensor_copy(
-                tile[:].bitcast(I32).rearrange("p (t g w) -> p t g w", t=4, w=2),
-                w1_s_raw[:, a, 128 * b : 128 * (b + 1)].rearrange("p (g t w) -> p t g w", t=4, w=2),
+                w1_s[a][:].bitcast(I32).rearrange("p (b t g w) -> p b t g w", b=2, t=4, w=2),
+                w1_s_raw[:, a, :].rearrange("p (b g t w) -> p b t g w", b=2, t=4, w=2),
             )
-            w1_s[a, b] = tile
 
-        def order_w1_words(a, b):
-            tile = keep.tile([P, BANK // 2], I32, name="w1_w%d%d" % (a, b), align_bytes=64)
+        def order_w1_words(a):
+            w1_w[a] = big.tile([P, H // 2], I32, name="w1_w%d" % a, align_bytes=64, offset=(2 + 2 * a) * KB)
             nc.vector.tensor_copy(
-                tile[:].rearrange("p (t g w) -> p t g w", t=4, w=4),
-                w1_raw[:, a, 256 * b : 256 * (b + 1)].rearrange("p (g t w) -> p t g w", t=4, w=4),
+                w1_w[a][:].rearrange("p (b t g w) -> p b t g w", b=2, t=4, w=4),
+                w1_raw[:, a, :].rearrange("p (b g t w) -> p b t g w", b=2, t=4, w=4),
             )
-            w1_w[a, b] = tile
 
         w2_raw = {}
 
         def load_w2(b):
             for a in range(PASSES):
                 rows = big.tile(
-                    [P, 4, BANK], F32, name="w2_raw%d%d" % (b, a), align_bytes=64, offset=KB * ((2, 10), (34, 47))[b][a]
+                    [P, 4, BANK], F32, name="w2_raw%d%d" % (b, a), align_bytes=64, offset=KB * ((53, 6), (32, 45))[b][a]
                 )
                 nc.sync.dma_start(
                     rows[:],
@@ -126,24 +127,21 @@ def tile_list_layering_chain_features_kernel(
         gather_words(0, 0)
         gather_words(0, 1)
         load_w2(0)
-        for b in range(PASSES):
-            for a in range(PASSES):
-                order_w1_scales(a, b)
+        for a in range(PASSES):
+            order_w1_scales(a)
+            order_w1_words(a)
         gather_words(1, 0)
-        for b in range(PASSES):
-            for a in range(PASSES):
-                order_w1_words(a, b)
         gather_words(1, 1)
         load_w2(1)
 
-        w3_raw = big.tile([P, PASSES, 4, N], F32, name="w3_raw", align_bytes=64, offset=18 * KB)
+        w3_raw = big.tile([P, PASSES, 4, N], F32, name="w3_raw", align_bytes=64, offset=16 * KB)
         for b in range(PASSES):
             rows = w3[512 * b : 512 * (b + 1), :].rearrange("(g t j) n -> t g j n", t=4, j=8)
             for t in range(4):
                 nc.sync.dma_start(w3_raw[:, b, t, :], rows[t])
-        w4_s = big.tile([P, PASSES, N], U8, name="w4_s", align_bytes=64, offset=42 * KB)
+        w4_s = big.tile([P, PASSES, N], U8, name="w4_s", align_bytes=64, offset=40 * KB)
         nc.gpsimd.memset(w4_s[:].rearrange("p a n -> p (a n)").bitcast(I32), 0)
-        w4_w = big.tile([P, PASSES, N], I32, name="w4_w", align_bytes=64, offset=43 * KB)
+        w4_w = big.tile([P, PASSES, N], I32, name="w4_w", align_bytes=64, offset=41 * KB)
         nc.sync.dma_start(
             w4_w[:], w4_words.rearrange("a p c i -> a p (c i)").bitcast(I32).rearrange("a p c -> p a c")
         )
@@ -158,14 +156,13 @@ def tile_list_layering_chain_features_kernel(
         a4, c4 = {}, {}
 
         def x1_product(i):
-            b, t = divmod(i, 4)
             for h in range(2):
                 bank = psum.tile([P, BANK], F32, name="x1", tag="x1")
                 for a in range(PASSES):
                     nc.tensor.matmul_mx(
                         out=bank[:],
-                        lhsT=w1_w[a, b][:, 64 * t : 64 * (t + 1)].bitcast(FP4X4),
-                        lhsT_scale=w1_s[a, b][:, 128 * t : 128 * (t + 1)],
+                        lhsT=w1_w[a][:, 64 * i : 64 * (i + 1)].bitcast(FP4X4),
+                        lhsT_scale=w1_s[a][:, P * i : P * (i + 1)],
                         rhs=v_w[a, h][:].bitcast(FP8X4),
                         rhs_scale=v_s[a][:, BANK * h : BANK * (h + 1)],
                         start=(a == 0),
@@ -173,51 +170,72 @@ def tile_list_layering_chain_features_kernel(
                     )
                 x1_ps[i, h] = bank
 
-        def square(i):
-            if i < 2:
-                sq[i] = big.tile([P, S], F32, name="sq%d" % i, align_bytes=64, offset=(62 + 4 * i) * KB)
-            else:
+        def square(i, h):
+            if h == 0 and i < 2:
+                sq[i] = big.tile([P, S], F32, name="sq%d" % i, align_bytes=64, offset=(64 + 6 * i) * KB)
+            elif h == 0:
                 sq[i] = work.tile([P, S], F32, name="sq")
-            for h in range(2):
-                nc.scalar.activation(sq[i][:, BANK * h : BANK * (h + 1)], x1_ps[i, h][:], ACT.Square)
+            nc.scalar.activation(sq[i][:, BANK * h : BANK * (h + 1)], x1_ps[i, h][:], ACT.Square)
 
         def sigmoid(i):
             sig[i] = work.tile([P, S], F32, name="sig")
             for h in range(2):
                 nc.scalar.activation(sig[i][:, BANK * h : BANK * (h + 1)], x1_ps[i, h][:], ACT.Sigmoid)
 
-        def cast_w2(i, a, on_vector):
-            b, t = divmod(i, 4)
-            if a == 0 and 1 <= i <= 3:
-                w2_bf[i] = big.tile(
-                    [P, PASSES, BANK], BF16, name="w2_bf%d" % i, align_bytes=64, offset=(60 + 2 * i) * KB
-                )
-            elif a == 0:
-                w2_bf[i] = work.tile([P, PASSES, BANK], BF16, name="w2_bf", align_bytes=64)
-            dst = w2_bf[i][:, a, :].rearrange("p (g u e i) -> p g u i e", u=2, e=4, i=4)
+        x1_sb, s2, s3 = {}, {}, {}
+
+        def picked_sigmoids(i):
+            x1_sb[i] = work.tile([P, S], F32, name="sig")
+            for h in range(2):
+                nc.scalar.copy(x1_sb[i][:, BANK * h : BANK * (h + 1)], x1_ps[i, h][:])
+            s2[i] = work.tile([P, M], F32, name="s2", bufs=2)
+            nc.scalar.activation(s2[i][:], x1_sb[i][:].indirect(p2[:]), ACT.Sigmoid)
+            s3[i] = work.tile([P, M], F32, name="s3", bufs=2)
+            nc.scalar.activation(s3[i][:], x1_sb[i][:].indirect(p3[:]), ACT.Sigmoid)
+
+        def copy_u(i):
+            x2[i] = work.tile([P, S], F32, name="x2", bufs=X2B)
+            for h in range(2):
+                nc.scalar.copy(x2[i][:, BANK * h : BANK * (h + 1)], u_ps[i, h][:])
+
+        def stage_w2(b, a, t0, t1, offset=None):
+            shape = [P, t1 - t0, BANK]
+            if offset is None:
+                tile = work.tile(shape, BF16, name="w2_bf", align_bytes=64, bufs=2)
+            else:
+                tile = big.tile(shape, BF16, name="w2_bf%d" % t0, align_bytes=64, offset=offset)
+            for t in range(t0, t1):
+                w2_bf[b, a, t] = (tile, t - t0)
+
+        def cast_w2(b, a, t, on_vector):
+            tile, row = w2_bf[b, a, t]
+            dst = tile[:, row, :].rearrange("p (g u e i) -> p g u i e", u=2, e=4, i=4)
             src = w2_raw[b, a][:].rearrange("p i (g t u e) -> p t g u i e", t=4, u=2, e=4)[:, t]
             if on_vector:
                 nc.vector.tensor_copy(dst, src)
             else:
                 nc.scalar.copy(dst, src)
 
-        def quantize_w2(i):
-            w2_w[i] = work.tile([P, PASSES * P], U32, name="w2_w", align_bytes=64)
-            w2_s[i] = work.tile([P, PASSES * P], U8, name="w2_s", align_bytes=64)
+        def quantize_w2(b, a, t0, t1):
+            if t0 == 0:
+                w2_w[b, a] = keep.tile([P, BANK], U32, name="w2_w%d%d" % (b, a), align_bytes=64)
+                w2_s[b, a] = keep.tile([P, BANK], U8, name="w2_s%d%d" % (b, a), align_bytes=64)
+            tile, row = w2_bf[b, a, t0]
             nc.vector.quantize_mx(
-                out=w2_w[i][:].bitcast(FP8X4),
-                scales=w2_s[i][:],
-                in_=w2_bf[i][:].rearrange("p a c -> p (a c)"),
+                out=w2_w[b, a][:, P * t0 : P * t1].bitcast(FP8X4),
+                scales=w2_s[b, a][:, P * t0 : P * t1],
+                in_=tile[:, row : row + t1 - t0, :].rearrange("p t c -> p (t c)"),
             )
 
         def u_product(i):
+            b, t = divmod(i, 4)
             for h in range(2):
                 bank = psum.tile([P, BANK], F32, name="u", tag="u")
                 for a in range(PASSES):
                     nc.tensor.matmul_mx(
                         out=bank[:],
-                        lhsT=w2_w[i][:, P * a : P * (a + 1)].bitcast(FP8X4),
-                        lhsT_scale=w2_s[i][:, P * a : P * (a + 1)],
+                        lhsT=w2_w[b, a][:, P * t : P * (t + 1)].bitcast(FP8X4),
+                        lhsT_scale=w2_s[b, a][:, P * t : P * (t + 1)],
                         rhs=v_w[a, h][:].bitcast(FP8X4),
                         rhs_scale=v_s[a][:, BANK * h : BANK * (h + 1)],
                         start=(a == 0),
@@ -226,20 +244,30 @@ def tile_list_layering_chain_features_kernel(
                 u_ps[i, h] = bank
 
         def gate(i):
-            x2[i] = work.tile([P, S], F32, name="x2", bufs=2)
+            x2[i] = work.tile([P, S], F32, name="x2", bufs=X2B)
             for h in range(2):
                 cols = slice(BANK * h, BANK * (h + 1))
                 nc.vector.tensor_tensor(x2[i][:, cols], u_ps[i, h][:], sig[i][:, cols], ALU.mult)
 
         def pick_deposit(i):
-            g1[i] = work.tile([P, M], F32, name="g1")
-            nc.vector.tensor_copy(g1[i][:], sq[i][:].indirect(p1[:]))
+            if i < 2:
+                g1[i] = big.tile([P, M], F32, name="g1_%d" % i, align_bytes=64, offset=(53, 67)[i] * KB)
+            else:
+                g1[i] = work.tile([P, M], F32, name="g1")
+            if i in LATE_GATE:
+                nc.vector.tensor_tensor(g1[i][:], sq[i][:].indirect(p1[:]), s2[i][:], ALU.mult)
+            else:
+                nc.vector.tensor_copy(g1[i][:], sq[i][:].indirect(p1[:]))
 
         def pick_withdrawal(i, lo, hi):
             b, t = divmod(i, 4)
             if b not in c4:
                 c4[b] = work.tile([P, 4, M], F32, name="c4", bufs=2)
-            nc.vector.tensor_copy(c4[b][:, t, lo:hi], x2[i][:].indirect(p3[:, lo // 16 : hi // 16]))
+            picked = x2[i][:].indirect(p3[:, lo // 16 : hi // 16])
+            if i in LATE_GATE:
+                nc.vector.tensor_tensor(c4[b][:, t, lo:hi], picked, s3[i][:, lo:hi], ALU.mult)
+            else:
+                nc.vector.tensor_copy(c4[b][:, t, lo:hi], picked)
 
         def pick_hop(i, lo, hi):
             b, t = divmod(i, 4)
@@ -252,7 +280,7 @@ def tile_list_layering_chain_features_kernel(
         z_bf, z_w, z_s = {}, {}, {}
 
         def larger(b, lo, hi):
-            z_bf[b, lo] = work.tile([P, hi - lo, 4], BF16, name="z_bf", align_bytes=64, bufs=2)
+            z_bf[b, lo] = work.tile([P, hi - lo, 4], BF16, name="z_bf", align_bytes=64, bufs=1)
             nc.vector.tensor_tensor(
                 z_bf[b, lo][:].rearrange("p (c e) t -> p c t e", e=2),
                 a4[b][:, :, lo:hi].rearrange("p t (c e) -> p c t e", e=2),
@@ -273,70 +301,89 @@ def tile_list_layering_chain_features_kernel(
             )
 
         late_bf, late_q = {}, {}
-        late_raw = [w3_raw]
+        late_raw = [w3_raw[:, 0], w3_raw[:, 1]]
 
         def load_prior():
-            prior_raw = big.tile([P, PASSES, 4, M], F32, name="prior_raw", align_bytes=64, offset=2 * KB)
             for b in range(PASSES):
-                nc.sync.dma_start(
-                    prior_raw[:, b, :, :], prior[512 * b : 512 * (b + 1), :].rearrange("(p t) m -> p t m", t=4)
-                )
-            late_raw.append(prior_raw)
+                rows = big.tile([P, 4, M], F32, name="prior_raw%d" % b, align_bytes=64, offset=(53, 6)[b] * KB)
+                nc.sync.dma_start(rows[:], prior[512 * b : 512 * (b + 1), :].rearrange("(p t) m -> p t m", t=4))
+                late_raw.append(rows[:])
 
         def cast_late(n, half):
-            raw = late_raw[n // 2]
+            raw = late_raw[n]
             if n not in late_bf:
                 late_bf[n] = big.tile(
-                    [P, BANK, 4], BF16, name="late_bf%d" % n, align_bytes=64, offset=(62 + 4 * (n % 2)) * KB
+                    [P, BANK, 4], BF16, name="late_bf%d" % n, align_bytes=64, offset=(64 + 6 * (n % 2)) * KB
                 )
             cols = slice(256 * half, 256 * (half + 1))
             nc.scalar.copy(
                 late_bf[n][:, cols, :].rearrange("p (c e) t -> p c t e", e=4),
-                raw[:, n % 2, :, cols].rearrange("p t (c e) -> p c t e", e=4),
+                raw[:, :, cols].rearrange("p t (c e) -> p c t e", e=4),
             )
 
         def quantize_late(n):
             late_q[n] = quantize("late%d" % n, late_bf[n][:].rearrange("p c t -> p (c t)"), BANK)
 
-        x1_product(0)
-        square(0)
-        x1_product(1)
-        square(1)
-        cast_w2(0, 0, True)
+        for i in range(2):
+            x1_product(i)
+            square(i, 0)
+            square(i, 1)
+        stage_w2(0, 0, 0, 4)
+        for t in range(4):
+            cast_w2(0, 0, t, True)
         pick_deposit(0)
-        cast_w2(0, 1, True)
-        quantize_w2(0)
+        quantize_w2(0, 0, 0, 4)
+        stage_w2(0, 1, 0, 1, 67 * KB)
+        cast_w2(0, 1, 0, True)
+        quantize_w2(0, 1, 0, 1)
         pick_deposit(1)
         for i in range(ROW_TILES):
-            nxt = i + 1
             u_product(i)
             if i >= 2:
                 x1_product(i)
-                square(i)
+                square(i, 0)
+            if i in LATE_GATE:
+                square(i, 1)
+                picked_sigmoids(i)
                 pick_deposit(i)
-            sigmoid(i)
-            gate(i)
-            if nxt < ROW_TILES:
-                cast_w2(nxt, 0, False)
-                cast_w2(nxt, 1, False)
-                quantize_w2(nxt)
-            if nxt == 3:
-                load_prior()
+                copy_u(i)
+            else:
+                if i != 1:
+                    sigmoid(i)
+                gate(i)
+                if i >= 2:
+                    square(i, 1)
+                    pick_deposit(i)
+            if i == 0:
+                sigmoid(1)
+                stage_w2(0, 1, 1, 4, 64 * KB)
+                cast_w2(0, 1, 1, False)
+                quantize_w2(0, 1, 1, 2)
+                cast_w2(0, 1, 2, False)
+                cast_w2(0, 1, 3, False)
+                quantize_w2(0, 1, 2, 4)
+            if i in (1, 2):
+                stage_w2(1, i - 1, 0, 4)
+                for t in range(4):
+                    cast_w2(1, i - 1, t, False)
             if i == 4:
                 quantize_z(0, 0)
-            if 3 <= i < 7:
-                cast_late(i - 3, 0)
-                cast_late(i - 3, 1)
             if i < ROW_TILES - 1:
                 pick_withdrawal(i, 0, M)
                 pick_hop(i, 0, M)
-            if 3 <= i < 7:
-                quantize_late(i - 3)
+            if i == 0:
+                load_prior()
+            if i in (1, 2):
+                quantize_w2(1, i - 1, 0, 4)
+            if LATE0 <= i < LATE0 + 4:
+                cast_late(i - LATE0, 0)
+                cast_late(i - LATE0, 1)
+                quantize_late(i - LATE0)
             if i == 3:
                 larger(0, 0, M)
 
         sin_warm = keep.tile([P, 8], F32, name="sin_warm")
-        nc.scalar.activation(sin_warm[:], sig[ROW_TILES - 1][:, S - 8 : S], ACT.Sin)
+        nc.scalar.activation(sin_warm[:], (s3 if ROW_TILES - 1 in LATE_GATE else sig)[ROW_TILES - 1][:, M - 8 : M], ACT.Sin)
 
         y_ps = {}
         for lo in range(0, M, CHUNK):

@@ -21,8 +21,8 @@ PASSES = 2
 BANK = 512
 ROW_TILES = 8
 CHUNK = 256
-LATE_GATE = (3, 7)
-LATE0 = 3
+LATE_GATE = (3, 5, 7)
+LATE_AT = (4, 5, 6)
 X2B = 2
 
 
@@ -139,17 +139,21 @@ def tile_list_layering_chain_features_kernel(
             rows = w3[512 * b : 512 * (b + 1), :].rearrange("(g t j) n -> t g j n", t=4, j=8)
             for t in range(4):
                 nc.sync.dma_start(w3_raw[:, b, t, :], rows[t])
-        w4_s = big.tile([P, PASSES, N], U8, name="w4_s", align_bytes=64, offset=40 * KB)
-        nc.gpsimd.memset(w4_s[:].rearrange("p a n -> p (a n)").bitcast(I32), 0)
-        w4_w = big.tile([P, PASSES, N], I32, name="w4_w", align_bytes=64, offset=41 * KB)
-        nc.sync.dma_start(
-            w4_w[:], w4_words.rearrange("a p c i -> a p (c i)").bitcast(I32).rearrange("a p c -> p a c")
-        )
-        for q in range(4):
+        w4 = []
+
+        def load_w4():
+            w4_s = big.tile([P, PASSES, N], U8, name="w4_s", align_bytes=64, offset=40 * KB)
+            nc.gpsimd.memset(w4_s[:].rearrange("p a n -> p (a n)").bitcast(I32), 0)
+            w4_w = big.tile([P, PASSES, N], I32, name="w4_w", align_bytes=64, offset=41 * KB)
             nc.sync.dma_start(
-                w4_s[32 * q : 32 * q + 4, :, :].bitcast(I32),
-                w4_scales[:, 4 * q : 4 * q + 4, :].bitcast(I32).rearrange("a q n -> q a n"),
+                w4_w[:], w4_words.rearrange("a p c i -> a p (c i)").bitcast(I32).rearrange("a p c -> p a c")
             )
+            for q in range(4):
+                nc.sync.dma_start(
+                    w4_s[32 * q : 32 * q + 4, :, :].bitcast(I32),
+                    w4_scales[:, 4 * q : 4 * q + 4, :].bitcast(I32).rearrange("a q n -> q a n"),
+                )
+            w4.extend([w4_w, w4_s])
 
         x1_ps, u_ps, sq, sig, x2, g1 = {}, {}, {}, {}, {}, {}
         w2_bf, w2_w, w2_s = {}, {}, {}
@@ -172,7 +176,7 @@ def tile_list_layering_chain_features_kernel(
 
         def square(i, h):
             if h == 0 and i < 2:
-                sq[i] = big.tile([P, S], F32, name="sq%d" % i, align_bytes=64, offset=(64 + 6 * i) * KB)
+                sq[i] = big.tile([P, S], F32, name="sq%d" % i, align_bytes=64, offset=(64 + 4 * i) * KB)
             elif h == 0:
                 sq[i] = work.tile([P, S], F32, name="sq")
             nc.scalar.activation(sq[i][:, BANK * h : BANK * (h + 1)], x1_ps[i, h][:], ACT.Square)
@@ -203,7 +207,7 @@ def tile_list_layering_chain_features_kernel(
             if offset is None:
                 tile = work.tile(shape, BF16, name="w2_bf", align_bytes=64, bufs=2)
             else:
-                tile = big.tile(shape, BF16, name="w2_bf%d" % t0, align_bytes=64, offset=offset)
+                tile = big.tile(shape, BF16, name="w2_bf%d%d" % (a, t0), align_bytes=64, offset=offset)
             for t in range(t0, t1):
                 w2_bf[b, a, t] = (tile, t - t0)
 
@@ -250,8 +254,8 @@ def tile_list_layering_chain_features_kernel(
                 nc.vector.tensor_tensor(x2[i][:, cols], u_ps[i, h][:], sig[i][:, cols], ALU.mult)
 
         def pick_deposit(i):
-            if i < 2:
-                g1[i] = big.tile([P, M], F32, name="g1_%d" % i, align_bytes=64, offset=(53, 67)[i] * KB)
+            if i == 0:
+                g1[i] = big.tile([P, M], F32, name="g1_first", align_bytes=64, offset=40 * KB)
             else:
                 g1[i] = work.tile([P, M], F32, name="g1")
             if i in LATE_GATE:
@@ -301,19 +305,19 @@ def tile_list_layering_chain_features_kernel(
             )
 
         late_bf, late_q = {}, {}
-        late_raw = [w3_raw[:, 0], w3_raw[:, 1]]
+        late_raw = {0: w3_raw[:, 0], 3: w3_raw[:, 1]}
 
         def load_prior():
             for b in range(PASSES):
                 rows = big.tile([P, 4, M], F32, name="prior_raw%d" % b, align_bytes=64, offset=(53, 6)[b] * KB)
                 nc.sync.dma_start(rows[:], prior[512 * b : 512 * (b + 1), :].rearrange("(p t) m -> p t m", t=4))
-                late_raw.append(rows[:])
+                late_raw[1 + b] = rows[:]
 
         def cast_late(n, half):
             raw = late_raw[n]
             if n not in late_bf:
                 late_bf[n] = big.tile(
-                    [P, BANK, 4], BF16, name="late_bf%d" % n, align_bytes=64, offset=(64 + 6 * (n % 2)) * KB
+                    [P, BANK, 4], BF16, name="late_bf%d" % n, align_bytes=64, offset=(64 + 4 * (n % 2)) * KB
                 )
             cols = slice(256 * half, 256 * (half + 1))
             nc.scalar.copy(
@@ -328,14 +332,14 @@ def tile_list_layering_chain_features_kernel(
             x1_product(i)
             square(i, 0)
             square(i, 1)
-        stage_w2(0, 0, 0, 4)
+        stage_w2(0, 0, 0, 4, 41 * KB)
         for t in range(4):
             cast_w2(0, 0, t, True)
-        pick_deposit(0)
-        quantize_w2(0, 0, 0, 4)
-        stage_w2(0, 1, 0, 1, 67 * KB)
+        stage_w2(0, 1, 0, 1, 40 * KB)
         cast_w2(0, 1, 0, True)
+        quantize_w2(0, 0, 0, 4)
         quantize_w2(0, 1, 0, 1)
+        pick_deposit(0)
         pick_deposit(1)
         for i in range(ROW_TILES):
             u_product(i)
@@ -373,17 +377,30 @@ def tile_list_layering_chain_features_kernel(
                 pick_hop(i, 0, M)
             if i == 0:
                 load_prior()
+                load_w4()
             if i in (1, 2):
                 quantize_w2(1, i - 1, 0, 4)
-            if LATE0 <= i < LATE0 + 4:
-                cast_late(i - LATE0, 0)
-                cast_late(i - LATE0, 1)
-                quantize_late(i - LATE0)
+            if i in LATE_AT:
+                cast_late(LATE_AT.index(i), 0)
+                cast_late(LATE_AT.index(i), 1)
+                quantize_late(LATE_AT.index(i))
             if i == 3:
                 larger(0, 0, M)
 
+        for n in range(len(LATE_AT), 4):
+            cast_late(n, 0)
+            cast_late(n, 1)
         sin_warm = keep.tile([P, 8], F32, name="sin_warm")
         nc.scalar.activation(sin_warm[:], (s3 if ROW_TILES - 1 in LATE_GATE else sig)[ROW_TILES - 1][:, M - 8 : M], ACT.Sin)
+
+        last = ROW_TILES - 1
+        pick_withdrawal(last, 0, CHUNK)
+        pick_hop(last, 0, CHUNK)
+        pick_withdrawal(last, CHUNK, M)
+        for n in range(len(LATE_AT), 4):
+            quantize_late(n)
+        larger(1, 0, CHUNK)
+        pick_hop(last, CHUNK, M)
 
         y_ps = {}
         for lo in range(0, M, CHUNK):
@@ -392,32 +409,26 @@ def tile_list_layering_chain_features_kernel(
                 rows = slice(P * c, P * (c + 1))
                 tag = "x1" if lo == 0 else "u"
                 bank = psum.tile([P, CHUNK], F32, name=tag, tag=tag)
-                for b in range(PASSES):
-                    nc.tensor.matmul_mx(
-                        out=bank[:],
-                        lhsT=w4_w[:, b, rows].bitcast(FP8X4),
-                        lhsT_scale=w4_s[:, b, rows],
-                        rhs=late_q[2 + b][0][:, cols].bitcast(FP8X4),
-                        rhs_scale=late_q[2 + b][1][:, cols],
-                        start=(b == 0),
-                        stop=False,
-                    )
                 nc.tensor.matmul_mx(
                     out=bank[:],
                     lhsT=late_q[0][0][:, rows].bitcast(FP8X4),
                     lhsT_scale=late_q[0][1][:, rows],
                     rhs=z_w[0, 0][:, cols].bitcast(FP8X4),
                     rhs_scale=z_s[0, 0][:, cols],
-                    start=False,
+                    start=True,
                     stop=False,
                 )
+                for b in range(PASSES):
+                    nc.tensor.matmul_mx(
+                        out=bank[:],
+                        lhsT=w4[0][:, b, rows].bitcast(FP8X4),
+                        lhsT_scale=w4[1][:, b, rows],
+                        rhs=late_q[1 + b][0][:, cols].bitcast(FP8X4),
+                        rhs_scale=late_q[1 + b][1][:, cols],
+                        start=False,
+                        stop=False,
+                    )
                 y_ps[lo, c] = bank
-        last = ROW_TILES - 1
-        pick_withdrawal(last, 0, CHUNK)
-        pick_hop(last, 0, CHUNK)
-        pick_withdrawal(last, CHUNK, M)
-        larger(1, 0, CHUNK)
-        pick_hop(last, CHUNK, M)
         quantize_z(1, 0)
         larger(1, CHUNK, M)
         quantize_z(1, CHUNK)
@@ -426,8 +437,8 @@ def tile_list_layering_chain_features_kernel(
                 rows = slice(P * c, P * (c + 1))
                 nc.tensor.matmul_mx(
                     out=y_ps[lo, c][:],
-                    lhsT=late_q[1][0][:, rows].bitcast(FP8X4),
-                    lhsT_scale=late_q[1][1][:, rows],
+                    lhsT=late_q[3][0][:, rows].bitcast(FP8X4),
+                    lhsT_scale=late_q[3][1][:, rows],
                     rhs=z_w[1, lo][:].bitcast(FP8X4),
                     rhs_scale=z_s[1, lo][:],
                     start=False,

@@ -17,13 +17,32 @@ ACT = mybir.ActivationFunctionType
 ALU = mybir.AluOpType
 
 P = 128
+PACK = 4
 PASSES = 2
+SPAN = P * PACK
 BANK = 512
-ROW_TILES = 8
-CHUNK = 256
-LATE_GATE = (3, 5, 7)
-LATE_AT = (4, 5, 6)
-X2B = 2
+ROW_TILES = PASSES * PACK
+LAST = ROW_TILES - 1
+CHUNK = M // 2
+
+FIRST_GATE_AFTER_PICK = 3
+FIRST_OPERAND_CAST = 4
+
+AT_TABLE = (0, 31.5)
+AT_W1_SCALES, AT_W1_WORDS = 0, 2
+AT_W1_RAW = 27
+AT_W3 = 16
+AT_TABLE_SCALES = 62
+AT_SECOND_HALF = 64
+AT_W2 = ((55, 6), (32, 47))
+AT_FIRST_CASTS = (43, 41)
+AT_FIRST_DEPOSITS = (42, 40)
+AT_W4_SCALES, AT_W4_WORDS = 40, 41
+AT_SQUARES = (66, 70)
+
+
+def gate_after_pick(i):
+    return i >= FIRST_GATE_AFTER_PICK and (i - FIRST_GATE_AFTER_PICK) % 2 == 0
 
 
 def tile_list_layering_chain_features_kernel(
@@ -34,17 +53,18 @@ def tile_list_layering_chain_features_kernel(
     with ExitStack() as ctx:
         lists = ctx.enter_context(tc.tile_pool(name="lists", bufs=1))
         keep = ctx.enter_context(tc.tile_pool(name="keep", bufs=1))
-        big = ctx.enter_context(tc.tile_pool(name="big", bufs=1))
+        laid = ctx.enter_context(tc.tile_pool(name="laid", bufs=1))
         work = ctx.enter_context(tc.tile_pool(name="work", bufs=3))
         psum = ctx.enter_context(tc.psum_pool(name="psum", bufs=4))
 
-        KB = 1024
-        tab_s = big.tile([P, T], U8, name="tab_s", align_bytes=64, offset=60 * KB)
+        def place(shape, dtype, name, kib):
+            return laid.tile(shape, dtype, name=name, align_bytes=64, offset=int(1024 * kib))
+
+        def scale_rows(scales):
+            return scales.bitcast(I32).rearrange("a (q s) n -> s q a n", s=4)
+
+        tab_s = place([P, T], U8, "tab_s", AT_TABLE_SCALES)
         nc.vector.memset(tab_s[:].bitcast(I32), 0)
-        warm = big.tile([P, 32], F32, name="warm", align_bytes=64, offset=31 * KB - 64)
-        nc.vector.memset(warm[:], 0.0)
-        warm_out = keep.tile([P, 32], F32, name="warm_out")
-        nc.scalar.activation(warm_out[:], warm[:], ACT.Sigmoid)
         w1_s_raw = keep.tile([P, PASSES, H // 4], I32, name="w1_s_raw")
         nc.gpsimd.memset(w1_s_raw[:], 0)
         v_s1 = keep.tile([P, S], U8, name="v_s1", align_bytes=64)
@@ -58,392 +78,349 @@ def tile_list_layering_chain_features_kernel(
         nc.sync.dma_start(p1[:], pos1)
         nc.sync.dma_start(p2[:], pos2)
         nc.sync.dma_start(p3[:], pos3)
-        for q in range(4):
-            nc.gpsimd.dma_start(
-                w1_s_raw[32 * q : 32 * q + 4, :, :],
-                w1_scales[:, 4 * q : 4 * q + 4, :].bitcast(I32).rearrange("a q n -> q a n"),
-            )
-        tab_w = []
-        for a in range(PASSES):
-            words = big.tile([P, T], I32, name="tab_w%d" % a, align_bytes=64, offset=31 * KB * a)
+        for s in range(4):
+            nc.gpsimd.dma_start(w1_s_raw[s:P:32, :, :], scale_rows(w1_scales)[s])
+
+        def load_table_words(a):
+            words = place([P, T], I32, "tab_w%d" % a, AT_TABLE[a])
             nc.sync.dma_start(words[:], tab_words[a].rearrange("p t i -> p (t i)").bitcast(I32))
-            tab_w.append(words)
-            if a == 0:
-                for q in range(4):
-                    nc.sync.dma_start(
-                        tab_s[32 * q : 32 * q + 4, :].bitcast(I32),
-                        tab_scales[0, 4 * q : 4 * q + 4, :].bitcast(I32),
-                    )
-                nc.sync.dma_start(tab_s[4:P:8, :].bitcast(I32), tab_scales[1].bitcast(I32))
-                w1_raw = big.tile([P, PASSES, H // 2], I32, name="w1_raw", align_bytes=64, offset=27 * KB)
-                nc.sync.dma_start(w1_raw[:], w1_words.bitcast(I32).rearrange("a p c -> p a c"))
+            return words
+
+        tab_w = [load_table_words(0)]
+        for s in range(4):
+            nc.sync.dma_start(
+                tab_s[s:P:32, :].bitcast(I32), tab_scales[0].bitcast(I32).rearrange("(q s) n -> s q n", s=4)[s]
+            )
+        nc.sync.dma_start(tab_s[4:P:8, :].bitcast(I32), tab_scales[1].bitcast(I32))
+        w1_raw = place([P, PASSES, H // 2], I32, "w1_raw", AT_W1_RAW)
+        nc.sync.dma_start(w1_raw[:], w1_words.bitcast(I32).rearrange("a p c -> p a c"))
+        tab_w.append(load_table_words(1))
 
         v_s0 = keep.tile([P, S], U8, name="v_s0", align_bytes=64)
         nc.vector.tensor_copy(v_s0[:], tab_s[:].indirect(idx[:]))
-        for q in range(4):
-            nc.sync.dma_start(
-                v_s1[32 * q : 32 * q + 4, :].bitcast(I32), v_s0[32 * q + 4 : 32 * q + 32 : 8, :].bitcast(I32)
-            )
-        v_s = [v_s0, v_s1]
-        v_w = {}
+        for s in range(4):
+            nc.sync.dma_start(v_s1[s:P:32, :].bitcast(I32), v_s0[8 * s + 4 : P : 32, :].bitcast(I32))
+        v_s = (v_s0, v_s1)
+        v_w, w1_w, w1_s, w2_raw = {}, {}, {}, {}
 
         def gather_words(a, h):
             if (a, h) == (0, 1):
-                tile = big.tile([P, BANK], U32, name="v_w01", align_bytes=64, offset=62 * KB)
+                v_w[a, h] = place([P, BANK], U32, "v_w01", AT_SECOND_HALF)
             else:
-                tile = keep.tile([P, BANK], U32, name="v_w%d%d" % (a, h), align_bytes=64)
-            nc.vector.tensor_copy(tile[:], tab_w[a][:].bitcast(U32).indirect(idx[:, 32 * h : 32 * (h + 1)]))
-            v_w[a, h] = tile
+                v_w[a, h] = keep.tile([P, BANK], U32, name="v_w%d%d" % (a, h), align_bytes=64)
+            entries = idx[:, h * BANK // 16 : (h + 1) * BANK // 16]
+            nc.vector.tensor_copy(v_w[a, h][:], tab_w[a][:].bitcast(U32).indirect(entries))
 
-        w1_w, w1_s = {}, {}
-
-        def order_w1_scales(a):
-            w1_s[a] = big.tile([P, H], U8, name="w1_s%d" % a, align_bytes=64, offset=KB * a)
+        def order_w1(a):
+            w1_s[a] = place([P, H], U8, "w1_s%d" % a, AT_W1_SCALES + a)
             nc.vector.tensor_copy(
-                w1_s[a][:].bitcast(I32).rearrange("p (b t g w) -> p b t g w", b=2, t=4, w=2),
-                w1_s_raw[:, a, :].rearrange("p (b g t w) -> p b t g w", b=2, t=4, w=2),
+                w1_s[a][:].bitcast(I32).rearrange("p (b t g w) -> p b t g w", b=PASSES, t=PACK, w=2),
+                w1_s_raw[:, a, :].rearrange("p (b g t w) -> p b t g w", b=PASSES, t=PACK, w=2),
             )
-
-        def order_w1_words(a):
-            w1_w[a] = big.tile([P, H // 2], I32, name="w1_w%d" % a, align_bytes=64, offset=(2 + 2 * a) * KB)
+            w1_w[a] = place([P, H // 2], I32, "w1_w%d" % a, AT_W1_WORDS + 2 * a)
             nc.vector.tensor_copy(
-                w1_w[a][:].rearrange("p (b t g w) -> p b t g w", b=2, t=4, w=4),
-                w1_raw[:, a, :].rearrange("p (b g t w) -> p b t g w", b=2, t=4, w=4),
+                w1_w[a][:].rearrange("p (b t g w) -> p b t g w", b=PASSES, t=PACK, w=4),
+                w1_raw[:, a, :].rearrange("p (b g t w) -> p b t g w", b=PASSES, t=PACK, w=4),
             )
-
-        w2_raw = {}
 
         def load_w2(b):
             for a in range(PASSES):
-                rows = big.tile(
-                    [P, 4, BANK], F32, name="w2_raw%d%d" % (b, a), align_bytes=64, offset=KB * ((53, 6), (32, 45))[b][a]
-                )
-                nc.sync.dma_start(
-                    rows[:],
-                    w2[512 * a : 512 * (a + 1), 512 * b : 512 * (b + 1)].rearrange("(p i) c -> p i c", i=4),
-                )
-                w2_raw[b, a] = rows
+                w2_raw[b, a] = place([P, PACK, SPAN], F32, "w2_raw%d%d" % (b, a), AT_W2[b][a])
+                piece = w2[SPAN * a : SPAN * (a + 1), SPAN * b : SPAN * (b + 1)]
+                nc.sync.dma_start(w2_raw[b, a][:], piece.rearrange("(p i) c -> p i c", i=PACK))
 
         gather_words(0, 0)
         gather_words(0, 1)
         load_w2(0)
         for a in range(PASSES):
-            order_w1_scales(a)
-            order_w1_words(a)
+            order_w1(a)
         gather_words(1, 0)
         gather_words(1, 1)
         load_w2(1)
 
-        w3_raw = big.tile([P, PASSES, 4, N], F32, name="w3_raw", align_bytes=64, offset=16 * KB)
+        w3_raw = place([P, PASSES, PACK, N], F32, "w3_raw", AT_W3)
         for b in range(PASSES):
-            rows = w3[512 * b : 512 * (b + 1), :].rearrange("(g t j) n -> t g j n", t=4, j=8)
-            for t in range(4):
-                nc.sync.dma_start(w3_raw[:, b, t, :], rows[t])
-        w4 = []
+            by_slot = w3[SPAN * b : SPAN * (b + 1), :].rearrange("(g t j) n -> t g j n", t=PACK, j=8)
+            for t in range(PACK):
+                nc.sync.dma_start(w3_raw[:, b, t, :], by_slot[t])
 
-        def load_w4():
-            w4_s = big.tile([P, PASSES, N], U8, name="w4_s", align_bytes=64, offset=40 * KB)
-            nc.gpsimd.memset(w4_s[:].rearrange("p a n -> p (a n)").bitcast(I32), 0)
-            w4_w = big.tile([P, PASSES, N], I32, name="w4_w", align_bytes=64, offset=41 * KB)
-            nc.sync.dma_start(
-                w4_w[:], w4_words.rearrange("a p c i -> a p (c i)").bitcast(I32).rearrange("a p c -> p a c")
-            )
-            for q in range(4):
-                nc.sync.dma_start(
-                    w4_s[32 * q : 32 * q + 4, :, :].bitcast(I32),
-                    w4_scales[:, 4 * q : 4 * q + 4, :].bitcast(I32).rearrange("a q n -> q a n"),
-                )
-            w4.extend([w4_w, w4_s])
-
-        x1_ps, u_ps, sq, sig, x2, g1 = {}, {}, {}, {}, {}, {}
+        x1_ps, u_ps, sq, sig, hop_window, deposit = {}, {}, {}, {}, {}, {}
+        gate2, gate3, product, withdrawal = {}, {}, {}, {}
         w2_bf, w2_w, w2_s = {}, {}, {}
-        a4, c4 = {}, {}
 
-        def x1_product(i):
+        def first_stage_product(tag, words, scales):
+            banks = []
             for h in range(2):
-                bank = psum.tile([P, BANK], F32, name="x1", tag="x1")
+                bank = psum.tile([P, BANK], F32, name=tag, tag=tag)
                 for a in range(PASSES):
                     nc.tensor.matmul_mx(
                         out=bank[:],
-                        lhsT=w1_w[a][:, 64 * i : 64 * (i + 1)].bitcast(FP4X4),
-                        lhsT_scale=w1_s[a][:, P * i : P * (i + 1)],
+                        lhsT=words(a),
+                        lhsT_scale=scales(a),
                         rhs=v_w[a, h][:].bitcast(FP8X4),
                         rhs_scale=v_s[a][:, BANK * h : BANK * (h + 1)],
                         start=(a == 0),
                         stop=(a == PASSES - 1),
                     )
-                x1_ps[i, h] = bank
+                banks.append(bank)
+            return banks
 
-        def square(i, h):
-            if h == 0 and i < 2:
-                sq[i] = big.tile([P, S], F32, name="sq%d" % i, align_bytes=64, offset=(64 + 4 * i) * KB)
-            elif h == 0:
-                sq[i] = work.tile([P, S], F32, name="sq")
-            nc.scalar.activation(sq[i][:, BANK * h : BANK * (h + 1)], x1_ps[i, h][:], ACT.Square)
-
-        def sigmoid(i):
-            sig[i] = work.tile([P, S], F32, name="sig")
-            for h in range(2):
-                nc.scalar.activation(sig[i][:, BANK * h : BANK * (h + 1)], x1_ps[i, h][:], ACT.Sigmoid)
-
-        x1_sb, s2, s3 = {}, {}, {}
-
-        def picked_sigmoids(i):
-            x1_sb[i] = work.tile([P, S], F32, name="sig")
-            for h in range(2):
-                nc.scalar.copy(x1_sb[i][:, BANK * h : BANK * (h + 1)], x1_ps[i, h][:])
-            s2[i] = work.tile([P, M], F32, name="s2", bufs=2)
-            nc.scalar.activation(s2[i][:], x1_sb[i][:].indirect(p2[:]), ACT.Sigmoid)
-            s3[i] = work.tile([P, M], F32, name="s3", bufs=2)
-            nc.scalar.activation(s3[i][:], x1_sb[i][:].indirect(p3[:]), ACT.Sigmoid)
-
-        def copy_u(i):
-            x2[i] = work.tile([P, S], F32, name="x2", bufs=X2B)
-            for h in range(2):
-                nc.scalar.copy(x2[i][:, BANK * h : BANK * (h + 1)], u_ps[i, h][:])
-
-        def stage_w2(b, a, t0, t1, offset=None):
-            shape = [P, t1 - t0, BANK]
-            if offset is None:
-                tile = work.tile(shape, BF16, name="w2_bf", align_bytes=64, bufs=2)
-            else:
-                tile = big.tile(shape, BF16, name="w2_bf%d%d" % (a, t0), align_bytes=64, offset=offset)
-            for t in range(t0, t1):
-                w2_bf[b, a, t] = (tile, t - t0)
-
-        def cast_w2(b, a, t, on_vector):
-            tile, row = w2_bf[b, a, t]
-            dst = tile[:, row, :].rearrange("p (g u e i) -> p g u i e", u=2, e=4, i=4)
-            src = w2_raw[b, a][:].rearrange("p i (g t u e) -> p t g u i e", t=4, u=2, e=4)[:, t]
-            if on_vector:
-                nc.vector.tensor_copy(dst, src)
-            else:
-                nc.scalar.copy(dst, src)
-
-        def quantize_w2(b, a, t0, t1):
-            if t0 == 0:
-                w2_w[b, a] = keep.tile([P, BANK], U32, name="w2_w%d%d" % (b, a), align_bytes=64)
-                w2_s[b, a] = keep.tile([P, BANK], U8, name="w2_s%d%d" % (b, a), align_bytes=64)
-            tile, row = w2_bf[b, a, t0]
-            nc.vector.quantize_mx(
-                out=w2_w[b, a][:, P * t0 : P * t1].bitcast(FP8X4),
-                scales=w2_s[b, a][:, P * t0 : P * t1],
-                in_=tile[:, row : row + t1 - t0, :].rearrange("p t c -> p (t c)"),
+        def x1_product(i):
+            x1_ps[i] = first_stage_product(
+                "x1",
+                lambda a: w1_w[a][:, P // 2 * i : P // 2 * (i + 1)].bitcast(FP4X4),
+                lambda a: w1_s[a][:, P * i : P * (i + 1)],
             )
 
         def u_product(i):
-            b, t = divmod(i, 4)
-            for h in range(2):
-                bank = psum.tile([P, BANK], F32, name="u", tag="u")
-                for a in range(PASSES):
-                    nc.tensor.matmul_mx(
-                        out=bank[:],
-                        lhsT=w2_w[b, a][:, P * t : P * (t + 1)].bitcast(FP8X4),
-                        lhsT_scale=w2_s[b, a][:, P * t : P * (t + 1)],
-                        rhs=v_w[a, h][:].bitcast(FP8X4),
-                        rhs_scale=v_s[a][:, BANK * h : BANK * (h + 1)],
-                        start=(a == 0),
-                        stop=(a == PASSES - 1),
-                    )
-                u_ps[i, h] = bank
-
-        def gate(i):
-            x2[i] = work.tile([P, S], F32, name="x2", bufs=X2B)
-            for h in range(2):
-                cols = slice(BANK * h, BANK * (h + 1))
-                nc.vector.tensor_tensor(x2[i][:, cols], u_ps[i, h][:], sig[i][:, cols], ALU.mult)
-
-        def pick_deposit(i):
-            if i == 0:
-                g1[i] = big.tile([P, M], F32, name="g1_first", align_bytes=64, offset=40 * KB)
-            else:
-                g1[i] = work.tile([P, M], F32, name="g1")
-            if i in LATE_GATE:
-                nc.vector.tensor_tensor(g1[i][:], sq[i][:].indirect(p1[:]), s2[i][:], ALU.mult)
-            else:
-                nc.vector.tensor_copy(g1[i][:], sq[i][:].indirect(p1[:]))
-
-        def pick_withdrawal(i, lo, hi):
-            b, t = divmod(i, 4)
-            if b not in c4:
-                c4[b] = work.tile([P, 4, M], F32, name="c4", bufs=2)
-            picked = x2[i][:].indirect(p3[:, lo // 16 : hi // 16])
-            if i in LATE_GATE:
-                nc.vector.tensor_tensor(c4[b][:, t, lo:hi], picked, s3[i][:, lo:hi], ALU.mult)
-            else:
-                nc.vector.tensor_copy(c4[b][:, t, lo:hi], picked)
-
-        def pick_hop(i, lo, hi):
-            b, t = divmod(i, 4)
-            if b not in a4:
-                a4[b] = work.tile([P, 4, M], F32, name="a4", bufs=2)
-            nc.vector.tensor_tensor(
-                a4[b][:, t, lo:hi], x2[i][:].indirect(p2[:, lo // 16 : hi // 16]), g1[i][:, lo:hi], ALU.mult
+            b, t = divmod(i, PACK)
+            u_ps[i] = first_stage_product(
+                "u",
+                lambda a: w2_w[b, a][:, P * t : P * (t + 1)].bitcast(FP8X4),
+                lambda a: w2_s[b, a][:, P * t : P * (t + 1)],
             )
 
-        z_bf, z_w, z_s = {}, {}, {}
+        def square(i, h):
+            if h == 0 and i < len(AT_SQUARES):
+                sq[i] = place([P, S], F32, "sq%d" % i, AT_SQUARES[i])
+            elif h == 0:
+                sq[i] = work.tile([P, S], F32, name="sq")
+            nc.scalar.activation(sq[i][:, BANK * h : BANK * (h + 1)], x1_ps[i][h][:], ACT.Square)
+
+        def sigmoid(i, h):
+            if h == 0:
+                sig[i] = work.tile([P, S], F32, name="sig", tag="from_x1")
+            nc.scalar.activation(sig[i][:, BANK * h : BANK * (h + 1)], x1_ps[i][h][:], ACT.Sigmoid)
+
+        def gate(i):
+            hop_window[i] = work.tile([P, S], F32, name="x2", tag="hop_window", bufs=2)
+            for h in range(2):
+                cols = slice(BANK * h, BANK * (h + 1))
+                nc.vector.tensor_tensor(hop_window[i][:, cols], u_ps[i][h][:], sig[i][:, cols], ALU.mult)
+
+        def picked_gates(i):
+            x1_sb = work.tile([P, S], F32, name="x1_sb", tag="from_x1")
+            for h in range(2):
+                nc.scalar.copy(x1_sb[:, BANK * h : BANK * (h + 1)], x1_ps[i][h][:])
+            gate2[i] = work.tile([P, M], F32, name="gate2", bufs=2)
+            nc.scalar.activation(gate2[i][:], x1_sb[:].indirect(p2[:]), ACT.Sigmoid)
+            gate3[i] = work.tile([P, M], F32, name="gate3", bufs=2)
+            nc.scalar.activation(gate3[i][:], x1_sb[:].indirect(p3[:]), ACT.Sigmoid)
+
+        def copy_u(i):
+            hop_window[i] = work.tile([P, S], F32, name="u_sb", tag="hop_window", bufs=2)
+            for h in range(2):
+                nc.scalar.copy(hop_window[i][:, BANK * h : BANK * (h + 1)], u_ps[i][h][:])
+
+        def pick_deposit(i):
+            if i < len(AT_FIRST_DEPOSITS):
+                deposit[i] = place([P, M], F32, "deposit%d" % i, AT_FIRST_DEPOSITS[i])
+            else:
+                deposit[i] = work.tile([P, M], F32, name="deposit")
+            picked = sq[i][:].indirect(p1[:])
+            if gate_after_pick(i):
+                nc.vector.tensor_tensor(deposit[i][:], picked, gate2[i][:], ALU.mult)
+            else:
+                nc.vector.tensor_copy(deposit[i][:], picked)
+
+        def pick_withdrawal(i, lo, hi):
+            b, t = divmod(i, PACK)
+            if t == 0:
+                withdrawal[b] = work.tile([P, PACK, M], F32, name="withdrawal", bufs=2)
+            picked = hop_window[i][:].indirect(p3[:, lo // 16 : hi // 16])
+            if gate_after_pick(i):
+                nc.vector.tensor_tensor(withdrawal[b][:, t, lo:hi], picked, gate3[i][:, lo:hi], ALU.mult)
+            else:
+                nc.vector.tensor_copy(withdrawal[b][:, t, lo:hi], picked)
+
+        def pick_hop(i, lo, hi):
+            b, t = divmod(i, PACK)
+            if t == 0:
+                product[b] = work.tile([P, PACK, M], F32, name="product", bufs=2)
+            picked = hop_window[i][:].indirect(p2[:, lo // 16 : hi // 16])
+            nc.vector.tensor_tensor(product[b][:, t, lo:hi], picked, deposit[i][:, lo:hi], ALU.mult)
+
+        def cast_w2(copy, staging, b, a, t0, t1):
+            for t in range(t0, t1):
+                w2_bf[b, a, t] = staging
+                copy(
+                    staging[:, t - t0, :].rearrange("p (g u e i) -> p g u i e", u=2, e=4, i=PACK),
+                    w2_raw[b, a][:].rearrange("p i (g t u e) -> p t g u i e", t=PACK, u=2, e=4)[:, t],
+                )
+
+        def quantize_w2(b, a, t0, t1):
+            if t0 == 0:
+                w2_w[b, a] = keep.tile([P, SPAN], U32, name="w2_w%d%d" % (b, a), align_bytes=64)
+                w2_s[b, a] = keep.tile([P, SPAN], U8, name="w2_s%d%d" % (b, a), align_bytes=64)
+            nc.vector.quantize_mx(
+                out=w2_w[b, a][:, P * t0 : P * t1].bitcast(FP8X4),
+                scales=w2_s[b, a][:, P * t0 : P * t1],
+                in_=w2_bf[b, a, t0][:].rearrange("p t c -> p (t c)"),
+            )
+
+        z_bf, z_q, operand_bf, operand_q = {}, {}, {}, {}
+        operand_raw = {"w3_0": w3_raw[:, 0], "w3_1": w3_raw[:, 1]}
+        operands = ("w3_0", "prior_0", "prior_1", "w3_1")
+
+        def quantize(name, staged):
+            words = keep.tile([P, staged.shape[1]], U32, name=name + "_w", align_bytes=64)
+            scales = keep.tile([P, staged.shape[1]], U8, name=name + "_s", align_bytes=64)
+            nc.vector.quantize_mx(
+                out=words[:].bitcast(FP8X4), scales=scales[:], in_=staged[:].rearrange("p c t -> p (c t)")
+            )
+            return words, scales
 
         def larger(b, lo, hi):
-            z_bf[b, lo] = work.tile([P, hi - lo, 4], BF16, name="z_bf", align_bytes=64, bufs=1)
+            z_bf[b, lo] = work.tile([P, hi - lo, PACK], BF16, name="z_bf", align_bytes=64, bufs=1)
             nc.vector.tensor_tensor(
                 z_bf[b, lo][:].rearrange("p (c e) t -> p c t e", e=2),
-                a4[b][:, :, lo:hi].rearrange("p t (c e) -> p c t e", e=2),
-                c4[b][:, :, lo:hi].rearrange("p t (c e) -> p c t e", e=2),
+                product[b][:, :, lo:hi].rearrange("p t (c e) -> p c t e", e=2),
+                withdrawal[b][:, :, lo:hi].rearrange("p t (c e) -> p c t e", e=2),
                 ALU.max,
             )
 
-        def quantize(name, src, width):
-            words = keep.tile([P, width], U32, name=name + "_w", align_bytes=64)
-            scales = keep.tile([P, width], U8, name=name + "_s", align_bytes=64)
-            nc.vector.quantize_mx(out=words[:].bitcast(FP8X4), scales=scales[:], in_=src)
-            return words, scales
-
         def quantize_z(b, lo):
-            tile = z_bf[b, lo]
-            z_w[b, lo], z_s[b, lo] = quantize(
-                "z%d_%d" % (b, lo), tile[:].rearrange("p m t -> p (m t)"), tile.shape[1]
-            )
-
-        late_bf, late_q = {}, {}
-        late_raw = {0: w3_raw[:, 0], 3: w3_raw[:, 1]}
+            z_q[b, lo] = quantize("z%d_%d" % (b, lo), z_bf[b, lo])
 
         def load_prior():
             for b in range(PASSES):
-                rows = big.tile([P, 4, M], F32, name="prior_raw%d" % b, align_bytes=64, offset=(53, 6)[b] * KB)
-                nc.sync.dma_start(rows[:], prior[512 * b : 512 * (b + 1), :].rearrange("(p t) m -> p t m", t=4))
-                late_raw[1 + b] = rows[:]
+                rows = place([P, PACK, M], F32, "prior_raw%d" % b, AT_W2[0][b])
+                nc.sync.dma_start(rows[:], prior[SPAN * b : SPAN * (b + 1), :].rearrange("(p i) m -> p i m", i=PACK))
+                operand_raw["prior_%d" % b] = rows[:]
 
-        def cast_late(n, half):
-            raw = late_raw[n]
-            if n not in late_bf:
-                late_bf[n] = big.tile(
-                    [P, BANK, 4], BF16, name="late_bf%d" % n, align_bytes=64, offset=(64 + 4 * (n % 2)) * KB
-                )
-            cols = slice(256 * half, 256 * (half + 1))
-            nc.scalar.copy(
-                late_bf[n][:, cols, :].rearrange("p (c e) t -> p c t e", e=4),
-                raw[:, :, cols].rearrange("p t (c e) -> p c t e", e=4),
+        def load_w4():
+            scales = place([P, PASSES, N], U8, "w4_s", AT_W4_SCALES)
+            nc.gpsimd.memset(scales[:].rearrange("p a n -> p (a n)").bitcast(I32), 0)
+            words = place([P, PASSES, N], I32, "w4_w", AT_W4_WORDS)
+            nc.sync.dma_start(
+                words[:], w4_words.rearrange("a p c i -> a p (c i)").bitcast(I32).rearrange("a p c -> p a c")
             )
+            for s in range(4):
+                nc.sync.dma_start(scales[s:P:32, :, :].bitcast(I32), scale_rows(w4_scales)[s])
+            return words, scales
 
-        def quantize_late(n):
-            late_q[n] = quantize("late%d" % n, late_bf[n][:].rearrange("p c t -> p (c t)"), BANK)
+        def cast_operand(n):
+            name = operands[n]
+            operand_bf[name] = place([P, N, PACK], BF16, name + "_bf", AT_SQUARES[n % 2])
+            for lo in range(0, N, N // 2):
+                cols = slice(lo, lo + N // 2)
+                nc.scalar.copy(
+                    operand_bf[name][:, cols, :].rearrange("p (c e) t -> p c t e", e=4),
+                    operand_raw[name][:, :, cols].rearrange("p t (c e) -> p c t e", e=4),
+                )
 
-        for i in range(2):
-            x1_product(i)
-            square(i, 0)
-            square(i, 1)
-        stage_w2(0, 0, 0, 4, 41 * KB)
-        for t in range(4):
-            cast_w2(0, 0, t, True)
-        stage_w2(0, 1, 0, 1, 40 * KB)
-        cast_w2(0, 1, 0, True)
-        quantize_w2(0, 0, 0, 4)
-        quantize_w2(0, 1, 0, 1)
+        def quantize_operand(n):
+            operand_q[operands[n]] = quantize(operands[n], operand_bf[operands[n]])
+
+        x1_product(0)
+        sigmoid(0, 0)
+        square(0, 0)
+        square(0, 1)
+        x1_product(1)
+        square(1, 0)
+        square(1, 1)
+        cast_w2(nc.vector.tensor_copy, place([P, PACK, SPAN], BF16, "w2_bf00", AT_FIRST_CASTS[0]), 0, 0, 0, PACK)
+        cast_w2(nc.vector.tensor_copy, place([P, 2, SPAN], BF16, "w2_bf01a", AT_FIRST_CASTS[1]), 0, 1, 0, 2)
+        quantize_w2(0, 0, 0, PACK)
+        quantize_w2(0, 1, 0, 2)
         pick_deposit(0)
         pick_deposit(1)
-        for i in range(ROW_TILES):
-            u_product(i)
-            if i >= 2:
-                x1_product(i)
-                square(i, 0)
-            if i in LATE_GATE:
+
+        def start_row_tile(i):
+            x1_product(i)
+            square(i, 0)
+            if gate_after_pick(i):
                 square(i, 1)
-                picked_sigmoids(i)
+                picked_gates(i)
                 pick_deposit(i)
                 copy_u(i)
             else:
-                if i != 1:
-                    sigmoid(i)
+                sigmoid(i, 0)
+                sigmoid(i, 1)
                 gate(i)
-                if i >= 2:
-                    square(i, 1)
-                    pick_deposit(i)
-            if i == 0:
-                sigmoid(1)
-                stage_w2(0, 1, 1, 4, 64 * KB)
-                cast_w2(0, 1, 1, False)
-                quantize_w2(0, 1, 1, 2)
-                cast_w2(0, 1, 2, False)
-                cast_w2(0, 1, 3, False)
-                quantize_w2(0, 1, 2, 4)
-            if i in (1, 2):
-                stage_w2(1, i - 1, 0, 4)
-                for t in range(4):
-                    cast_w2(1, i - 1, t, False)
-            if i == 4:
+                square(i, 1)
+                pick_deposit(i)
+
+        def finish_row_tile(i):
+            pick_withdrawal(i, 0, M)
+            pick_hop(i, 0, M)
+
+        u_product(0)
+        sigmoid(0, 1)
+        gate(0)
+        sigmoid(1, 0)
+        sigmoid(1, 1)
+        cast_w2(nc.scalar.copy, place([P, 2, SPAN], BF16, "w2_bf01b", AT_SQUARES[0]), 0, 1, 2, PACK)
+        quantize_w2(0, 1, 2, PACK)
+        finish_row_tile(0)
+        load_prior()
+
+        for i in range(1, ROW_TILES):
+            u_product(i)
+            if i == 1:
+                gate(i)
+            else:
+                start_row_tile(i)
+            if i <= PASSES:
+                staging = work.tile([P, PACK, SPAN], BF16, name="w2_bf1", align_bytes=64, bufs=2)
+                cast_w2(nc.scalar.copy, staging, 1, i - 1, 0, PACK)
+            if i == PACK:
                 quantize_z(0, 0)
-            if i < ROW_TILES - 1:
-                pick_withdrawal(i, 0, M)
-                pick_hop(i, 0, M)
-            if i == 0:
-                load_prior()
-                load_w4()
-            if i in (1, 2):
-                quantize_w2(1, i - 1, 0, 4)
-            if i in LATE_AT:
-                cast_late(LATE_AT.index(i), 0)
-                cast_late(LATE_AT.index(i), 1)
-                quantize_late(LATE_AT.index(i))
-            if i == 3:
+            if i < LAST:
+                finish_row_tile(i)
+            if i == 1:
+                w4_w, w4_s = load_w4()
+            if i <= PASSES:
+                quantize_w2(1, i - 1, 0, PACK)
+            if 0 <= i - FIRST_OPERAND_CAST < len(operands) - 1:
+                cast_operand(i - FIRST_OPERAND_CAST)
+                quantize_operand(i - FIRST_OPERAND_CAST)
+            if i == PACK - 1:
                 larger(0, 0, M)
 
-        for n in range(len(LATE_AT), 4):
-            cast_late(n, 0)
-            cast_late(n, 1)
-        sin_warm = keep.tile([P, 8], F32, name="sin_warm")
-        nc.scalar.activation(sin_warm[:], (s3 if ROW_TILES - 1 in LATE_GATE else sig)[ROW_TILES - 1][:, M - 8 : M], ACT.Sin)
-
-        last = ROW_TILES - 1
-        pick_withdrawal(last, 0, CHUNK)
-        pick_hop(last, 0, CHUNK)
-        pick_withdrawal(last, CHUNK, M)
-        for n in range(len(LATE_AT), 4):
-            quantize_late(n)
+        cast_operand(len(operands) - 1)
+        pick_withdrawal(LAST, 0, CHUNK)
+        pick_hop(LAST, 0, CHUNK)
+        pick_withdrawal(LAST, CHUNK, M)
+        quantize_operand(len(operands) - 1)
         larger(1, 0, CHUNK)
-        pick_hop(last, CHUNK, M)
+        pick_hop(LAST, CHUNK, M)
+
+        def y_pass(bank, weights, weight_scales, moving, moving_scales, start, stop):
+            nc.tensor.matmul_mx(
+                out=bank[:],
+                lhsT=weights.bitcast(FP8X4),
+                lhsT_scale=weight_scales,
+                rhs=moving.bitcast(FP8X4),
+                rhs_scale=moving_scales,
+                start=start,
+                stop=stop,
+            )
 
         y_ps = {}
-        for lo in range(0, M, CHUNK):
+        for lo, tag in ((0, "x1"), (CHUNK, "u")):
             cols = slice(lo, lo + CHUNK)
-            for c in range(N // P):
-                rows = slice(P * c, P * (c + 1))
-                tag = "x1" if lo == 0 else "u"
-                bank = psum.tile([P, CHUNK], F32, name=tag, tag=tag)
-                nc.tensor.matmul_mx(
-                    out=bank[:],
-                    lhsT=late_q[0][0][:, rows].bitcast(FP8X4),
-                    lhsT_scale=late_q[0][1][:, rows],
-                    rhs=z_w[0, 0][:, cols].bitcast(FP8X4),
-                    rhs_scale=z_s[0, 0][:, cols],
-                    start=True,
-                    stop=False,
-                )
+            for n0 in range(0, N, P):
+                rows = slice(n0, n0 + P)
+                bank = psum.tile([P, CHUNK], F32, name="y", tag=tag)
+                w3_w, w3_s = operand_q["w3_0"]
+                z_w, z_s = z_q[0, 0]
+                y_pass(bank, w3_w[:, rows], w3_s[:, rows], z_w[:, cols], z_s[:, cols], True, False)
                 for b in range(PASSES):
-                    nc.tensor.matmul_mx(
-                        out=bank[:],
-                        lhsT=w4[0][:, b, rows].bitcast(FP8X4),
-                        lhsT_scale=w4[1][:, b, rows],
-                        rhs=late_q[1 + b][0][:, cols].bitcast(FP8X4),
-                        rhs_scale=late_q[1 + b][1][:, cols],
-                        start=False,
-                        stop=False,
+                    prior_w, prior_s = operand_q["prior_%d" % b]
+                    y_pass(
+                        bank, w4_w[:, b, rows], w4_s[:, b, rows], prior_w[:, cols], prior_s[:, cols], False, False
                     )
-                y_ps[lo, c] = bank
+                y_ps[lo, n0] = bank
         quantize_z(1, 0)
         larger(1, CHUNK, M)
         quantize_z(1, CHUNK)
         for lo in range(0, M, CHUNK):
-            for c in range(N // P):
-                rows = slice(P * c, P * (c + 1))
-                nc.tensor.matmul_mx(
-                    out=y_ps[lo, c][:],
-                    lhsT=late_q[3][0][:, rows].bitcast(FP8X4),
-                    lhsT_scale=late_q[3][1][:, rows],
-                    rhs=z_w[1, lo][:].bitcast(FP8X4),
-                    rhs_scale=z_s[1, lo][:],
-                    start=False,
-                    stop=True,
-                )
-                res = work.tile([P, CHUNK], F32, name="res", bufs=8)
-                nc.scalar.activation(res[:], y_ps[lo, c][:], ACT.Sin)
-                nc.sync.dma_start(out[rows, lo : lo + CHUNK], res[:])
+            for n0 in range(0, N, P):
+                rows = slice(n0, n0 + P)
+                w3_w, w3_s = operand_q["w3_1"]
+                z_w, z_s = z_q[1, lo]
+                y_pass(y_ps[lo, n0], w3_w[:, rows], w3_s[:, rows], z_w[:], z_s[:], False, True)
+                result = work.tile([P, CHUNK], F32, name="result", bufs=8)
+                nc.scalar.activation(result[:], y_ps[lo, n0][:], ACT.Sin)
+                nc.sync.dma_start(out[rows, lo : lo + CHUNK], result[:])

@@ -23,26 +23,20 @@ SPAN = P * PACK
 BANK = 512
 ROW_TILES = PASSES * PACK
 LAST = ROW_TILES - 1
-CHUNK = M // 2
+CHUNK = 128
+RING = 3
 
-FIRST_GATE_AFTER_PICK = 3
-FIRST_OPERAND_CAST = 4
-
-AT_TABLE = (0, 31.5)
+AT_TABLE = (0, 23)
+AT_TABLE_SCALES = 46
 AT_W1_SCALES, AT_W1_WORDS = 0, 2
-AT_W1_RAW = 27
-AT_W3 = 16
-AT_TABLE_SCALES = 62
-AT_SECOND_HALF = 64
-AT_W2 = ((55, 6), (32, 47))
-AT_FIRST_CASTS = (43, 41)
-AT_FIRST_DEPOSITS = (42, 40)
-AT_W4_SCALES, AT_W4_WORDS = 40, 41
-AT_SQUARES = (66, 70)
-
-
-def gate_after_pick(i):
-    return i >= FIRST_GATE_AFTER_PICK and (i - FIRST_GATE_AFTER_PICK) % 2 == 0
+AT_FIRST_CASTS = (23, 27, 29)
+AT_W2 = ((39, 49), (31, 16))
+AT_W3 = (49, 49)
+AT_PRIOR = (31, 16)
+AT_W4_WORDS = 27
+AT_GATE0 = (6, 8, 10, 12, 14, 57, 59, 61)
+AT_GATE1 = 63
+AT_WINDOW = 75
 
 
 def tile_list_layering_chain_features_kernel(
@@ -54,7 +48,7 @@ def tile_list_layering_chain_features_kernel(
         lists = ctx.enter_context(tc.tile_pool(name="lists", bufs=1))
         keep = ctx.enter_context(tc.tile_pool(name="keep", bufs=1))
         laid = ctx.enter_context(tc.tile_pool(name="laid", bufs=1))
-        work = ctx.enter_context(tc.tile_pool(name="work", bufs=3))
+        work = ctx.enter_context(tc.tile_pool(name="work", bufs=RING))
         psum = ctx.enter_context(tc.psum_pool(name="psum", bufs=4))
 
         def place(shape, dtype, name, kib):
@@ -65,8 +59,8 @@ def tile_list_layering_chain_features_kernel(
 
         tab_s = place([P, T], U8, "tab_s", AT_TABLE_SCALES)
         nc.vector.memset(tab_s[:].bitcast(I32), 0)
-        w1_s_raw = keep.tile([P, PASSES, H // 4], I32, name="w1_s_raw")
-        nc.gpsimd.memset(w1_s_raw[:], 0)
+        loaded_s = keep.tile([P, PASSES, H // 4], I32, name="loaded_s", align_bytes=64)
+        nc.gpsimd.memset(loaded_s[:], 0)
         v_s1 = keep.tile([P, S], U8, name="v_s1", align_bytes=64)
         nc.vector.memset(v_s1[:].bitcast(I32), 0)
 
@@ -78,8 +72,6 @@ def tile_list_layering_chain_features_kernel(
         nc.sync.dma_start(p1[:], pos1)
         nc.sync.dma_start(p2[:], pos2)
         nc.sync.dma_start(p3[:], pos3)
-        for s in range(4):
-            nc.gpsimd.dma_start(w1_s_raw[s:P:32, :, :], scale_rows(w1_scales)[s])
 
         def load_table_words(a):
             words = place([P, T], I32, "tab_w%d" % a, AT_TABLE[a])
@@ -87,66 +79,88 @@ def tile_list_layering_chain_features_kernel(
             return words
 
         tab_w = [load_table_words(0)]
+        for q in range(4):
+            nc.sync.dma_start(tab_s[32 * q : 32 * q + 8, :].bitcast(I32), tab_scales.bitcast(I32)[:, 4 * q : 4 * q + 4, :])
         for s in range(4):
-            nc.sync.dma_start(
-                tab_s[s:P:32, :].bitcast(I32), tab_scales[0].bitcast(I32).rearrange("(q s) n -> s q n", s=4)[s]
-            )
-        nc.sync.dma_start(tab_s[4:P:8, :].bitcast(I32), tab_scales[1].bitcast(I32))
-        w1_raw = place([P, PASSES, H // 2], I32, "w1_raw", AT_W1_RAW)
+            nc.sync.dma_start(loaded_s[s:P:32, :, :], scale_rows(w1_scales)[s])
+        w1_raw = keep.tile([P, PASSES, H // 2], I32, name="w1_raw")
         nc.sync.dma_start(w1_raw[:], w1_words.bitcast(I32).rearrange("a p c -> p a c"))
         tab_w.append(load_table_words(1))
 
-        v_s0 = keep.tile([P, S], U8, name="v_s0", align_bytes=64)
-        nc.vector.tensor_copy(v_s0[:], tab_s[:].indirect(idx[:]))
-        for s in range(4):
-            nc.sync.dma_start(v_s1[s:P:32, :].bitcast(I32), v_s0[8 * s + 4 : P : 32, :].bitcast(I32))
-        v_s = (v_s0, v_s1)
-        v_w, w1_w, w1_s, w2_raw = {}, {}, {}, {}
+        v_w = {}
 
-        def gather_words(a, h):
-            if (a, h) == (0, 1):
-                v_w[a, h] = place([P, BANK], U32, "v_w01", AT_SECOND_HALF)
-            else:
-                v_w[a, h] = keep.tile([P, BANK], U32, name="v_w%d%d" % (a, h), align_bytes=64)
+        def pick_words(a, h):
+            v_w[a, h] = keep.tile([P, BANK], U32, name="v_w%d%d" % (a, h), align_bytes=64)
             entries = idx[:, h * BANK // 16 : (h + 1) * BANK // 16]
             nc.vector.tensor_copy(v_w[a, h][:], tab_w[a][:].bitcast(U32).indirect(entries))
 
-        def order_w1(a):
-            w1_s[a] = place([P, H], U8, "w1_s%d" % a, AT_W1_SCALES + a)
-            nc.vector.tensor_copy(
-                w1_s[a][:].bitcast(I32).rearrange("p (b t g w) -> p b t g w", b=PASSES, t=PACK, w=2),
-                w1_s_raw[:, a, :].rearrange("p (b g t w) -> p b t g w", b=PASSES, t=PACK, w=2),
-            )
-            w1_w[a] = place([P, H // 2], I32, "w1_w%d" % a, AT_W1_WORDS + 2 * a)
-            nc.vector.tensor_copy(
-                w1_w[a][:].rearrange("p (b t g w) -> p b t g w", b=PASSES, t=PACK, w=4),
-                w1_raw[:, a, :].rearrange("p (b g t w) -> p b t g w", b=PASSES, t=PACK, w=4),
-            )
+        pick_words(0, 0)
+        pick_words(0, 1)
+        v_s0 = keep.tile([P, S], U8, name="v_s0", align_bytes=64)
+        nc.vector.tensor_copy(v_s0[:], tab_s[:].indirect(idx[:]))
+        for s in range(4):
+            nc.sync.dma_start(v_s1[s:P:32, :].bitcast(I32), v_s0[4 + s : P : 32, :].bitcast(I32))
+        v_s = (v_s0, v_s1)
 
-        def load_w2(b):
-            for a in range(PASSES):
-                w2_raw[b, a] = place([P, PACK, SPAN], F32, "w2_raw%d%d" % (b, a), AT_W2[b][a])
-                piece = w2[SPAN * a : SPAN * (a + 1), SPAN * b : SPAN * (b + 1)]
-                nc.sync.dma_start(w2_raw[b, a][:], piece.rearrange("(p i) c -> p i c", i=PACK))
+        w1_s = place([P, PASSES * H // 4], I32, "w1_s", AT_W1_SCALES)
+        nc.vector.tensor_copy(
+            w1_s[:].rearrange("p (f t c) -> p f t c", f=4, t=PACK),
+            loaded_s[:].rearrange("p a (b c t) -> p (a b) t c", b=PASSES, t=PACK),
+        )
+        w1_w = place([P, PASSES * H // 2], I32, "w1_w", AT_W1_WORDS)
+        nc.vector.tensor_copy(
+            w1_w[:].rearrange("p (f t c w) -> p f t c w", f=4, t=PACK, w=2),
+            w1_raw[:].rearrange("p a (b c t w) -> p (a b) t c w", b=PASSES, t=PACK, w=2),
+        )
 
-        gather_words(0, 0)
-        gather_words(0, 1)
-        load_w2(0)
-        for a in range(PASSES):
-            order_w1(a)
-        gather_words(1, 0)
-        gather_words(1, 1)
-        load_w2(1)
+        raw = {}
 
-        w3_raw = place([P, PASSES, PACK, N], F32, "w3_raw", AT_W3)
-        for b in range(PASSES):
-            by_slot = w3[SPAN * b : SPAN * (b + 1), :].rearrange("(g t j) n -> t g j n", t=PACK, j=8)
+        def load_rows(name, rows, kib):
+            raw[name] = place([P, PACK, rows.shape[1]], F32, name + "_raw", kib)
+            nc.sync.dma_start(raw[name][:], rows.rearrange("(p i) c -> p i c", i=PACK))
+
+        def load_w2(b, a):
+            load_rows("w2_%d%d" % (b, a), w2[SPAN * a : SPAN * (a + 1), SPAN * b : SPAN * (b + 1)], AT_W2[b][a])
+
+        def load_w3(b):
+            name = "w3_%d" % b
+            raw[name] = place([P, PACK, N], F32, name + "_raw", AT_W3[b])
+            by_slot = w3[SPAN * b : SPAN * (b + 1), :].rearrange("(c t e) n -> t c e n", t=PACK, e=4)
             for t in range(PACK):
-                nc.sync.dma_start(w3_raw[:, b, t, :], by_slot[t])
+                nc.sync.dma_start(raw[name][:, t, :], by_slot[t])
 
-        x1_ps, u_ps, sq, sig, hop_window, deposit = {}, {}, {}, {}, {}, {}
-        gate2, gate3, product, withdrawal = {}, {}, {}, {}
-        w2_bf, w2_w, w2_s = {}, {}, {}
+        load_w2(0, 0)
+        load_w2(0, 1)
+        pick_words(1, 0)
+        pick_words(1, 1)
+
+        staged, codes = {}, {}
+
+        def cast_w2(name, b, a, t0, t1, kib):
+            staged[name] = place([P, (t1 - t0) * SPAN], BF16, name + "_bf", kib)
+            nc.vector.tensor_copy(
+                staged[name][:].rearrange("p (t c e i) -> p t c i e", e=4, i=PACK, t=t1 - t0),
+                raw["w2_%d%d" % (b, a)][:].rearrange("p i (c t e) -> p t c i e", t=PACK, e=4)[:, t0:t1],
+            )
+
+        def cast_rows(name, kib):
+            staged[name] = place([P, PACK * N], BF16, name + "_bf", kib)
+            nc.vector.tensor_copy(
+                staged[name][:].rearrange("p (c e t) -> p c t e", e=4, t=PACK),
+                raw[name][:].rearrange("p t (c e) -> p c t e", e=4),
+            )
+
+        def quantize(name, kib=None):
+            columns = staged[name].shape[1] // PACK
+            if kib is None:
+                words = keep.tile([P, columns], U32, name=name + "_w", align_bytes=64)
+            else:
+                words = place([P, columns], U32, name + "_w", kib)
+            scales = keep.tile([P, columns], U8, name=name + "_s", align_bytes=64)
+            nc.vector.quantize_mx(out=words[:].bitcast(FP8X4), scales=scales[:], in_=staged[name][:])
+            codes[name] = (words, scales)
+
+        x1_ps, u_ps, gate, x2, deposit, product, withdrawal = {}, {}, {}, {}, {}, {}, {}
 
         def first_stage_product(tag, words, scales):
             banks = []
@@ -168,259 +182,136 @@ def tile_list_layering_chain_features_kernel(
         def x1_product(i):
             x1_ps[i] = first_stage_product(
                 "x1",
-                lambda a: w1_w[a][:, P // 2 * i : P // 2 * (i + 1)].bitcast(FP4X4),
-                lambda a: w1_s[a][:, P * i : P * (i + 1)],
+                lambda a: w1_w[:, P // 2 * (ROW_TILES * a + i) : P // 2 * (ROW_TILES * a + i + 1)].bitcast(FP4X4),
+                lambda a: w1_s[:, P // 4 * (ROW_TILES * a + i) : P // 4 * (ROW_TILES * a + i + 1)].bitcast(U8),
             )
+
+        def w2_codes(i, a):
+            b, t = divmod(i, PACK)
+            name = "w2_%d%d" % (b, a)
+            if name == "w2_01":
+                name, t = name + "ab"[t // 2], t % 2
+            words, scales = codes[name]
+            return words[:, P * t : P * (t + 1)].bitcast(FP8X4), scales[:, P * t : P * (t + 1)]
 
         def u_product(i):
-            b, t = divmod(i, PACK)
-            u_ps[i] = first_stage_product(
-                "u",
-                lambda a: w2_w[b, a][:, P * t : P * (t + 1)].bitcast(FP8X4),
-                lambda a: w2_s[b, a][:, P * t : P * (t + 1)],
-            )
+            u_ps[i] = first_stage_product("u", lambda a: w2_codes(i, a)[0], lambda a: w2_codes(i, a)[1])
 
-        def square(i, h):
-            if h == 0 and i < len(AT_SQUARES):
-                sq[i] = place([P, S], F32, "sq%d" % i, AT_SQUARES[i])
-            elif h == 0:
-                sq[i] = work.tile([P, S], F32, name="sq")
-            nc.scalar.activation(sq[i][:, BANK * h : BANK * (h + 1)], x1_ps[i][h][:], ACT.Square)
+        def from_x1(i):
+            x1_product(i)
+            squares = place([P, S], F32, "squares%d" % i, AT_WINDOW + 4 * (i % RING))
+            for h, kib in enumerate((AT_GATE0[i], AT_GATE1 + 4 * (i % RING))):
+                gate[i, h] = place([P, BANK], F32, "gate%d%d" % (i, h), kib)
+                nc.scalar.activation(gate[i, h][:], x1_ps[i][h][:], ACT.Sigmoid)
+                nc.scalar.activation(squares[:, BANK * h : BANK * (h + 1)], x1_ps[i][h][:], ACT.Square)
+            deposit[i] = work.tile([P, M], F32, name="deposit")
+            nc.scalar.activation(deposit[i][:], squares[:].indirect(p1[:]), ACT.Copy)
 
-        def sigmoid(i, h):
-            if h == 0:
-                sig[i] = work.tile([P, S], F32, name="sig", tag="from_x1")
-            nc.scalar.activation(sig[i][:, BANK * h : BANK * (h + 1)], x1_ps[i][h][:], ACT.Sigmoid)
-
-        def gate(i):
-            hop_window[i] = work.tile([P, S], F32, name="x2", tag="hop_window", bufs=2)
+        def make_x2(i):
+            x2[i] = place([P, S], F32, "x2_%d" % i, AT_WINDOW + 4 * (i % RING))
             for h in range(2):
-                cols = slice(BANK * h, BANK * (h + 1))
-                nc.vector.tensor_tensor(hop_window[i][:, cols], u_ps[i][h][:], sig[i][:, cols], ALU.mult)
-
-        def picked_gates(i):
-            x1_sb = work.tile([P, S], F32, name="x1_sb", tag="from_x1")
-            for h in range(2):
-                nc.scalar.copy(x1_sb[:, BANK * h : BANK * (h + 1)], x1_ps[i][h][:])
-            gate2[i] = work.tile([P, M], F32, name="gate2", bufs=2)
-            nc.scalar.activation(gate2[i][:], x1_sb[:].indirect(p2[:]), ACT.Sigmoid)
-            gate3[i] = work.tile([P, M], F32, name="gate3", bufs=2)
-            nc.scalar.activation(gate3[i][:], x1_sb[:].indirect(p3[:]), ACT.Sigmoid)
-
-        def copy_u(i):
-            hop_window[i] = work.tile([P, S], F32, name="u_sb", tag="hop_window", bufs=2)
-            for h in range(2):
-                nc.scalar.copy(hop_window[i][:, BANK * h : BANK * (h + 1)], u_ps[i][h][:])
-
-        def pick_deposit(i):
-            if i < len(AT_FIRST_DEPOSITS):
-                deposit[i] = place([P, M], F32, "deposit%d" % i, AT_FIRST_DEPOSITS[i])
-            else:
-                deposit[i] = work.tile([P, M], F32, name="deposit")
-            picked = sq[i][:].indirect(p1[:])
-            if gate_after_pick(i):
-                nc.vector.tensor_tensor(deposit[i][:], picked, gate2[i][:], ALU.mult)
-            else:
-                nc.vector.tensor_copy(deposit[i][:], picked)
+                nc.vector.tensor_tensor(x2[i][:, BANK * h : BANK * (h + 1)], u_ps[i][h][:], gate[i, h][:], ALU.mult)
 
         def pick_withdrawal(i, lo, hi):
             b, t = divmod(i, PACK)
             if t == 0:
                 withdrawal[b] = work.tile([P, PACK, M], F32, name="withdrawal", bufs=2)
-            picked = hop_window[i][:].indirect(p3[:, lo // 16 : hi // 16])
-            if gate_after_pick(i):
-                nc.vector.tensor_tensor(withdrawal[b][:, t, lo:hi], picked, gate3[i][:, lo:hi], ALU.mult)
-            else:
-                nc.vector.tensor_copy(withdrawal[b][:, t, lo:hi], picked)
+            nc.scalar.activation(withdrawal[b][:, t, lo:hi], x2[i][:].indirect(p3[:, lo // 16 : hi // 16]), ACT.Copy)
 
         def pick_hop(i, lo, hi):
             b, t = divmod(i, PACK)
             if t == 0:
                 product[b] = work.tile([P, PACK, M], F32, name="product", bufs=2)
-            picked = hop_window[i][:].indirect(p2[:, lo // 16 : hi // 16])
+            picked = x2[i][:].indirect(p2[:, lo // 16 : hi // 16])
             nc.vector.tensor_tensor(product[b][:, t, lo:hi], picked, deposit[i][:, lo:hi], ALU.mult)
 
-        def cast_w2(copy, staging, b, a, t0, t1):
-            for t in range(t0, t1):
-                w2_bf[b, a, t] = staging
-                copy(
-                    staging[:, t - t0, :].rearrange("p (g u e i) -> p g u i e", u=2, e=4, i=PACK),
-                    w2_raw[b, a][:].rearrange("p i (g t u e) -> p t g u i e", t=PACK, u=2, e=4)[:, t],
-                )
-
-        def quantize_w2(b, a, t0, t1):
-            if t0 == 0:
-                w2_w[b, a] = keep.tile([P, SPAN], U32, name="w2_w%d%d" % (b, a), align_bytes=64)
-                w2_s[b, a] = keep.tile([P, SPAN], U8, name="w2_s%d%d" % (b, a), align_bytes=64)
-            nc.vector.quantize_mx(
-                out=w2_w[b, a][:, P * t0 : P * t1].bitcast(FP8X4),
-                scales=w2_s[b, a][:, P * t0 : P * t1],
-                in_=w2_bf[b, a, t0][:].rearrange("p t c -> p (t c)"),
-            )
-
-        z_bf, z_q, operand_bf, operand_q = {}, {}, {}, {}
-        operand_raw = {"w3_0": w3_raw[:, 0], "w3_1": w3_raw[:, 1]}
-        operands = ("w3_0", "prior_0", "prior_1", "w3_1")
-
-        def quantize(name, staged):
-            words = keep.tile([P, staged.shape[1]], U32, name=name + "_w", align_bytes=64)
-            scales = keep.tile([P, staged.shape[1]], U8, name=name + "_s", align_bytes=64)
-            nc.vector.quantize_mx(
-                out=words[:].bitcast(FP8X4), scales=scales[:], in_=staged[:].rearrange("p c t -> p (c t)")
-            )
-            return words, scales
-
-        def larger(b, lo, hi):
-            z_bf[b, lo] = work.tile([P, hi - lo, PACK], BF16, name="z_bf", align_bytes=64, bufs=1)
+        def larger(name, b, lo, hi, kib):
+            staged[name] = place([P, (hi - lo) * PACK], BF16, name + "_bf", kib)
             nc.vector.tensor_tensor(
-                z_bf[b, lo][:].rearrange("p (c e) t -> p c t e", e=2),
+                staged[name][:].rearrange("p (c e t) -> p c t e", e=2, t=PACK),
                 product[b][:, :, lo:hi].rearrange("p t (c e) -> p c t e", e=2),
                 withdrawal[b][:, :, lo:hi].rearrange("p t (c e) -> p c t e", e=2),
                 ALU.max,
             )
 
-        def quantize_z(b, lo):
-            z_q[b, lo] = quantize("z%d_%d" % (b, lo), z_bf[b, lo])
+        from_x1(0)
+        cast_w2("w2_00", 0, 0, 0, PACK, AT_FIRST_CASTS[0])
+        quantize("w2_00")
+        load_w2(1, 0)
+        load_w2(1, 1)
+        cast_w2("w2_01a", 0, 1, 0, 2, AT_FIRST_CASTS[1])
+        quantize("w2_01a")
+        cast_w2("w2_01b", 0, 1, 2, PACK, AT_FIRST_CASTS[2])
+        load_w3(0)
+        for s in range(4):
+            nc.sync.dma_start(loaded_s[s:P:32, :, : N // 4], scale_rows(w4_scales)[s])
 
-        def load_prior():
-            for b in range(PASSES):
-                rows = place([P, PACK, M], F32, "prior_raw%d" % b, AT_W2[0][b])
-                nc.sync.dma_start(rows[:], prior[SPAN * b : SPAN * (b + 1), :].rearrange("(p i) m -> p i m", i=PACK))
-                operand_raw["prior_%d" % b] = rows[:]
-
-        def load_w4():
-            scales = place([P, PASSES, N], U8, "w4_s", AT_W4_SCALES)
-            nc.gpsimd.memset(scales[:].rearrange("p a n -> p (a n)").bitcast(I32), 0)
-            words = place([P, PASSES, N], I32, "w4_w", AT_W4_WORDS)
-            nc.sync.dma_start(
-                words[:], w4_words.rearrange("a p c i -> a p (c i)").bitcast(I32).rearrange("a p c -> p a c")
-            )
-            for s in range(4):
-                nc.sync.dma_start(scales[s:P:32, :, :].bitcast(I32), scale_rows(w4_scales)[s])
-            return words, scales
-
-        def cast_operand(n):
-            name = operands[n]
-            operand_bf[name] = place([P, N, PACK], BF16, name + "_bf", AT_SQUARES[n % 2])
-            for lo in range(0, N, N // 2):
-                cols = slice(lo, lo + N // 2)
-                nc.scalar.copy(
-                    operand_bf[name][:, cols, :].rearrange("p (c e) t -> p c t e", e=4),
-                    operand_raw[name][:, :, cols].rearrange("p t (c e) -> p c t e", e=4),
-                )
-
-        def quantize_operand(n):
-            operand_q[operands[n]] = quantize(operands[n], operand_bf[operands[n]])
-
-        x1_product(0)
-        sigmoid(0, 0)
-        square(0, 0)
-        square(0, 1)
-        x1_product(1)
-        square(1, 0)
-        square(1, 1)
-        cast_w2(nc.vector.tensor_copy, place([P, PACK, SPAN], BF16, "w2_bf00", AT_FIRST_CASTS[0]), 0, 0, 0, PACK)
-        cast_w2(nc.vector.tensor_copy, place([P, 2, SPAN], BF16, "w2_bf01a", AT_FIRST_CASTS[1]), 0, 1, 0, 2)
-        quantize_w2(0, 0, 0, PACK)
-        quantize_w2(0, 1, 0, 2)
-        pick_deposit(0)
-        pick_deposit(1)
-
-        def start_row_tile(i):
-            x1_product(i)
-            square(i, 0)
-            if gate_after_pick(i):
-                square(i, 1)
-                picked_gates(i)
-                pick_deposit(i)
-                copy_u(i)
-            else:
-                sigmoid(i, 0)
-                sigmoid(i, 1)
-                gate(i)
-                square(i, 1)
-                pick_deposit(i)
-
-        def finish_row_tile(i):
-            pick_withdrawal(i, 0, M)
-            pick_hop(i, 0, M)
-
-        u_product(0)
-        sigmoid(0, 1)
-        gate(0)
-        sigmoid(1, 0)
-        sigmoid(1, 1)
-        cast_w2(nc.scalar.copy, place([P, 2, SPAN], BF16, "w2_bf01b", AT_SQUARES[0]), 0, 1, 2, PACK)
-        quantize_w2(0, 1, 2, PACK)
-        finish_row_tile(0)
-        load_prior()
-
-        for i in range(1, ROW_TILES):
+        operands = ("w2_01b", "w2_10", "w2_11", "w3_0", "prior_0", "z_0", "prior_1", "w3_1")
+        for i in range(ROW_TILES):
             u_product(i)
-            if i == 1:
-                gate(i)
-            else:
-                start_row_tile(i)
-            if i <= PASSES:
-                staging = work.tile([P, PACK, SPAN], BF16, name="w2_bf1", align_bytes=64, bufs=2)
-                cast_w2(nc.scalar.copy, staging, 1, i - 1, 0, PACK)
-            if i == PACK:
-                quantize_z(0, 0)
             if i < LAST:
-                finish_row_tile(i)
-            if i == 1:
-                w4_w, w4_s = load_w4()
-            if i <= PASSES:
-                quantize_w2(1, i - 1, 0, PACK)
-            if 0 <= i - FIRST_OPERAND_CAST < len(operands) - 1:
-                cast_operand(i - FIRST_OPERAND_CAST)
-                quantize_operand(i - FIRST_OPERAND_CAST)
-            if i == PACK - 1:
-                larger(0, 0, M)
+                from_x1(i + 1)
+            make_x2(i)
+            quantize(operands[i], AT_GATE0[i])
+            if i == 0:
+                w4_w = place([P, PASSES, N], I32, "w4_w", AT_W4_WORDS)
+                nc.sync.dma_start(
+                    w4_w[:], w4_words.rearrange("a p c i -> a p (c i)").bitcast(I32).rearrange("a p c -> p a c")
+                )
+            if i == LAST:
+                break
+            pick_hop(i, 0, M)
+            pick_withdrawal(i, 0, M)
+            name, kib = operands[i + 1], AT_GATE1 + 4 * (i % RING)
+            if name == "z_0":
+                larger(name, 0, 0, M, kib)
+            elif name in ("w2_10", "w2_11"):
+                cast_w2(name, 1, i, 0, PACK, kib)
+                load_rows("prior_%d" % i, prior[SPAN * i : SPAN * (i + 1), :], AT_PRIOR[i])
+            else:
+                cast_rows(name, kib)
+                if name == "w3_0":
+                    load_w3(1)
 
-        cast_operand(len(operands) - 1)
-        pick_withdrawal(LAST, 0, CHUNK)
-        pick_hop(LAST, 0, CHUNK)
-        pick_withdrawal(LAST, CHUNK, M)
-        quantize_operand(len(operands) - 1)
-        larger(1, 0, CHUNK)
-        pick_hop(LAST, CHUNK, M)
+        for lo in range(0, M, M // 2):
+            pick_withdrawal(LAST, lo, lo + M // 2)
+            pick_hop(LAST, lo, lo + M // 2)
 
-        def y_pass(bank, weights, weight_scales, moving, moving_scales, start, stop):
+        def y_pass(bank, n0, weights, moving, start, stop):
             nc.tensor.matmul_mx(
-                out=bank[:],
-                lhsT=weights.bitcast(FP8X4),
-                lhsT_scale=weight_scales,
-                rhs=moving.bitcast(FP8X4),
-                rhs_scale=moving_scales,
+                out=bank[:, n0 // P, :],
+                lhsT=weights[0][:, n0 : n0 + P].bitcast(FP8X4),
+                lhsT_scale=weights[1][:, n0 : n0 + P],
+                rhs=moving[0].bitcast(FP8X4),
+                rhs_scale=moving[1],
                 start=start,
                 stop=stop,
             )
 
+        def columns(name, lo):
+            return [plane[:, lo : lo + CHUNK] for plane in codes[name]]
+
+        for b in range(PASSES):
+            codes["w4_%d" % b] = (w4_w[:, b, :], loaded_s[:, b, : N // 4].bitcast(U8))
+        chunks = range(0, M, CHUNK)
         y_ps = {}
-        for lo, tag in ((0, "x1"), (CHUNK, "u")):
-            cols = slice(lo, lo + CHUNK)
+        for lo in chunks:
+            y_ps[lo] = psum.tile([P, N // P, CHUNK], F32, name="y", tag="x1")
+            for weights, moving in (("w3_0", "z_0"), ("w4_0", "prior_0"), ("w4_1", "prior_1")):
+                for n0 in range(0, N, P):
+                    y_pass(y_ps[lo], n0, codes[weights], columns(moving, lo), weights == "w3_0" and n0 == 0, False)
+
+        def finish(lo):
+            name = "z_1_%d" % lo
+            quantize(name)
             for n0 in range(0, N, P):
-                rows = slice(n0, n0 + P)
-                bank = psum.tile([P, CHUNK], F32, name="y", tag=tag)
-                w3_w, w3_s = operand_q["w3_0"]
-                z_w, z_s = z_q[0, 0]
-                y_pass(bank, w3_w[:, rows], w3_s[:, rows], z_w[:, cols], z_s[:, cols], True, False)
-                for b in range(PASSES):
-                    prior_w, prior_s = operand_q["prior_%d" % b]
-                    y_pass(
-                        bank, w4_w[:, b, rows], w4_s[:, b, rows], prior_w[:, cols], prior_s[:, cols], False, False
-                    )
-                y_ps[lo, n0] = bank
-        quantize_z(1, 0)
-        larger(1, CHUNK, M)
-        quantize_z(1, CHUNK)
-        for lo in range(0, M, CHUNK):
-            for n0 in range(0, N, P):
-                rows = slice(n0, n0 + P)
-                w3_w, w3_s = operand_q["w3_1"]
-                z_w, z_s = z_q[1, lo]
-                y_pass(y_ps[lo, n0], w3_w[:, rows], w3_s[:, rows], z_w[:], z_s[:], False, True)
-                result = work.tile([P, CHUNK], F32, name="result", bufs=8)
-                nc.scalar.activation(result[:], y_ps[lo, n0][:], ACT.Sin)
-                nc.sync.dma_start(out[rows, lo : lo + CHUNK], result[:])
+                y_pass(y_ps[lo], n0, codes["w3_1"], columns(name, 0), False, n0 == N - P)
+            result = work.tile([P, N // P, CHUNK], F32, name="result", bufs=len(chunks))
+            nc.scalar.activation(result[:], y_ps[lo][:], ACT.Sin)
+            nc.sync.dma_start(out[:, lo : lo + CHUNK].rearrange("(j p) m -> p j m", p=P), result[:])
+
+        for lo in chunks:
+            larger("z_1_%d" % lo, 1, lo, lo + CHUNK, AT_GATE1 + 4 * (LAST % RING) + lo // CHUNK)
+            if lo > 0:
+                finish(lo - CHUNK)
+        finish(M - CHUNK)

@@ -24,6 +24,9 @@ BANK = 512
 ROW_TILES = PASSES * PACK
 LAST = ROW_TILES - 1
 CHUNK = 128
+PAIRS = 4
+Y_BANKS = (0, 1, 2, 3, 6)
+WINDOWS = 4
 RING = 3
 
 AT_TABLE = (0, 23)
@@ -31,12 +34,17 @@ AT_TABLE_SCALES = 46
 AT_W1_SCALES, AT_W1_WORDS = 0, 2
 AT_FIRST_CASTS = (23, 27, 29)
 AT_W2 = ((39, 49), (31, 16))
-AT_W3 = (49, 49)
-AT_PRIOR = (31, 16)
+AT_W3 = (49, 16)
+AT_PRIOR = (31, 49)
 AT_W4_WORDS = 27
 AT_GATE0 = (6, 8, 10, 12, 14, 57, 59, 61)
 AT_GATE1 = 63
+AT_DEPOSIT = 95
 AT_WINDOW = 75
+
+
+def deposit_place(i):
+    return AT_FIRST_CASTS[1] - 1 if i == 0 else AT_DEPOSIT + 2 * (i % RING)
 
 
 def tile_list_layering_chain_features_kernel(
@@ -49,10 +57,13 @@ def tile_list_layering_chain_features_kernel(
         keep = ctx.enter_context(tc.tile_pool(name="keep", bufs=1))
         laid = ctx.enter_context(tc.tile_pool(name="laid", bufs=1))
         work = ctx.enter_context(tc.tile_pool(name="work", bufs=RING))
-        psum = ctx.enter_context(tc.psum_pool(name="psum", bufs=4))
+        psum = ctx.enter_context(tc.psum_pool(name="psum", bufs=1))
 
         def place(shape, dtype, name, kib):
             return laid.tile(shape, dtype, name=name, align_bytes=64, offset=int(1024 * kib))
+
+        def bank_tile(shape, name, bank):
+            return psum.tile(shape, F32, name=name, offset=4 * BANK * bank)
 
         def scale_rows(scales):
             return scales.bitcast(I32).rearrange("a (q s) n -> s q a n", s=4)
@@ -79,8 +90,11 @@ def tile_list_layering_chain_features_kernel(
             return words
 
         tab_w = [load_table_words(0)]
-        for q in range(4):
-            nc.sync.dma_start(tab_s[32 * q : 32 * q + 8, :].bitcast(I32), tab_scales.bitcast(I32)[:, 4 * q : 4 * q + 4, :])
+        for s in range(4):
+            nc.sync.dma_start(
+                tab_s[s:P:32, :].bitcast(I32), tab_scales[0].bitcast(I32).rearrange("(q s) n -> s q n", s=4)[s]
+            )
+        nc.sync.dma_start(tab_s[4:P:8, :].bitcast(I32), tab_scales[1].bitcast(I32))
         for s in range(4):
             nc.sync.dma_start(loaded_s[s:P:32, :, :], scale_rows(w1_scales)[s])
         w1_raw = keep.tile([P, PASSES, H // 2], I32, name="w1_raw")
@@ -99,7 +113,7 @@ def tile_list_layering_chain_features_kernel(
         v_s0 = keep.tile([P, S], U8, name="v_s0", align_bytes=64)
         nc.vector.tensor_copy(v_s0[:], tab_s[:].indirect(idx[:]))
         for s in range(4):
-            nc.sync.dma_start(v_s1[s:P:32, :].bitcast(I32), v_s0[4 + s : P : 32, :].bitcast(I32))
+            nc.sync.dma_start(v_s1[s:P:32, :].bitcast(I32), v_s0[8 * s + 4 : P : 32, :].bitcast(I32))
         v_s = (v_s0, v_s1)
 
         w1_s = place([P, PASSES * H // 4], I32, "w1_s", AT_W1_SCALES)
@@ -136,52 +150,64 @@ def tile_list_layering_chain_features_kernel(
 
         staged, codes = {}, {}
 
-        def cast_w2(name, b, a, t0, t1, kib):
-            staged[name] = place([P, (t1 - t0) * SPAN], BF16, name + "_bf", kib)
-            nc.vector.tensor_copy(
-                staged[name][:].rearrange("p (t c e i) -> p t c i e", e=4, i=PACK, t=t1 - t0),
-                raw["w2_%d%d" % (b, a)][:].rearrange("p i (c t e) -> p t c i e", t=PACK, e=4)[:, t0:t1],
-            )
+        def gpsimd_cast(out, in_):
+            nc.gpsimd.tensor_scalar(out, in_, 1.0, 0.0, ALU.mult, ALU.add)
 
-        def cast_rows(name, kib):
-            staged[name] = place([P, PACK * N], BF16, name + "_bf", kib)
-            nc.vector.tensor_copy(
-                staged[name][:].rearrange("p (c e t) -> p c t e", e=4, t=PACK),
-                raw[name][:].rearrange("p t (c e) -> p c t e", e=4),
+        def stage(name, lo, hi, kib):
+            piece = place([P, (hi - lo) * PACK], BF16, "%s_bf%d" % (name, lo), kib)
+            staged.setdefault(name, {})[lo, hi] = piece
+            return piece
+
+        def cast_w2(copy, name, b, a, t0, t1, kib):
+            piece = stage(name, t0 * P, t1 * P, kib)[:].rearrange("p (t c e i) -> p c t i e", e=4, i=PACK, t=t1 - t0)
+            rows = raw["w2_%d%d" % (b, a)][:].rearrange("p i (c t e) -> p c t i e", t=PACK, e=4)[:, :, t0:t1]
+            if t1 - t0 == 1:
+                piece, rows = piece[:, :, 0], rows[:, :, 0]
+            copy(piece, rows)
+
+        def cast_rows(copy, name, lo, hi, kib):
+            copy(
+                stage(name, lo, hi, kib)[:].rearrange("p (c e t) -> p c t e", e=4, t=PACK),
+                raw[name][:, :, lo:hi].rearrange("p t (c e) -> p c t e", e=4),
             )
 
         def quantize(name, kib=None):
-            columns = staged[name].shape[1] // PACK
+            first = min(lo for lo, hi in staged[name])
+            columns = max(hi for lo, hi in staged[name]) - first
             if kib is None:
                 words = keep.tile([P, columns], U32, name=name + "_w", align_bytes=64)
             else:
                 words = place([P, columns], U32, name + "_w", kib)
             scales = keep.tile([P, columns], U8, name=name + "_s", align_bytes=64)
-            nc.vector.quantize_mx(out=words[:].bitcast(FP8X4), scales=scales[:], in_=staged[name][:])
+            for lo, hi in sorted(staged[name]):
+                cols = slice(lo - first, hi - first)
+                nc.vector.quantize_mx(out=words[:, cols].bitcast(FP8X4), scales=scales[:, cols], in_=staged[name][lo, hi][:])
             codes[name] = (words, scales)
 
-        x1_ps, u_ps, gate, x2, deposit, product, withdrawal = {}, {}, {}, {}, {}, {}, {}
+        x1_ps, u_ps, gate, squares, x2, deposit, product, withdrawal = {}, {}, {}, {}, {}, {}, {}, {}
 
-        def first_stage_product(tag, words, scales):
+        def first_stage_product(name, pair, passes, words, scales):
             banks = []
             for h in range(2):
-                bank = psum.tile([P, BANK], F32, name=tag, tag=tag)
-                for a in range(PASSES):
+                bank = bank_tile([P, BANK], "%s_%d" % (name, h), 2 * pair + h)
+                for a in passes:
                     nc.tensor.matmul_mx(
                         out=bank[:],
                         lhsT=words(a),
                         lhsT_scale=scales(a),
                         rhs=v_w[a, h][:].bitcast(FP8X4),
                         rhs_scale=v_s[a][:, BANK * h : BANK * (h + 1)],
-                        start=(a == 0),
-                        stop=(a == PASSES - 1),
+                        start=(a == passes[0]),
+                        stop=(a == passes[-1]),
                     )
                 banks.append(bank)
             return banks
 
         def x1_product(i):
             x1_ps[i] = first_stage_product(
-                "x1",
+                "x1_%d" % i,
+                i % PAIRS,
+                (0, 1) if i == 0 else (1, 0),
                 lambda a: w1_w[:, P // 2 * (ROW_TILES * a + i) : P // 2 * (ROW_TILES * a + i + 1)].bitcast(FP4X4),
                 lambda a: w1_s[:, P // 4 * (ROW_TILES * a + i) : P // 4 * (ROW_TILES * a + i + 1)].bitcast(U8),
             )
@@ -195,20 +221,33 @@ def tile_list_layering_chain_features_kernel(
             return words[:, P * t : P * (t + 1)].bitcast(FP8X4), scales[:, P * t : P * (t + 1)]
 
         def u_product(i):
-            u_ps[i] = first_stage_product("u", lambda a: w2_codes(i, a)[0], lambda a: w2_codes(i, a)[1])
+            passes = (0, 1) if i == 0 else (1, 0)
+            u_ps[i] = first_stage_product(
+                "u_%d" % i, (i - 1) % PAIRS, passes, lambda a: w2_codes(i, a)[0], lambda a: w2_codes(i, a)[1]
+            )
 
         def from_x1(i):
             x1_product(i)
-            squares = place([P, S], F32, "squares%d" % i, AT_WINDOW + 4 * (i % RING))
-            for h, kib in enumerate((AT_GATE0[i], AT_GATE1 + 4 * (i % RING))):
-                gate[i, h] = place([P, BANK], F32, "gate%d%d" % (i, h), kib)
-                nc.scalar.activation(gate[i, h][:], x1_ps[i][h][:], ACT.Sigmoid)
-                nc.scalar.activation(squares[:, BANK * h : BANK * (h + 1)], x1_ps[i][h][:], ACT.Square)
-            deposit[i] = work.tile([P, M], F32, name="deposit")
-            nc.scalar.activation(deposit[i][:], squares[:].indirect(p1[:]), ACT.Copy)
+            squares[i] = place([P, S], F32, "squares%d" % i, AT_WINDOW + 4 * (i % WINDOWS))
+            funcs = (ACT.Square, ACT.Sigmoid) if 0 < i < LAST else (ACT.Sigmoid, ACT.Square)
+            steps = [(h, func) for func in funcs for h in range(2)]
+            for h, func in sorted(steps, key=lambda step: step[0]) if i == 0 else steps:
+                if func == ACT.Sigmoid:
+                    kib = (AT_GATE0[i], AT_GATE1 + 4 * (i % RING))[h]
+                    gate[i, h] = place([P, BANK], F32, "gate%d%d" % (i, h), kib)
+                    nc.scalar.activation(gate[i, h][:], x1_ps[i][h][:], func)
+                else:
+                    nc.scalar.activation(squares[i][:, BANK * h : BANK * (h + 1)], x1_ps[i][h][:], func)
+
+        def pick_deposit(i):
+            deposit[i] = place([P, M], F32, "deposit%d" % i, deposit_place(i))
+            lo = M // 2 if i == 0 else 0
+            if i == 0:
+                nc.vector.tensor_copy(deposit[i][:, :lo], squares[i][:].indirect(p1[:, : lo // 16]))
+            nc.scalar.activation(deposit[i][:, lo:], squares[i][:].indirect(p1[:, lo // 16 :]), ACT.Copy)
 
         def make_x2(i):
-            x2[i] = place([P, S], F32, "x2_%d" % i, AT_WINDOW + 4 * (i % RING))
+            x2[i] = place([P, S], F32, "x2_%d" % i, AT_WINDOW + 4 * (i % WINDOWS if i < LAST else WINDOWS))
             for h in range(2):
                 nc.vector.tensor_tensor(x2[i][:, BANK * h : BANK * (h + 1)], u_ps[i][h][:], gate[i, h][:], ALU.mult)
 
@@ -226,31 +265,35 @@ def tile_list_layering_chain_features_kernel(
             nc.vector.tensor_tensor(product[b][:, t, lo:hi], picked, deposit[i][:, lo:hi], ALU.mult)
 
         def larger(name, b, lo, hi, kib):
-            staged[name] = place([P, (hi - lo) * PACK], BF16, name + "_bf", kib)
             nc.vector.tensor_tensor(
-                staged[name][:].rearrange("p (c e t) -> p c t e", e=2, t=PACK),
+                stage(name, lo, hi, kib)[:].rearrange("p (c e t) -> p c t e", e=2, t=PACK),
                 product[b][:, :, lo:hi].rearrange("p t (c e) -> p c t e", e=2),
                 withdrawal[b][:, :, lo:hi].rearrange("p t (c e) -> p c t e", e=2),
                 ALU.max,
             )
 
         from_x1(0)
-        cast_w2("w2_00", 0, 0, 0, PACK, AT_FIRST_CASTS[0])
+        cast_w2(nc.vector.tensor_copy, "w2_00", 0, 0, 0, PACK, AT_FIRST_CASTS[0])
         quantize("w2_00")
         load_w2(1, 0)
         load_w2(1, 1)
-        cast_w2("w2_01a", 0, 1, 0, 2, AT_FIRST_CASTS[1])
+        cast_w2(nc.vector.tensor_copy, "w2_01a", 0, 1, 0, 2, AT_FIRST_CASTS[1])
+        cast_w2(nc.vector.tensor_copy, "w2_01b", 0, 1, 2, 3, AT_FIRST_CASTS[2])
         quantize("w2_01a")
-        cast_w2("w2_01b", 0, 1, 2, PACK, AT_FIRST_CASTS[2])
+        pick_deposit(0)
+        cast_w2(gpsimd_cast, "w2_01b", 0, 1, 3, PACK, AT_FIRST_CASTS[1] + 1)
         load_w3(0)
         for s in range(4):
             nc.sync.dma_start(loaded_s[s:P:32, :, : N // 4], scale_rows(w4_scales)[s])
 
-        operands = ("w2_01b", "w2_10", "w2_11", "w3_0", "prior_0", "z_0", "prior_1", "w3_1")
+        operands = ("w2_01b", "w2_10", "w2_11", "w3_0", "prior_0", "w3_1", "z_0", "prior_1")
         for i in range(ROW_TILES):
             u_product(i)
             if i < LAST:
                 from_x1(i + 1)
+                pick_deposit(i + 1)
+            if i > 0:
+                pick_withdrawal(i - 1, 0, M)
             make_x2(i)
             quantize(operands[i], AT_GATE0[i])
             if i == 0:
@@ -261,17 +304,24 @@ def tile_list_layering_chain_features_kernel(
             if i == LAST:
                 break
             pick_hop(i, 0, M)
-            pick_withdrawal(i, 0, M)
             name, kib = operands[i + 1], AT_GATE1 + 4 * (i % RING)
+            quarter_kib = deposit_place(i)
             if name == "z_0":
                 larger(name, 0, 0, M, kib)
+                cast_rows(gpsimd_cast, operands[LAST], N - P, N, quarter_kib)
             elif name in ("w2_10", "w2_11"):
-                cast_w2(name, 1, i, 0, PACK, kib)
-                load_rows("prior_%d" % i, prior[SPAN * i : SPAN * (i + 1), :], AT_PRIOR[i])
-            else:
-                cast_rows(name, kib)
-                if name == "w3_0":
+                cast_w2(nc.vector.tensor_copy, name, 1, i, 0, PACK - 1, kib)
+                cast_w2(gpsimd_cast, name, 1, i, PACK - 1, PACK, quarter_kib)
+                if i == 0:
+                    load_rows("prior_0", prior[:SPAN, :], AT_PRIOR[0])
+                else:
                     load_w3(1)
+            else:
+                hi = N - P if name in staged else N
+                cast_rows(nc.vector.tensor_copy, name, 0, hi - P, kib)
+                cast_rows(gpsimd_cast, name, hi - P, hi, quarter_kib)
+                if name == "w3_0":
+                    load_rows("prior_1", prior[SPAN:, :], AT_PRIOR[1])
 
         for lo in range(0, M, M // 2):
             pick_withdrawal(LAST, lo, lo + M // 2)
@@ -279,7 +329,7 @@ def tile_list_layering_chain_features_kernel(
 
         def y_pass(bank, n0, weights, moving, start, stop):
             nc.tensor.matmul_mx(
-                out=bank[:, n0 // P, :],
+                out=bank,
                 lhsT=weights[0][:, n0 : n0 + P].bitcast(FP8X4),
                 lhsT_scale=weights[1][:, n0 : n0 + P],
                 rhs=moving[0].bitcast(FP8X4),
@@ -294,21 +344,26 @@ def tile_list_layering_chain_features_kernel(
         for b in range(PASSES):
             codes["w4_%d" % b] = (w4_w[:, b, :], loaded_s[:, b, : N // 4].bitcast(U8))
         chunks = range(0, M, CHUNK)
+        pieces = [(lo, 0, N) for lo in chunks[:-1]] + [(M - CHUNK, 0, N // 2), (M - CHUNK, N // 2, N)]
         y_ps = {}
-        for lo in chunks:
-            y_ps[lo] = psum.tile([P, N // P, CHUNK], F32, name="y", tag="x1")
+        for (lo, n_lo, n_hi), bank in zip(pieces, Y_BANKS):
+            y_ps[lo, n_lo] = bank_tile([P, (n_hi - n_lo) // P, CHUNK], "y_%d_%d" % (lo, n_lo), bank)
             for weights, moving in (("w3_0", "z_0"), ("w4_0", "prior_0"), ("w4_1", "prior_1")):
-                for n0 in range(0, N, P):
-                    y_pass(y_ps[lo], n0, codes[weights], columns(moving, lo), weights == "w3_0" and n0 == 0, False)
+                for n0 in range(n_lo, n_hi, P):
+                    part = y_ps[lo, n_lo][:, (n0 - n_lo) // P, :]
+                    y_pass(part, n0, codes[weights], columns(moving, lo), weights == "w3_0" and n0 == n_lo, False)
 
-        def finish(lo):
-            name = "z_1_%d" % lo
+        def finish(chunk):
+            name = "z_1_%d" % chunk
             quantize(name)
-            for n0 in range(0, N, P):
-                y_pass(y_ps[lo], n0, codes["w3_1"], columns(name, 0), False, n0 == N - P)
-            result = work.tile([P, N // P, CHUNK], F32, name="result", bufs=len(chunks))
-            nc.scalar.activation(result[:], y_ps[lo][:], ACT.Sin)
-            nc.sync.dma_start(out[:, lo : lo + CHUNK].rearrange("(j p) m -> p j m", p=P), result[:])
+            for lo, n_lo, n_hi in pieces:
+                if lo == chunk:
+                    for n0 in range(n_lo, n_hi, P):
+                        part = y_ps[lo, n_lo][:, (n0 - n_lo) // P, :]
+                        y_pass(part, n0, codes["w3_1"], columns(name, 0), False, n0 == n_hi - P)
+                    result = keep.tile([P, (n_hi - n_lo) // P, CHUNK], F32, name="result_%d_%d" % (lo, n_lo))
+                    nc.scalar.activation(result[:], y_ps[lo, n_lo][:], ACT.Sin)
+                    nc.sync.dma_start(out[n_lo:n_hi, lo : lo + CHUNK].rearrange("(j p) m -> p j m", p=P), result[:])
 
         for lo in chunks:
             larger("z_1_%d" % lo, 1, lo, lo + CHUNK, AT_GATE1 + 4 * (LAST % RING) + lo // CHUNK)

@@ -29,18 +29,18 @@ Y_BANKS = (0, 1, 2, 3, 6)
 WINDOWS = 4
 RING = 3
 
-AT_TABLE = (0, 23)
-AT_TABLE_SCALES = 46
-AT_W1_SCALES, AT_W1_WORDS = 0, 2
-AT_FIRST_CASTS = (23, 27, 29)
-AT_W2 = ((39, 49), (31, 16))
-AT_W3 = (49, 16)
-AT_PRIOR = (31, 49)
-AT_W4_WORDS = 27
-AT_GATE0 = (6, 8, 10, 12, 14, 57, 59, 61)
-AT_GATE1 = 63
-AT_DEPOSIT = 95
-AT_WINDOW = 75
+AT_TABLE = (7, 33)
+AT_TABLE_SCALES = 30
+AT_W1_SCALES, AT_W1_WORDS = 8, 10
+AT_FIRST_CASTS = (33, 37, 39)
+AT_W2 = ((0, 22), (40, 48))
+AT_W3 = (22, 48)
+AT_PRIOR = (40, 22)
+AT_W4_WORDS = 0
+AT_GATE0 = (14, 16, 18, 20, 56, 58, 60, 62)
+AT_GATE1 = 64
+AT_WINDOW = 76
+AT_DEPOSIT = 96
 
 
 def deposit_place(i):
@@ -69,38 +69,44 @@ def tile_list_layering_chain_features_kernel(
             return scales.bitcast(I32).rearrange("a (q s) n -> s q a n", s=4)
 
         tab_s = place([P, T], U8, "tab_s", AT_TABLE_SCALES)
-        nc.vector.memset(tab_s[:].bitcast(I32), 0)
+        nc.vector.memset(tab_s[:, : T // 2].bitcast(I32), 0)
+        nc.gpsimd.memset(tab_s[:, T // 2 :].bitcast(I32), 0)
         loaded_s = keep.tile([P, PASSES, H // 4], I32, name="loaded_s", align_bytes=64)
         nc.gpsimd.memset(loaded_s[:], 0)
-        v_s1 = keep.tile([P, S], U8, name="v_s1", align_bytes=64)
-        nc.vector.memset(v_s1[:].bitcast(I32), 0)
+        v_s = keep.tile([P, PASSES, S], U8, name="v_s", align_bytes=64)
+        nc.vector.memset(v_s[:].rearrange("p a n -> p (a n)").bitcast(I32), 0)
 
         idx = lists.tile([P, S // 16], U16, name="idx")
         p1 = lists.tile([P, M // 16], U16, name="p1")
         p2 = lists.tile([P, M // 16], U16, name="p2")
         p3 = lists.tile([P, M // 16], U16, name="p3")
+        tab_w = [place([P, T], I32, "tab_w%d" % a, AT_TABLE[a]) for a in range(PASSES)]
+
+        def load_table_words(a, lo, hi):
+            cols = slice(lo, hi)
+            nc.sync.dma_start(tab_w[a][:, cols], tab_words[a].rearrange("p t i -> p (t i)").bitcast(I32)[:, cols])
+
         nc.sync.dma_start(idx[:], offs)
+        load_table_words(0, 0, T // 4)
+        nc.sync.dma_start(tab_s[0:P:4, :].bitcast(I32), tab_scales.bitcast(I32).rearrange("a m n -> (a m) n"))
+        w1_raw = keep.tile([P, PASSES, H // 2], I32, name="w1_raw")
+        nc.sync.dma_start(w1_raw[:], w1_words.bitcast(I32).rearrange("a p c -> p a c"))
         nc.sync.dma_start(p1[:], pos1)
         nc.sync.dma_start(p2[:], pos2)
         nc.sync.dma_start(p3[:], pos3)
-
-        def load_table_words(a):
-            words = place([P, T], I32, "tab_w%d" % a, AT_TABLE[a])
-            nc.sync.dma_start(words[:], tab_words[a].rearrange("p t i -> p (t i)").bitcast(I32))
-            return words
-
-        tab_w = [load_table_words(0)]
-        for s in range(4):
-            nc.sync.dma_start(
-                tab_s[s:P:32, :].bitcast(I32), tab_scales[0].bitcast(I32).rearrange("(q s) n -> s q n", s=4)[s]
-            )
-        nc.sync.dma_start(tab_s[4:P:8, :].bitcast(I32), tab_scales[1].bitcast(I32))
+        load_table_words(0, T // 4, T)
         for s in range(4):
             nc.sync.dma_start(loaded_s[s:P:32, :, :], scale_rows(w1_scales)[s])
-        w1_raw = keep.tile([P, PASSES, H // 2], I32, name="w1_raw")
-        nc.sync.dma_start(w1_raw[:], w1_words.bitcast(I32).rearrange("a p c -> p a c"))
-        tab_w.append(load_table_words(1))
 
+        picked_s = keep.tile([P, S], U8, name="picked_s")
+        nc.vector.tensor_copy(picked_s[:], tab_s[:].indirect(idx[:]))
+        for a in range(PASSES):
+            for s in range(4):
+                rows = picked_s[64 * a + 4 * s : 64 * (a + 1) : 16, :]
+                nc.sync.dma_start(v_s[s:P:32, a, :].bitcast(I32), rows.bitcast(I32))
+                if (a, s) == (0, 1):
+                    load_table_words(1, 0, T // 2)
+        load_table_words(1, T // 2, T)
         v_w = {}
 
         def pick_words(a, h):
@@ -110,11 +116,6 @@ def tile_list_layering_chain_features_kernel(
 
         pick_words(0, 0)
         pick_words(0, 1)
-        v_s0 = keep.tile([P, S], U8, name="v_s0", align_bytes=64)
-        nc.vector.tensor_copy(v_s0[:], tab_s[:].indirect(idx[:]))
-        for s in range(4):
-            nc.sync.dma_start(v_s1[s:P:32, :].bitcast(I32), v_s0[8 * s + 4 : P : 32, :].bitcast(I32))
-        v_s = (v_s0, v_s1)
 
         w1_s = place([P, PASSES * H // 4], I32, "w1_s", AT_W1_SCALES)
         nc.vector.tensor_copy(
@@ -196,7 +197,7 @@ def tile_list_layering_chain_features_kernel(
                         lhsT=words(a),
                         lhsT_scale=scales(a),
                         rhs=v_w[a, h][:].bitcast(FP8X4),
-                        rhs_scale=v_s[a][:, BANK * h : BANK * (h + 1)],
+                        rhs_scale=v_s[:, a, BANK * h : BANK * (h + 1)],
                         start=(a == passes[0]),
                         stop=(a == passes[-1]),
                     )

@@ -27,24 +27,24 @@ CHUNK = 128
 PAIRS = 4
 Y_BANKS = (0, 1, 2, 3, 6)
 WINDOWS = 4
-RING = 3
 
 AT_TABLE = (7, 33)
 AT_TABLE_SCALES = 30
 AT_W1_SCALES, AT_W1_WORDS = 8, 10
-AT_FIRST_CASTS = (33, 37, 39)
+AT_FIRST_CASTS = (30, 37, 34, 36)
 AT_W2 = ((0, 22), (40, 48))
-AT_W3 = (22, 48)
-AT_PRIOR = (40, 22)
-AT_W4_WORDS = 0
+AT_W3 = (0, 40)
+AT_PRIOR_FIRST = 38
+AT_PRIOR = (22, 28)
+AT_W4_WORDS, AT_W4_SCALES = 48, 52
 AT_GATE0 = (14, 16, 18, 20, 56, 58, 60, 62)
 AT_GATE1 = 64
-AT_WINDOW = 76
-AT_DEPOSIT = 96
-
-
-def deposit_place(i):
-    return AT_FIRST_CASTS[1] - 1 if i == 0 else AT_DEPOSIT + 2 * (i % RING)
+AT_LATE_WITHDRAWAL = 89
+AT_LAST_Z = 93
+AT_WINDOW = 98
+AT_DEPOSIT = 118
+SHARE = 192
+WIDTHS = (512, 384, 256, 128, 64)
 
 
 def tile_list_layering_chain_features_kernel(
@@ -56,7 +56,6 @@ def tile_list_layering_chain_features_kernel(
         lists = ctx.enter_context(tc.tile_pool(name="lists", bufs=1))
         keep = ctx.enter_context(tc.tile_pool(name="keep", bufs=1))
         laid = ctx.enter_context(tc.tile_pool(name="laid", bufs=1))
-        work = ctx.enter_context(tc.tile_pool(name="work", bufs=RING))
         psum = ctx.enter_context(tc.psum_pool(name="psum", bufs=1))
 
         def place(shape, dtype, name, kib):
@@ -74,7 +73,6 @@ def tile_list_layering_chain_features_kernel(
         loaded_s = keep.tile([P, PASSES, H // 4], I32, name="loaded_s", align_bytes=64)
         nc.gpsimd.memset(loaded_s[:], 0)
         v_s = keep.tile([P, PASSES, S], U8, name="v_s", align_bytes=64)
-        nc.vector.memset(v_s[:].rearrange("p a n -> p (a n)").bitcast(I32), 0)
 
         idx = lists.tile([P, S // 16], U16, name="idx")
         p1 = lists.tile([P, M // 16], U16, name="p1")
@@ -109,13 +107,14 @@ def tile_list_layering_chain_features_kernel(
         load_table_words(1, T // 2, T)
         v_w = {}
 
-        def pick_words(a, h):
-            v_w[a, h] = keep.tile([P, BANK], U32, name="v_w%d%d" % (a, h), align_bytes=64)
-            entries = idx[:, h * BANK // 16 : (h + 1) * BANK // 16]
-            nc.vector.tensor_copy(v_w[a, h][:], tab_w[a][:].bitcast(U32).indirect(entries))
+        def pick_words(a, cuts):
+            v_w[a] = keep.tile([P, S], U32, name="v_w%d" % a, align_bytes=64)
+            for lo, hi in cuts:
+                nc.vector.tensor_copy(v_w[a][:, lo:hi], tab_w[a][:].bitcast(U32).indirect(idx[:, lo // 16 : hi // 16]))
 
-        pick_words(0, 0)
-        pick_words(0, 1)
+        halves = ((0, BANK), (BANK, S))
+        quarters = ((0, BANK // 2), (BANK // 2, BANK))
+        pick_words(0, halves)
 
         w1_s = place([P, PASSES * H // 4], I32, "w1_s", AT_W1_SCALES)
         nc.vector.tensor_copy(
@@ -146,8 +145,7 @@ def tile_list_layering_chain_features_kernel(
 
         load_w2(0, 0)
         load_w2(0, 1)
-        pick_words(1, 0)
-        pick_words(1, 1)
+        pick_words(1, quarters + halves[1:])
 
         staged, codes = {}, {}
 
@@ -166,10 +164,10 @@ def tile_list_layering_chain_features_kernel(
                 piece, rows = piece[:, :, 0], rows[:, :, 0]
             copy(piece, rows)
 
-        def cast_rows(copy, name, lo, hi, kib):
+        def cast_rows(copy, name, lo, hi, kib, source=None, first=0):
             copy(
                 stage(name, lo, hi, kib)[:].rearrange("p (c e t) -> p c t e", e=4, t=PACK),
-                raw[name][:, :, lo:hi].rearrange("p t (c e) -> p c t e", e=4),
+                raw[source or name][:, :, lo - first : hi - first].rearrange("p t (c e) -> p c t e", e=4),
             )
 
         def quantize(name, kib=None):
@@ -181,152 +179,181 @@ def tile_list_layering_chain_features_kernel(
                 words = place([P, columns], U32, name + "_w", kib)
             scales = keep.tile([P, columns], U8, name=name + "_s", align_bytes=64)
             for lo, hi in sorted(staged[name]):
-                cols = slice(lo - first, hi - first)
-                nc.vector.quantize_mx(out=words[:, cols].bitcast(FP8X4), scales=scales[:, cols], in_=staged[name][lo, hi][:])
-            codes[name] = (words, scales)
+                done = 0
+                while done < hi - lo:
+                    width = max(w for w in WIDTHS if w <= hi - lo - done)
+                    cols = slice(lo - first + done, lo - first + done + width)
+                    part = staged[name][lo, hi][:, PACK * done : PACK * (done + width)]
+                    nc.vector.quantize_mx(out=words[:, cols].bitcast(FP8X4), scales=scales[:, cols], in_=part)
+                    done = done + width
+            codes[name] = (words, scales, first)
 
-        x1_ps, u_ps, gate, squares, x2, deposit, product, withdrawal = {}, {}, {}, {}, {}, {}, {}, {}
+        u_ps, gate, squares, x2, deposit, product, withdrawal = {}, {}, {}, {}, {}, {}, {}
 
-        def first_stage_product(name, pair, passes, words, scales):
-            banks = []
-            for h in range(2):
-                bank = bank_tile([P, BANK], "%s_%d" % (name, h), 2 * pair + h)
-                for a in passes:
-                    nc.tensor.matmul_mx(
-                        out=bank[:],
-                        lhsT=words(a),
-                        lhsT_scale=scales(a),
-                        rhs=v_w[a, h][:].bitcast(FP8X4),
-                        rhs_scale=v_s[:, a, BANK * h : BANK * (h + 1)],
-                        start=(a == passes[0]),
-                        stop=(a == passes[-1]),
-                    )
-                banks.append(bank)
-            return banks
+        def first_stage_product(name, bank, lo, hi, passes, words, scales):
+            sums = bank_tile([P, hi - lo], name, bank)
+            for a in passes:
+                nc.tensor.matmul_mx(
+                    out=sums[:],
+                    lhsT=words(a),
+                    lhsT_scale=scales(a),
+                    rhs=v_w[a][:, lo:hi].bitcast(FP8X4),
+                    rhs_scale=v_s[:, a, lo:hi],
+                    start=(a == passes[0]),
+                    stop=(a == passes[-1]),
+                )
+            return sums
 
-        def x1_product(i):
-            x1_ps[i] = first_stage_product(
-                "x1_%d" % i,
-                i % PAIRS,
-                (0, 1) if i == 0 else (1, 0),
+        def w2_codes(i, a):
+            b, t = divmod(i, PACK)
+            for name in codes:
+                words, scales, first = codes[name]
+                if name.startswith("w2_%d%d" % (b, a)) and first <= P * t < first + scales[:].shape[1]:
+                    cols = slice(P * t - first, P * (t + 1) - first)
+                    return words[:, cols].bitcast(FP8X4), scales[:, cols]
+
+        def u_product(i):
+            passes = (0, 1) if i == 0 else (1, 0)
+            u_ps[i] = [
+                first_stage_product(
+                    "u_%d_%d" % (i, h), 2 * ((i - 1) % PAIRS) + h, lo, hi, passes,
+                    lambda a: w2_codes(i, a)[0], lambda a: w2_codes(i, a)[1],
+                )
+                for h, (lo, hi) in enumerate(halves)
+            ]
+
+        def x1_product(i, lo, hi, bank, passes):
+            return first_stage_product(
+                "x1_%d_%d" % (i, lo), bank, lo, hi, passes,
                 lambda a: w1_w[:, P // 2 * (ROW_TILES * a + i) : P // 2 * (ROW_TILES * a + i + 1)].bitcast(FP4X4),
                 lambda a: w1_s[:, P // 4 * (ROW_TILES * a + i) : P // 4 * (ROW_TILES * a + i + 1)].bitcast(U8),
             )
 
-        def w2_codes(i, a):
-            b, t = divmod(i, PACK)
-            name = "w2_%d%d" % (b, a)
-            if name == "w2_01":
-                name, t = name + "ab"[t // 2], t % 2
-            words, scales = codes[name]
-            return words[:, P * t : P * (t + 1)].bitcast(FP8X4), scales[:, P * t : P * (t + 1)]
-
-        def u_product(i):
-            passes = (0, 1) if i == 0 else (1, 0)
-            u_ps[i] = first_stage_product(
-                "u_%d" % i, (i - 1) % PAIRS, passes, lambda a: w2_codes(i, a)[0], lambda a: w2_codes(i, a)[1]
-            )
+        def out_of_x1(func, i, lo, hi, sums):
+            h = lo // BANK
+            if func == ACT.Sigmoid:
+                if (i, h) not in gate:
+                    gate[i, h] = place([P, BANK], F32, "gate%d%d" % (i, h), (AT_GATE0[i], AT_GATE1 + 4 * i)[h])
+                nc.scalar.activation(gate[i, h][:, lo - BANK * h : hi - BANK * h], sums[:], func)
+            else:
+                if i not in squares:
+                    squares[i] = place([P, S], F32, "squares%d" % i, AT_WINDOW + 4 * (i % WINDOWS))
+                nc.scalar.activation(squares[i][:, lo:hi], sums[:], func)
 
         def from_x1(i):
-            x1_product(i)
-            squares[i] = place([P, S], F32, "squares%d" % i, AT_WINDOW + 4 * (i % WINDOWS))
-            funcs = (ACT.Square, ACT.Sigmoid) if 0 < i < LAST else (ACT.Sigmoid, ACT.Square)
-            steps = [(h, func) for func in funcs for h in range(2)]
-            for h, func in sorted(steps, key=lambda step: step[0]) if i == 0 else steps:
-                if func == ACT.Sigmoid:
-                    kib = (AT_GATE0[i], AT_GATE1 + 4 * (i % RING))[h]
-                    gate[i, h] = place([P, BANK], F32, "gate%d%d" % (i, h), kib)
-                    nc.scalar.activation(gate[i, h][:], x1_ps[i][h][:], func)
-                else:
-                    nc.scalar.activation(squares[i][:, BANK * h : BANK * (h + 1)], x1_ps[i][h][:], func)
+            sums = [x1_product(i, lo, hi, 2 * (i % PAIRS) + h, (1, 0)) for h, (lo, hi) in enumerate(halves)]
+            for func in (ACT.Square, ACT.Sigmoid) if i < LAST else (ACT.Sigmoid, ACT.Square):
+                for h, (lo, hi) in enumerate(halves):
+                    out_of_x1(func, i, lo, hi, sums[h])
 
         def pick_deposit(i):
-            deposit[i] = place([P, M], F32, "deposit%d" % i, deposit_place(i))
-            lo = M // 2 if i == 0 else 0
-            if i == 0:
-                nc.vector.tensor_copy(deposit[i][:, :lo], squares[i][:].indirect(p1[:, : lo // 16]))
-            nc.scalar.activation(deposit[i][:, lo:], squares[i][:].indirect(p1[:, lo // 16 :]), ACT.Copy)
+            deposit[i] = place([P, M], F32, "deposit%d" % i, AT_DEPOSIT + 2 * i)
+            nc.scalar.activation(deposit[i][:], squares[i][:].indirect(p1[:]), ACT.Copy)
 
         def make_x2(i):
             x2[i] = place([P, S], F32, "x2_%d" % i, AT_WINDOW + 4 * (i % WINDOWS if i < LAST else WINDOWS))
             for h in range(2):
                 nc.vector.tensor_tensor(x2[i][:, BANK * h : BANK * (h + 1)], u_ps[i][h][:], gate[i, h][:], ALU.mult)
 
+        withdrawal[0, 0] = keep.tile([P, PACK, M], F32, name="withdrawal0")
+        withdrawal[1, 0] = keep.tile([P, PACK, M // 2], F32, name="withdrawal1")
+
         def pick_withdrawal(i, lo, hi):
             b, t = divmod(i, PACK)
-            if t == 0:
-                withdrawal[b] = work.tile([P, PACK, M], F32, name="withdrawal", bufs=2)
-            nc.scalar.activation(withdrawal[b][:, t, lo:hi], x2[i][:].indirect(p3[:, lo // 16 : hi // 16]), ACT.Copy)
+            nc.scalar.activation(withdrawal[b, lo][:, t, :], x2[i][:].indirect(p3[:, lo // 16 : hi // 16]), ACT.Copy)
 
         def pick_hop(i, lo, hi):
             b, t = divmod(i, PACK)
-            if t == 0:
-                product[b] = work.tile([P, PACK, M], F32, name="product", bufs=2)
+            if b not in product:
+                product[b] = keep.tile([P, PACK, M], F32, name="product%d" % b)
             picked = x2[i][:].indirect(p2[:, lo // 16 : hi // 16])
             nc.vector.tensor_tensor(product[b][:, t, lo:hi], picked, deposit[i][:, lo:hi], ALU.mult)
 
         def larger(name, b, lo, hi, kib):
+            first = max(start for (c, start) in withdrawal if c == b and start <= lo)
             nc.vector.tensor_tensor(
                 stage(name, lo, hi, kib)[:].rearrange("p (c e t) -> p c t e", e=2, t=PACK),
                 product[b][:, :, lo:hi].rearrange("p t (c e) -> p c t e", e=2),
-                withdrawal[b][:, :, lo:hi].rearrange("p t (c e) -> p c t e", e=2),
+                withdrawal[b, first][:, :, lo - first : hi - first].rearrange("p t (c e) -> p c t e", e=2),
                 ALU.max,
             )
 
-        from_x1(0)
+        first_steps = [(0, quarters[0], 0), (0, quarters[1], 4), (1, halves[0], 2), (0, halves[1], 1), (1, halves[1], 3)]
+        for step, (i, (lo, hi), bank) in enumerate(first_steps):
+            sums = x1_product(i, lo, hi, bank, (0, 1) if step < 4 else (1, 0))
+            out_of_x1(ACT.Sigmoid, i, lo, hi, sums)
+            out_of_x1(ACT.Square, i, lo, hi, sums)
+            if (i, hi) == (0, S):
+                pick_deposit(0)
+        pick_deposit(1)
         cast_w2(nc.vector.tensor_copy, "w2_00", 0, 0, 0, PACK, AT_FIRST_CASTS[0])
         quantize("w2_00")
+        load_rows("prior_first", prior[:SPAN, :CHUNK], AT_PRIOR_FIRST)
         load_w2(1, 0)
         load_w2(1, 1)
-        cast_w2(nc.vector.tensor_copy, "w2_01a", 0, 1, 0, 2, AT_FIRST_CASTS[1])
-        cast_w2(nc.vector.tensor_copy, "w2_01b", 0, 1, 2, 3, AT_FIRST_CASTS[2])
+        cast_w2(nc.vector.tensor_copy, "w2_01a", 0, 1, 0, 1, AT_FIRST_CASTS[1])
+        cast_w2(nc.vector.tensor_copy, "w2_01b", 0, 1, 1, 3, AT_FIRST_CASTS[2])
         quantize("w2_01a")
-        pick_deposit(0)
-        cast_w2(gpsimd_cast, "w2_01b", 0, 1, 3, PACK, AT_FIRST_CASTS[1] + 1)
+        cast_w2(nc.vector.tensor_copy, "w2_01c", 0, 1, 3, PACK, AT_FIRST_CASTS[3])
+        quantize("w2_01b")
+        cast_rows(gpsimd_cast, "prior_0", 0, CHUNK, AT_FIRST_CASTS[1], "prior_first")
         load_w3(0)
-        for s in range(4):
-            nc.sync.dma_start(loaded_s[s:P:32, :, : N // 4], scale_rows(w4_scales)[s])
+        load_rows("prior_0", prior[:SPAN, CHUNK:], AT_PRIOR[0])
+        load_rows("prior_1", prior[SPAN:, :], AT_PRIOR[1])
 
-        operands = ("w2_01b", "w2_10", "w2_11", "w3_0", "prior_0", "w3_1", "z_0", "prior_1")
+        quantised = (
+            ("w2_01c",), ("w2_10a",), ("w2_11a", "w2_10b"), ("w2_11b",), ("w3_0",), ("prior_0",), ("z_0",), ("prior_1",),
+        )
         for i in range(ROW_TILES):
             u_product(i)
-            if i < LAST:
+            if 0 < i < LAST:
                 from_x1(i + 1)
                 pick_deposit(i + 1)
             if i > 0:
-                pick_withdrawal(i - 1, 0, M)
+                pick_withdrawal(i - 1, 0, M if i <= PACK else M // 2)
             make_x2(i)
-            quantize(operands[i], AT_GATE0[i])
-            if i == 0:
-                w4_w = place([P, PASSES, N], I32, "w4_w", AT_W4_WORDS)
-                nc.sync.dma_start(
-                    w4_w[:], w4_words.rearrange("a p c i -> a p (c i)").bitcast(I32).rearrange("a p c -> p a c")
-                )
+            kib = AT_GATE0[i]
+            for name in quantised[i]:
+                quantize(name, kib)
+                kib = kib + 1.5
             if i == LAST:
                 break
             pick_hop(i, 0, M)
-            name, kib = operands[i + 1], AT_GATE1 + 4 * (i % RING)
-            quarter_kib = deposit_place(i)
-            if name == "z_0":
-                larger(name, 0, 0, M, kib)
-                cast_rows(gpsimd_cast, operands[LAST], N - P, N, quarter_kib)
-            elif name in ("w2_10", "w2_11"):
-                cast_w2(nc.vector.tensor_copy, name, 1, i, 0, PACK - 1, kib)
-                cast_w2(gpsimd_cast, name, 1, i, PACK - 1, PACK, quarter_kib)
+            kib, share_kib = AT_GATE1 + 4 * i, AT_DEPOSIT + 2 * i
+            if i < PASSES:
+                cast_w2(nc.vector.tensor_copy, "w2_1%da" % i, 1, i, 0, PACK - 1, kib)
+                cast_w2(gpsimd_cast, "w2_1%db" % i, 1, i, PACK - 1, PACK, share_kib)
                 if i == 0:
-                    load_rows("prior_0", prior[:SPAN, :], AT_PRIOR[0])
-                else:
                     load_w3(1)
+                else:
+                    w4_w = place([P, PASSES, N], I32, "w4_w", AT_W4_WORDS)
+                    nc.sync.dma_start(
+                        w4_w[:], w4_words.rearrange("a p c i -> a p (c i)").bitcast(I32).rearrange("a p c -> p a c")
+                    )
+                    w4_s = place([P, PASSES, N // 4], I32, "w4_s", AT_W4_SCALES)
+                    for s in range(4):
+                        nc.sync.dma_start(w4_s[s:P:32, :, :], scale_rows(w4_scales)[s])
+            elif i == 3:
+                cast_rows(nc.vector.tensor_copy, "prior_0", CHUNK, N - SHARE, kib, first=CHUNK)
+                cast_rows(gpsimd_cast, "prior_0", N - SHARE, N, share_kib, first=CHUNK)
+            elif i == 5:
+                larger("z_0", 0, 0, M, kib)
+                cast_rows(gpsimd_cast, "w3_1", N - SHARE, N, share_kib)
+            elif i == 6:
+                cast_rows(nc.vector.tensor_copy, "w3_1", 0, N - 2 * SHARE, kib)
+                cast_rows(gpsimd_cast, "w3_1", N - 2 * SHARE, N - SHARE, share_kib)
             else:
-                hi = N - P if name in staged else N
-                cast_rows(nc.vector.tensor_copy, name, 0, hi - P, kib)
-                cast_rows(gpsimd_cast, name, hi - P, hi, quarter_kib)
-                if name == "w3_0":
-                    load_rows("prior_1", prior[SPAN:, :], AT_PRIOR[1])
+                name = "w3_0" if i == 2 else "prior_1"
+                cast_rows(nc.vector.tensor_copy, name, 0, N - SHARE, kib)
+                cast_rows(gpsimd_cast, name, N - SHARE, N, share_kib)
 
+        pick_withdrawal(LAST, 0, M // 2)
+        withdrawal[1, M // 2] = place([P, PACK, M // 2], F32, "withdrawal_late", AT_LATE_WITHDRAWAL)
+        for i in range(PACK, ROW_TILES):
+            pick_withdrawal(i, M // 2, M)
         for lo in range(0, M, M // 2):
-            pick_withdrawal(LAST, lo, lo + M // 2)
             pick_hop(LAST, lo, lo + M // 2)
+        quantize("w3_1", AT_DEPOSIT + 2 * LAST)
 
         def y_pass(bank, n0, weights, moving, start, stop):
             nc.tensor.matmul_mx(
@@ -340,10 +367,10 @@ def tile_list_layering_chain_features_kernel(
             )
 
         def columns(name, lo):
-            return [plane[:, lo : lo + CHUNK] for plane in codes[name]]
+            return [plane[:, lo : lo + CHUNK] for plane in codes[name][:2]]
 
         for b in range(PASSES):
-            codes["w4_%d" % b] = (w4_w[:, b, :], loaded_s[:, b, : N // 4].bitcast(U8))
+            codes["w4_%d" % b] = (w4_w[:, b, :], w4_s[:, b, :].bitcast(U8), 0)
         chunks = range(0, M, CHUNK)
         pieces = [(lo, 0, N) for lo in chunks[:-1]] + [(M - CHUNK, 0, N // 2), (M - CHUNK, N // 2, N)]
         y_ps = {}
@@ -367,7 +394,7 @@ def tile_list_layering_chain_features_kernel(
                     nc.sync.dma_start(out[n_lo:n_hi, lo : lo + CHUNK].rearrange("(j p) m -> p j m", p=P), result[:])
 
         for lo in chunks:
-            larger("z_1_%d" % lo, 1, lo, lo + CHUNK, AT_GATE1 + 4 * (LAST % RING) + lo // CHUNK)
+            larger("z_1_%d" % lo, 1, lo, lo + CHUNK, AT_LAST_Z + lo // CHUNK)
             if lo > 0:
                 finish(lo - CHUNK)
         finish(M - CHUNK)

@@ -26,7 +26,6 @@ LAST = ROW_TILES - 1
 CHUNK = 128
 PAIRS = 4
 Y_BANKS = (0, 1, 2, 3, 6)
-WINDOWS = 4
 
 AT_TABLE = (7, 33)
 AT_TABLE_SCALES = 30
@@ -39,10 +38,11 @@ AT_PRIOR = (22, 28)
 AT_W4_WORDS, AT_W4_SCALES = 48, 52
 AT_GATE0 = (14, 16, 18, 20, 56, 58, 60, 62)
 AT_GATE1 = 64
-AT_LATE_WITHDRAWAL = 89
-AT_LAST_Z = 93
-AT_WINDOW = 98
-AT_DEPOSIT = 118
+AT_LATE_WITHDRAWAL = (91, 93)
+AT_LAST_Z = 138
+AT_SQUARES = 98
+AT_X2 = 106
+AT_DEPOSIT = 122
 SHARE = 192
 WIDTHS = (512, 384, 256, 128, 64)
 
@@ -73,6 +73,10 @@ def tile_list_layering_chain_features_kernel(
         loaded_s = keep.tile([P, PASSES, H // 4], I32, name="loaded_s", align_bytes=64)
         nc.gpsimd.memset(loaded_s[:], 0)
         v_s = keep.tile([P, PASSES, S], U8, name="v_s", align_bytes=64)
+
+        warm = keep.tile([P, 2], F32, name="warm")
+        nc.vector.memset(warm[:, 0:1], 0.0)
+        nc.scalar.activation(warm[:, 1:2], warm[:, 0:1], ACT.Silu)
 
         idx = lists.tile([P, S // 16], U16, name="idx")
         p1 = lists.tile([P, M // 16], U16, name="p1")
@@ -231,36 +235,38 @@ def tile_list_layering_chain_features_kernel(
 
         def out_of_x1(func, i, lo, hi, sums):
             h = lo // BANK
-            if func == ACT.Sigmoid:
+            if func == ACT.Tanh:
                 if (i, h) not in gate:
                     gate[i, h] = place([P, BANK], F32, "gate%d%d" % (i, h), (AT_GATE0[i], AT_GATE1 + 4 * i)[h])
-                nc.scalar.activation(gate[i, h][:, lo - BANK * h : hi - BANK * h], sums[:], func)
+                nc.scalar.activation(gate[i, h][:, lo - BANK * h : hi - BANK * h], sums[:], func, scale=0.5)
             else:
                 if i not in squares:
-                    squares[i] = place([P, S], F32, "squares%d" % i, AT_WINDOW + 4 * (i % WINDOWS))
+                    squares[i] = place([P, S], F32, "squares%d" % i, AT_SQUARES + 4 * (i % 2))
                 nc.scalar.activation(squares[i][:, lo:hi], sums[:], func)
 
         def from_x1(i):
             sums = [x1_product(i, lo, hi, 2 * (i % PAIRS) + h, (1, 0)) for h, (lo, hi) in enumerate(halves)]
-            for func in (ACT.Square, ACT.Sigmoid) if i < LAST else (ACT.Sigmoid, ACT.Square):
+            for func in (ACT.Tanh, ACT.Square):
                 for h, (lo, hi) in enumerate(halves):
                     out_of_x1(func, i, lo, hi, sums[h])
 
         def pick_deposit(i):
             deposit[i] = place([P, M], F32, "deposit%d" % i, AT_DEPOSIT + 2 * i)
-            nc.scalar.activation(deposit[i][:], squares[i][:].indirect(p1[:]), ACT.Copy)
+            nc.scalar.activation(deposit[i][:], squares[i][:].indirect(p1[:]), ACT.Copy, scale=0.5)
 
         def make_x2(i):
-            x2[i] = place([P, S], F32, "x2_%d" % i, AT_WINDOW + 4 * (i % WINDOWS if i < LAST else WINDOWS))
+            x2[i] = place([P, S], F32, "x2_%d" % i, AT_X2 + 4 * (i % PACK))
             for h in range(2):
-                nc.vector.tensor_tensor(x2[i][:, BANK * h : BANK * (h + 1)], u_ps[i][h][:], gate[i, h][:], ALU.mult)
+                nc.vector.scalar_tensor_tensor(
+                    x2[i][:, BANK * h : BANK * (h + 1)], gate[i, h][:], 1.0, u_ps[i][h][:], ALU.add, ALU.mult
+                )
 
         withdrawal[0, 0] = keep.tile([P, PACK, M], F32, name="withdrawal0")
         withdrawal[1, 0] = keep.tile([P, PACK, M // 2], F32, name="withdrawal1")
 
         def pick_withdrawal(i, lo, hi):
             b, t = divmod(i, PACK)
-            nc.scalar.activation(withdrawal[b, lo][:, t, :], x2[i][:].indirect(p3[:, lo // 16 : hi // 16]), ACT.Copy)
+            nc.scalar.activation(withdrawal[b, lo][:, t, :], x2[i][:].indirect(p3[:, lo // 16 : hi // 16]), ACT.Copy, scale=0.5)
 
         def pick_hop(i, lo, hi):
             b, t = divmod(i, PACK)
@@ -281,7 +287,7 @@ def tile_list_layering_chain_features_kernel(
         first_steps = [(0, quarters[0], 0), (0, quarters[1], 4), (1, halves[0], 2), (0, halves[1], 1), (1, halves[1], 3)]
         for step, (i, (lo, hi), bank) in enumerate(first_steps):
             sums = x1_product(i, lo, hi, bank, (0, 1) if step < 4 else (1, 0))
-            out_of_x1(ACT.Sigmoid, i, lo, hi, sums)
+            out_of_x1(ACT.Tanh, i, lo, hi, sums)
             out_of_x1(ACT.Square, i, lo, hi, sums)
             if (i, hi) == (0, S):
                 pick_deposit(0)
@@ -348,12 +354,12 @@ def tile_list_layering_chain_features_kernel(
                 cast_rows(gpsimd_cast, name, N - SHARE, N, share_kib)
 
         pick_withdrawal(LAST, 0, M // 2)
-        withdrawal[1, M // 2] = place([P, PACK, M // 2], F32, "withdrawal_late", AT_LATE_WITHDRAWAL)
-        for i in range(PACK, ROW_TILES):
-            pick_withdrawal(i, M // 2, M)
+        for lo, kib in zip(range(M // 2, M, CHUNK), AT_LATE_WITHDRAWAL):
+            withdrawal[1, lo] = place([P, PACK, CHUNK], F32, "withdrawal_%d" % lo, kib)
+            for i in range(PACK, ROW_TILES):
+                pick_withdrawal(i, lo, lo + CHUNK)
         for lo in range(0, M, M // 2):
             pick_hop(LAST, lo, lo + M // 2)
-        quantize("w3_1", AT_DEPOSIT + 2 * LAST)
 
         def y_pass(bank, n0, weights, moving, start, stop):
             nc.tensor.matmul_mx(
@@ -395,6 +401,8 @@ def tile_list_layering_chain_features_kernel(
 
         for lo in chunks:
             larger("z_1_%d" % lo, 1, lo, lo + CHUNK, AT_LAST_Z + lo // CHUNK)
+            if lo == CHUNK:
+                quantize("w3_1", AT_DEPOSIT + 2 * LAST)
             if lo > 0:
                 finish(lo - CHUNK)
         finish(M - CHUNK)

@@ -27,9 +27,9 @@ CHUNK = 128
 PAIRS = 4
 Y_BANKS = (0, 1, 2, 3, 6)
 
-AT_TABLE = (7, 33)
-AT_TABLE_SCALES = 30
-AT_W1_SCALES, AT_W1_WORDS = 8, 10
+AT_TABLE = (8, 33)
+AT_W1_SCALES = 8
+AT_W1_LATE = (10, 63)
 AT_FIRST_CASTS = (30, 37, 34, 36)
 AT_W2 = ((0, 22), (40, 48))
 AT_W3 = (0, 40)
@@ -67,12 +67,11 @@ def tile_list_layering_chain_features_kernel(
         def scale_rows(scales):
             return scales.bitcast(I32).rearrange("a (q s) n -> s q a n", s=4)
 
-        tab_s = place([P, T], U8, "tab_s", AT_TABLE_SCALES)
-        nc.vector.memset(tab_s[:, : T // 2].bitcast(I32), 0)
-        nc.gpsimd.memset(tab_s[:, T // 2 :].bitcast(I32), 0)
+        tab_s = place([P, PASSES * T], U8, "tab_s", AT_W2[0][0])
         loaded_s = keep.tile([P, PASSES, H // 4], I32, name="loaded_s", align_bytes=64)
-        nc.gpsimd.memset(loaded_s[:], 0)
-        v_s = keep.tile([P, PASSES, S], U8, name="v_s", align_bytes=64)
+        nc.vector.memset(tab_s[:, :T].bitcast(I32), 0)
+        nc.gpsimd.memset(tab_s[:, T:].bitcast(I32), 0)
+        nc.vector.memset(loaded_s[:], 0)
 
         warm = keep.tile([P, 2], F32, name="warm")
         nc.vector.memset(warm[:, 0:1], 0.0)
@@ -90,25 +89,42 @@ def tile_list_layering_chain_features_kernel(
 
         nc.sync.dma_start(idx[:], offs)
         load_table_words(0, 0, T // 4)
-        nc.sync.dma_start(tab_s[0:P:4, :].bitcast(I32), tab_scales.bitcast(I32).rearrange("a m n -> (a m) n"))
-        w1_raw = keep.tile([P, PASSES, H // 2], I32, name="w1_raw")
-        nc.sync.dma_start(w1_raw[:], w1_words.bitcast(I32).rearrange("a p c -> p a c"))
+        nc.sync.dma_start(
+            tab_s[4:P:8, :].bitcast(I32).rearrange("m (a n) -> m a n", a=PASSES),
+            tab_scales.bitcast(I32).rearrange("a m n -> m a n"),
+        )
+        w1_raw, w1_w = {}, {}
+
+        def load_w1(b, tile):
+            w1_raw[b] = tile
+            words = w1_words.bitcast(I32).rearrange("a p c -> p a c")
+            nc.sync.dma_start(tile[:], words[:, :, SPAN // 2 * b : SPAN // 2 * (b + 1)])
+
+        load_w1(0, keep.tile([P, PASSES, SPAN // 2], I32, name="w1_raw0"))
+        load_table_words(0, T // 4, T)
         nc.sync.dma_start(p1[:], pos1)
         nc.sync.dma_start(p2[:], pos2)
-        nc.sync.dma_start(p3[:], pos3)
-        load_table_words(0, T // 4, T)
-        for s in range(4):
-            nc.sync.dma_start(loaded_s[s:P:32, :, :], scale_rows(w1_scales)[s])
-
-        picked_s = keep.tile([P, S], U8, name="picked_s")
-        nc.vector.tensor_copy(picked_s[:], tab_s[:].indirect(idx[:]))
-        for a in range(PASSES):
-            for s in range(4):
-                rows = picked_s[64 * a + 4 * s : 64 * (a + 1) : 16, :]
-                nc.sync.dma_start(v_s[s:P:32, a, :].bitcast(I32), rows.bitcast(I32))
-                if (a, s) == (0, 1):
-                    load_table_words(1, 0, T // 2)
+        load_table_words(1, 0, T // 2)
         load_table_words(1, T // 2, T)
+        nc.sync.dma_start(p3[:], pos3)
+        for s in range(4):
+            nc.gpsimd.dma_start(loaded_s[s:P:32, :, :], scale_rows(w1_scales)[s])
+        v_s = keep.tile([P, PASSES, S], U8, name="v_s", align_bytes=64)
+
+        picked_s = keep.tile([P, PASSES, S], U8, name="picked_s")
+        for a in range(PASSES):
+            nc.vector.tensor_copy(picked_s[:, a, :], tab_s[:, T * a : T * (a + 1)].indirect(idx[:]))
+        for s in range(4):
+            nc.sync.dma_start(v_s[s:P:32, :, :].bitcast(I32), picked_s[8 * s + 4 : P : 32, :, :].bitcast(I32))
+
+        def order_w1(b, tile):
+            w1_w[b] = tile
+            nc.vector.tensor_copy(
+                tile[:].rearrange("p (a t c w) -> p a t c w", a=PASSES, t=PACK, w=2),
+                w1_raw[b][:].rearrange("p a (c t w) -> p a t c w", t=PACK, w=2),
+            )
+
+        order_w1(0, keep.tile([P, SPAN], I32, name="w1_w0", align_bytes=64))
         v_w = {}
 
         def pick_words(a, cuts):
@@ -124,11 +140,6 @@ def tile_list_layering_chain_features_kernel(
         nc.vector.tensor_copy(
             w1_s[:].rearrange("p (f t c) -> p f t c", f=4, t=PACK),
             loaded_s[:].rearrange("p a (b c t) -> p (a b) t c", b=PASSES, t=PACK),
-        )
-        w1_w = place([P, PASSES * H // 2], I32, "w1_w", AT_W1_WORDS)
-        nc.vector.tensor_copy(
-            w1_w[:].rearrange("p (f t c w) -> p f t c w", f=4, t=PACK, w=2),
-            w1_raw[:].rearrange("p a (b c t w) -> p (a b) t c w", b=PASSES, t=PACK, w=2),
         )
 
         raw = {}
@@ -229,7 +240,7 @@ def tile_list_layering_chain_features_kernel(
         def x1_product(i, lo, hi, bank, passes):
             return first_stage_product(
                 "x1_%d_%d" % (i, lo), bank, lo, hi, passes,
-                lambda a: w1_w[:, P // 2 * (ROW_TILES * a + i) : P // 2 * (ROW_TILES * a + i + 1)].bitcast(FP4X4),
+                lambda a: w1_w[i // PACK][:, P // 2 * (PACK * a + i % PACK) : P // 2 * (PACK * a + i % PACK + 1)].bitcast(FP4X4),
                 lambda a: w1_s[:, P // 4 * (ROW_TILES * a + i) : P // 4 * (ROW_TILES * a + i + 1)].bitcast(U8),
             )
 
@@ -295,6 +306,7 @@ def tile_list_layering_chain_features_kernel(
         cast_w2(nc.vector.tensor_copy, "w2_00", 0, 0, 0, PACK, AT_FIRST_CASTS[0])
         quantize("w2_00")
         load_rows("prior_first", prior[:SPAN, :CHUNK], AT_PRIOR_FIRST)
+        load_w1(1, place([P, PASSES, SPAN // 2], I32, "w1_raw1", AT_W1_LATE[0]))
         load_w2(1, 0)
         load_w2(1, 1)
         cast_w2(nc.vector.tensor_copy, "w2_01a", 0, 1, 0, 1, AT_FIRST_CASTS[1])
@@ -322,12 +334,14 @@ def tile_list_layering_chain_features_kernel(
             for name in quantised[i]:
                 quantize(name, kib)
                 kib = kib + 1.5
+            if i == 0:
+                order_w1(1, place([P, SPAN], I32, "w1_w1", AT_W1_LATE[1]))
             if i == LAST:
                 break
             pick_hop(i, 0, M)
             kib, share_kib = AT_GATE1 + 4 * i, AT_DEPOSIT + 2 * i
             if i < PASSES:
-                cast_w2(nc.vector.tensor_copy, "w2_1%da" % i, 1, i, 0, PACK - 1, kib)
+                cast_w2(nc.vector.tensor_copy, "w2_1%da" % i, 1, i, 0, PACK - 1, kib + 1)
                 cast_w2(gpsimd_cast, "w2_1%db" % i, 1, i, PACK - 1, PACK, share_kib)
                 if i == 0:
                     load_w3(1)

@@ -27,24 +27,24 @@ CHUNK = 128
 PAIRS = 4
 Y_BANKS = (0, 1, 2, 3, 6)
 
-AT_TABLE = (8, 33)
+AT_TABLE = (8, 31)
 AT_W1_SCALES = 8
-AT_W1_LATE = (10, 63)
-AT_FIRST_CASTS = (30, 37, 34, 36)
-AT_W2 = ((0, 22), (40, 48))
-AT_W3 = (0, 40)
-AT_PRIOR_FIRST = 38
-AT_PRIOR = (22, 28)
-AT_W4_WORDS, AT_W4_SCALES = 48, 52
-AT_GATE0 = (14, 16, 18, 20, 56, 58, 60, 62)
-AT_GATE1 = 64
-AT_LATE_WITHDRAWAL = (91, 93)
-AT_LAST_Z = 138
-AT_SQUARES = 98
-AT_X2 = 106
-AT_DEPOSIT = 122
+AT_W2 = ((0, 16), (24, 46))
+AT_PRIOR_0 = (32, 35)
+AT_W1_LATE = 40
+AT_FIRST_CAST = 42
+AT_PRIOR_1 = 0
+AT_W3 = (16, 24)
+AT_W4_WORDS, AT_W4_SCALES = 46, 50
+AT_SECOND_CASTS = (54, 55)
+AT_GATE = {
+    (0, 0): 57, (1, 0): 59, (2, 0): 62, (3, 0): 65, (5, 0): 67, (6, 0): 69, (7, 0): 71,
+    (0, 1): 73, (1, 1): 77, (4, 1): 81, (5, 1): 83, (7, 1): 88,
+}
+AT_SQUARES = 91
+AT_X2 = 99
+AT_LAST_Z = 115
 SHARE = 192
-WIDTHS = (512, 384, 256, 128, 64)
 
 
 def tile_list_layering_chain_features_kernel(
@@ -161,57 +161,67 @@ def tile_list_layering_chain_features_kernel(
         load_w2(0, 0)
         load_w2(0, 1)
         pick_words(1, quarters + halves[1:])
-
-        staged, codes = {}, {}
+        load_w2(1, 0)
+        load_rows("prior_0a", prior[:SPAN, :SHARE], AT_PRIOR_0[0])
+        load_w2(1, 1)
+        load_rows("prior_0b", prior[:SPAN, SHARE:], AT_PRIOR_0[1])
+        load_w1(1, place([P, PASSES, SPAN // 2], I32, "w1_raw1", AT_W1_LATE))
 
         def gpsimd_cast(out, in_):
             nc.gpsimd.tensor_scalar(out, in_, 1.0, 0.0, ALU.mult, ALU.add)
 
-        def stage(name, lo, hi, kib):
-            piece = place([P, (hi - lo) * PACK], BF16, "%s_bf%d" % (name, lo), kib)
-            staged.setdefault(name, {})[lo, hi] = piece
-            return piece
-
-        def cast_w2(copy, name, b, a, t0, t1, kib):
-            piece = stage(name, t0 * P, t1 * P, kib)[:].rearrange("p (t c e i) -> p c t i e", e=4, i=PACK, t=t1 - t0)
+        def cast_w2(copy, b, a, t0, t1, kib):
+            staged = place([P, (t1 - t0) * P * PACK], BF16, "w2_%d%d%d_bf" % (b, a, t0), kib)
+            piece = staged[:].rearrange("p (t c e i) -> p c t i e", e=4, i=PACK, t=t1 - t0)
             rows = raw["w2_%d%d" % (b, a)][:].rearrange("p i (c t e) -> p c t i e", t=PACK, e=4)[:, :, t0:t1]
             if t1 - t0 == 1:
                 piece, rows = piece[:, :, 0], rows[:, :, 0]
             copy(piece, rows)
+            return staged[:]
 
-        def cast_rows(copy, name, lo, hi, kib, source=None, first=0):
+        def cast_columns(copy, staged, lo, hi, rows):
             copy(
-                stage(name, lo, hi, kib)[:].rearrange("p (c e t) -> p c t e", e=4, t=PACK),
-                raw[source or name][:, :, lo - first : hi - first].rearrange("p t (c e) -> p c t e", e=4),
+                staged[:, PACK * lo : PACK * hi].rearrange("p (c e t) -> p c t e", e=4, t=PACK),
+                rows.rearrange("p t (c e) -> p c t e", e=4),
             )
 
-        def quantize(name, kib=None):
-            first = min(lo for lo, hi in staged[name])
-            columns = max(hi for lo, hi in staged[name]) - first
+        def quantize(name, staged, kib=None):
+            columns = staged.shape[1] // PACK
             if kib is None:
                 words = keep.tile([P, columns], U32, name=name + "_w", align_bytes=64)
             else:
                 words = place([P, columns], U32, name + "_w", kib)
             scales = keep.tile([P, columns], U8, name=name + "_s", align_bytes=64)
-            for lo, hi in sorted(staged[name]):
-                done = 0
-                while done < hi - lo:
-                    width = max(w for w in WIDTHS if w <= hi - lo - done)
-                    cols = slice(lo - first + done, lo - first + done + width)
-                    part = staged[name][lo, hi][:, PACK * done : PACK * (done + width)]
-                    nc.vector.quantize_mx(out=words[:, cols].bitcast(FP8X4), scales=scales[:, cols], in_=part)
-                    done = done + width
-            codes[name] = (words, scales, first)
+            nc.vector.quantize_mx(out=words[:].bitcast(FP8X4), scales=scales[:], in_=staged)
+            return words, scales
 
-        u_ps, gate, squares, x2, deposit, product, withdrawal = {}, {}, {}, {}, {}, {}, {}
+        codes = {}
 
-        def first_stage_product(name, bank, lo, hi, passes, words, scales):
+        def file_codes(name, first, planes):
+            words, scales = planes
+            for j in range(scales[:].shape[1] // P):
+                codes[name, first + j] = (words[:, P * j : P * (j + 1)].bitcast(FP8X4), scales[:, P * j : P * (j + 1)])
+
+        gate, deposit_at, staged = {}, {}, {}
+        for name, first, held_by in (("prior_0", 0, (2, 1)), ("prior_1", 2, (4, 0)), ("w3_0", 4, (6, 1))):
+            tile = keep.tile([P, 3 * M], F32, name=name + "_stage", align_bytes=64)
+            deposit_at[first], deposit_at[first + 1], gate[held_by] = tile[:, :M], tile[:, M : 2 * M], tile[:, 2 * M :]
+            start = M - 2 * SHARE
+            staged[name] = tile[:, start : start + 2 * N].bitcast(BF16)
+        tile = keep.tile([P, 2 * (N - SHARE) + M], F32, name="w3_1_stage", align_bytes=64)
+        gate[3, 1], deposit_at[6], staged["w3_1"] = tile[:, :BANK], tile[:, 2 * (N - SHARE) :], tile[:, : 2 * N].bitcast(BF16)
+        deposit_at[LAST] = keep.tile([P, M], F32, name="last_deposit")[:]
+
+        u_ps, squares, x2, product, withdrawal = {}, {}, {}, {}, {}
+
+        def first_stage_product(name, bank, lo, hi, passes, stationary):
             sums = bank_tile([P, hi - lo], name, bank)
             for a in passes:
+                words, scales = stationary(a)
                 nc.tensor.matmul_mx(
                     out=sums[:],
-                    lhsT=words(a),
-                    lhsT_scale=scales(a),
+                    lhsT=words,
+                    lhsT_scale=scales,
                     rhs=v_w[a][:, lo:hi].bitcast(FP8X4),
                     rhs_scale=v_s[:, a, lo:hi],
                     start=(a == passes[0]),
@@ -219,36 +229,30 @@ def tile_list_layering_chain_features_kernel(
                 )
             return sums
 
-        def w2_codes(i, a):
-            b, t = divmod(i, PACK)
-            for name in codes:
-                words, scales, first = codes[name]
-                if name.startswith("w2_%d%d" % (b, a)) and first <= P * t < first + scales[:].shape[1]:
-                    cols = slice(P * t - first, P * (t + 1) - first)
-                    return words[:, cols].bitcast(FP8X4), scales[:, cols]
-
         def u_product(i):
+            b, t = divmod(i, PACK)
             passes = (0, 1) if i == 0 else (1, 0)
             u_ps[i] = [
                 first_stage_product(
-                    "u_%d_%d" % (i, h), 2 * ((i - 1) % PAIRS) + h, lo, hi, passes,
-                    lambda a: w2_codes(i, a)[0], lambda a: w2_codes(i, a)[1],
+                    "u_%d_%d" % (i, h), 2 * ((i - 1) % PAIRS) + h, lo, hi, passes, lambda a: codes["w2_%d%d" % (b, a), t]
                 )
                 for h, (lo, hi) in enumerate(halves)
             ]
 
+        def w1_codes(i, a):
+            at = PACK * a + i % PACK
+            words = w1_w[i // PACK][:, P // 2 * at : P // 2 * (at + 1)].bitcast(FP4X4)
+            at = ROW_TILES * a + i
+            return words, w1_s[:, P // 4 * at : P // 4 * (at + 1)].bitcast(U8)
+
         def x1_product(i, lo, hi, bank, passes):
-            return first_stage_product(
-                "x1_%d_%d" % (i, lo), bank, lo, hi, passes,
-                lambda a: w1_w[i // PACK][:, P // 2 * (PACK * a + i % PACK) : P // 2 * (PACK * a + i % PACK + 1)].bitcast(FP4X4),
-                lambda a: w1_s[:, P // 4 * (ROW_TILES * a + i) : P // 4 * (ROW_TILES * a + i + 1)].bitcast(U8),
-            )
+            return first_stage_product("x1_%d_%d" % (i, lo), bank, lo, hi, passes, lambda a: w1_codes(i, a))
 
         def out_of_x1(func, i, lo, hi, sums):
             h = lo // BANK
             if func == ACT.Tanh:
                 if (i, h) not in gate:
-                    gate[i, h] = place([P, BANK], F32, "gate%d%d" % (i, h), (AT_GATE0[i], AT_GATE1 + 4 * i)[h])
+                    gate[i, h] = place([P, BANK], F32, "gate%d%d" % (i, h), AT_GATE[i, h])[:]
                 nc.scalar.activation(gate[i, h][:, lo - BANK * h : hi - BANK * h], sums[:], func, scale=0.5)
             else:
                 if i not in squares:
@@ -262,14 +266,13 @@ def tile_list_layering_chain_features_kernel(
                     out_of_x1(func, i, lo, hi, sums[h])
 
         def pick_deposit(i):
-            deposit[i] = place([P, M], F32, "deposit%d" % i, AT_DEPOSIT + 2 * i)
-            nc.scalar.activation(deposit[i][:], squares[i][:].indirect(p1[:]), ACT.Copy, scale=0.5)
+            nc.scalar.activation(deposit_at[i], squares[i][:].indirect(p1[:]), ACT.Copy, scale=0.5)
 
         def make_x2(i):
             x2[i] = place([P, S], F32, "x2_%d" % i, AT_X2 + 4 * (i % PACK))
             for h in range(2):
                 nc.vector.scalar_tensor_tensor(
-                    x2[i][:, BANK * h : BANK * (h + 1)], gate[i, h][:], 1.0, u_ps[i][h][:], ALU.add, ALU.mult
+                    x2[i][:, BANK * h : BANK * (h + 1)], gate[i, h], 1.0, u_ps[i][h][:], ALU.add, ALU.mult
                 )
 
         withdrawal[0, 0] = keep.tile([P, PACK, M], F32, name="withdrawal0")
@@ -284,16 +287,18 @@ def tile_list_layering_chain_features_kernel(
             if b not in product:
                 product[b] = keep.tile([P, PACK, M], F32, name="product%d" % b)
             picked = x2[i][:].indirect(p2[:, lo // 16 : hi // 16])
-            nc.vector.tensor_tensor(product[b][:, t, lo:hi], picked, deposit[i][:, lo:hi], ALU.mult)
+            nc.vector.tensor_tensor(product[b][:, t, lo:hi], picked, deposit_at[i][:, lo:hi], ALU.mult)
 
-        def larger(name, b, lo, hi, kib):
+        def larger(b, lo, hi, kib):
             first = max(start for (c, start) in withdrawal if c == b and start <= lo)
+            z = place([P, (hi - lo) * PACK], BF16, "z_%d_%d" % (b, lo), kib)
             nc.vector.tensor_tensor(
-                stage(name, lo, hi, kib)[:].rearrange("p (c e t) -> p c t e", e=2, t=PACK),
+                z[:].rearrange("p (c e t) -> p c t e", e=2, t=PACK),
                 product[b][:, :, lo:hi].rearrange("p t (c e) -> p c t e", e=2),
                 withdrawal[b, first][:, :, lo - first : hi - first].rearrange("p t (c e) -> p c t e", e=2),
                 ALU.max,
             )
+            return z[:]
 
         first_steps = [(0, quarters[0], 0), (0, quarters[1], 4), (1, halves[0], 2), (0, halves[1], 1), (1, halves[1], 3)]
         for step, (i, (lo, hi), bank) in enumerate(first_steps):
@@ -303,25 +308,15 @@ def tile_list_layering_chain_features_kernel(
             if (i, hi) == (0, S):
                 pick_deposit(0)
         pick_deposit(1)
-        cast_w2(nc.vector.tensor_copy, "w2_00", 0, 0, 0, PACK, AT_FIRST_CASTS[0])
-        quantize("w2_00")
-        load_rows("prior_first", prior[:SPAN, :CHUNK], AT_PRIOR_FIRST)
-        load_w1(1, place([P, PASSES, SPAN // 2], I32, "w1_raw1", AT_W1_LATE[0]))
-        load_w2(1, 0)
-        load_w2(1, 1)
-        cast_w2(nc.vector.tensor_copy, "w2_01a", 0, 1, 0, 1, AT_FIRST_CASTS[1])
-        cast_w2(nc.vector.tensor_copy, "w2_01b", 0, 1, 1, 3, AT_FIRST_CASTS[2])
-        quantize("w2_01a")
-        cast_w2(nc.vector.tensor_copy, "w2_01c", 0, 1, 3, PACK, AT_FIRST_CASTS[3])
-        quantize("w2_01b")
-        cast_rows(gpsimd_cast, "prior_0", 0, CHUNK, AT_FIRST_CASTS[1], "prior_first")
-        load_w3(0)
-        load_rows("prior_0", prior[:SPAN, CHUNK:], AT_PRIOR[0])
-        load_rows("prior_1", prior[SPAN:, :], AT_PRIOR[1])
+        file_codes("w2_00", 0, quantize("w2_00", cast_w2(nc.vector.tensor_copy, 0, 0, 0, PACK, AT_FIRST_CAST)))
+        load_rows("prior_1", prior[SPAN:, :], AT_PRIOR_1)
+        tile_0 = cast_w2(nc.vector.tensor_copy, 0, 1, 0, 1, AT_SECOND_CASTS[0])
+        tiles_1_2 = cast_w2(nc.vector.tensor_copy, 0, 1, 1, 3, AT_SECOND_CASTS[1])
+        file_codes("w2_01", 0, quantize("w2_01_0", tile_0))
+        tile_3 = cast_w2(gpsimd_cast, 0, 1, 3, PACK, AT_SECOND_CASTS[0])
+        file_codes("w2_01", 1, quantize("w2_01_1", tiles_1_2))
 
-        quantised = (
-            ("w2_01c",), ("w2_10a",), ("w2_11a", "w2_10b"), ("w2_11b",), ("w3_0",), ("prior_0",), ("z_0",), ("prior_1",),
-        )
+        vector_cast = nc.vector.tensor_copy
         for i in range(ROW_TILES):
             u_product(i)
             if 0 < i < LAST:
@@ -330,93 +325,100 @@ def tile_list_layering_chain_features_kernel(
             if i > 0:
                 pick_withdrawal(i - 1, 0, M if i <= PACK else M // 2)
             make_x2(i)
-            kib = AT_GATE0[i]
-            for name in quantised[i]:
-                quantize(name, kib)
-                kib = kib + 1.5
             if i == 0:
-                order_w1(1, place([P, SPAN], I32, "w1_w1", AT_W1_LATE[1]))
-            if i == LAST:
+                file_codes("w2_01", 3, quantize("w2_01_3", tile_3, AT_GATE[0, 0]))
+            elif i == 1:
+                file_codes("w2_10", 0, quantize("w2_10", staged["w2_10"], AT_GATE[1, 0]))
+            elif i == 2:
+                file_codes("w2_11", 0, quantize("w2_11", staged["w2_11"], AT_GATE[2, 0] - 1))
+                order_w1(1, place([P, SPAN], I32, "w1_w1", AT_GATE[2, 0] + 1))
+            elif i == 3:
+                file_codes("prior_0", 0, quantize("prior_0", staged["prior_0"], AT_GATE[3, 0]))
+            elif i == 4:
+                cast_columns(vector_cast, staged["prior_1"], 2 * SHARE, M, raw["prior_1"][:, :, 2 * SHARE :])
+            elif i == 5:
+                file_codes("prior_1", 2, quantize("prior_1b", staged["prior_1"][:, 2 * M :], AT_GATE[5, 0]))
+            elif i == 6:
+                file_codes("z_0", 0, quantize("z_0", staged["z_0"], AT_GATE[6, 0]))
+            else:
+                file_codes("w3_0", 0, quantize("w3_0", staged["w3_0"], AT_GATE[7, 0]))
                 break
             pick_hop(i, 0, M)
-            kib, share_kib = AT_GATE1 + 4 * i, AT_DEPOSIT + 2 * i
-            if i < PASSES:
-                cast_w2(nc.vector.tensor_copy, "w2_1%da" % i, 1, i, 0, PACK - 1, kib + 1)
-                cast_w2(gpsimd_cast, "w2_1%db" % i, 1, i, PACK - 1, PACK, share_kib)
-                if i == 0:
-                    load_w3(1)
-                else:
-                    w4_w = place([P, PASSES, N], I32, "w4_w", AT_W4_WORDS)
-                    nc.sync.dma_start(
-                        w4_w[:], w4_words.rearrange("a p c i -> a p (c i)").bitcast(I32).rearrange("a p c -> p a c")
-                    )
-                    w4_s = place([P, PASSES, N // 4], I32, "w4_s", AT_W4_SCALES)
-                    for s in range(4):
-                        nc.sync.dma_start(w4_s[s:P:32, :, :], scale_rows(w4_scales)[s])
+            if i == 0:
+                staged["w2_10"] = cast_w2(vector_cast, 1, 0, 0, PACK, AT_GATE[0, 1])
+                cast_columns(gpsimd_cast, staged["prior_0"], 0, SHARE, raw["prior_0a"][:])
+                load_w3(1)
+                load_w3(0)
+            elif i == 1:
+                staged["w2_11"] = cast_w2(vector_cast, 1, 1, 0, PACK, AT_GATE[1, 1])
+                cast_columns(gpsimd_cast, staged["prior_0"], SHARE, 2 * SHARE, raw["prior_0b"][:, :, :SHARE])
+                w4_w = place([P, PASSES, N], I32, "w4_w", AT_W4_WORDS)
+                nc.sync.dma_start(
+                    w4_w[:], w4_words.rearrange("a p c i -> a p (c i)").bitcast(I32).rearrange("a p c -> p a c")
+                )
+                w4_s = place([P, PASSES, N // 4], I32, "w4_s", AT_W4_SCALES)
+                for s in range(4):
+                    nc.sync.dma_start(w4_s[s:P:32, :, :], scale_rows(w4_scales)[s])
+            elif i == 2:
+                cast_columns(vector_cast, staged["prior_0"], 2 * SHARE, M, raw["prior_0b"][:, :, SHARE:])
+                cast_columns(gpsimd_cast, staged["prior_1"], 0, SHARE, raw["prior_1"][:, :, :SHARE])
             elif i == 3:
-                cast_rows(nc.vector.tensor_copy, "prior_0", CHUNK, N - SHARE, kib, first=CHUNK)
-                cast_rows(gpsimd_cast, "prior_0", N - SHARE, N, share_kib, first=CHUNK)
+                cast_columns(vector_cast, staged["w3_1"], 0, N - SHARE, raw["w3_1"][:, :, : N - SHARE])
+                cast_columns(gpsimd_cast, staged["prior_1"], SHARE, 2 * SHARE, raw["prior_1"][:, :, SHARE : 2 * SHARE])
+            elif i == 4:
+                file_codes("prior_1", 0, quantize("prior_1a", staged["prior_1"][:, : 2 * M], AT_GATE[4, 1]))
+                cast_columns(gpsimd_cast, staged["w3_0"], 0, SHARE, raw["w3_0"][:, :, :SHARE])
             elif i == 5:
-                larger("z_0", 0, 0, M, kib)
-                cast_rows(gpsimd_cast, "w3_1", N - SHARE, N, share_kib)
-            elif i == 6:
-                cast_rows(nc.vector.tensor_copy, "w3_1", 0, N - 2 * SHARE, kib)
-                cast_rows(gpsimd_cast, "w3_1", N - 2 * SHARE, N - SHARE, share_kib)
+                staged["z_0"] = larger(0, 0, M, AT_GATE[5, 1])
+                cast_columns(gpsimd_cast, staged["w3_0"], SHARE, 2 * SHARE, raw["w3_0"][:, :, SHARE : 2 * SHARE])
             else:
-                name = "w3_0" if i == 2 else "prior_1"
-                cast_rows(nc.vector.tensor_copy, name, 0, N - SHARE, kib)
-                cast_rows(gpsimd_cast, name, N - SHARE, N, share_kib)
+                cast_columns(vector_cast, staged["w3_0"], 2 * SHARE, N, raw["w3_0"][:, :, 2 * SHARE :])
+                cast_columns(gpsimd_cast, staged["w3_1"], N - SHARE, N, raw["w3_1"][:, :, N - SHARE :])
 
         pick_withdrawal(LAST, 0, M // 2)
-        for lo, kib in zip(range(M // 2, M, CHUNK), AT_LATE_WITHDRAWAL):
+        for lo, kib in zip(range(M // 2, M, CHUNK), (AT_GATE[7, 1] - 1, AT_GATE[7, 1] + 1)):
             withdrawal[1, lo] = place([P, PACK, CHUNK], F32, "withdrawal_%d" % lo, kib)
             for i in range(PACK, ROW_TILES):
                 pick_withdrawal(i, lo, lo + CHUNK)
-        for lo in range(0, M, M // 2):
-            pick_hop(LAST, lo, lo + M // 2)
 
-        def y_pass(bank, n0, weights, moving, start, stop):
+        def y_pass(bank, weights, moving, start, stop):
             nc.tensor.matmul_mx(
-                out=bank,
-                lhsT=weights[0][:, n0 : n0 + P].bitcast(FP8X4),
-                lhsT_scale=weights[1][:, n0 : n0 + P],
-                rhs=moving[0].bitcast(FP8X4),
-                rhs_scale=moving[1],
-                start=start,
-                stop=stop,
+                out=bank, lhsT=weights[0], lhsT_scale=weights[1], rhs=moving[0], rhs_scale=moving[1], start=start, stop=stop
             )
 
-        def columns(name, lo):
-            return [plane[:, lo : lo + CHUNK] for plane in codes[name][:2]]
-
         for b in range(PASSES):
-            codes["w4_%d" % b] = (w4_w[:, b, :], w4_s[:, b, :].bitcast(U8), 0)
-        chunks = range(0, M, CHUNK)
-        pieces = [(lo, 0, N) for lo in chunks[:-1]] + [(M - CHUNK, 0, N // 2), (M - CHUNK, N // 2, N)]
+            file_codes("w4_%d" % b, 0, (w4_w[:, b, :], w4_s[:, b, :].bitcast(U8)))
+        chunks = M // CHUNK
+        tiles = N // P
+        pieces = [(c, 0, tiles) for c in range(chunks - 1)] + [(chunks - 1, 0, tiles // 2), (chunks - 1, tiles // 2, tiles)]
         y_ps = {}
-        for (lo, n_lo, n_hi), bank in zip(pieces, Y_BANKS):
-            y_ps[lo, n_lo] = bank_tile([P, (n_hi - n_lo) // P, CHUNK], "y_%d_%d" % (lo, n_lo), bank)
-            for weights, moving in (("w3_0", "z_0"), ("w4_0", "prior_0"), ("w4_1", "prior_1")):
-                for n0 in range(n_lo, n_hi, P):
-                    part = y_ps[lo, n_lo][:, (n0 - n_lo) // P, :]
-                    y_pass(part, n0, codes[weights], columns(moving, lo), weights == "w3_0" and n0 == n_lo, False)
+        for weights, moving in (("w4_0", "prior_0"), ("w4_1", "prior_1"), ("w3_0", "z_0")):
+            for (c, j0, j1), bank in zip(pieces, Y_BANKS):
+                if weights == "w4_0":
+                    y_ps[c, j0] = bank_tile([P, j1 - j0, CHUNK], "y_%d_%d" % (c, j0), bank)
+                for j in range(j0, j1):
+                    y_pass(y_ps[c, j0][:, j - j0, :], codes[weights, j], codes[moving, c], weights == "w4_0" and j == j0, False)
 
         def finish(chunk):
-            name = "z_1_%d" % chunk
-            quantize(name)
-            for lo, n_lo, n_hi in pieces:
-                if lo == chunk:
-                    for n0 in range(n_lo, n_hi, P):
-                        part = y_ps[lo, n_lo][:, (n0 - n_lo) // P, :]
-                        y_pass(part, n0, codes["w3_1"], columns(name, 0), False, n0 == n_hi - P)
-                    result = keep.tile([P, (n_hi - n_lo) // P, CHUNK], F32, name="result_%d_%d" % (lo, n_lo))
-                    nc.scalar.activation(result[:], y_ps[lo, n_lo][:], ACT.Sin)
-                    nc.sync.dma_start(out[n_lo:n_hi, lo : lo + CHUNK].rearrange("(j p) m -> p j m", p=P), result[:])
+            file_codes("z_1", chunk, quantize("z_1_%d" % chunk, staged["z_1", chunk]))
+            for c, j0, j1 in pieces:
+                if c == chunk:
+                    for j in range(j0, j1):
+                        y_pass(y_ps[c, j0][:, j - j0, :], codes["w3_1", j], codes["z_1", c], False, j == j1 - 1)
+                    result = keep.tile([P, j1 - j0, CHUNK], F32, name="result_%d_%d" % (c, j0))
+                    nc.scalar.activation(result[:], y_ps[c, j0][:], ACT.Sin)
+                    rows = out[P * j0 : P * j1, CHUNK * c : CHUNK * (c + 1)]
+                    nc.sync.dma_start(rows.rearrange("(j p) m -> p j m", p=P), result[:])
 
-        for lo in chunks:
-            larger("z_1_%d" % lo, 1, lo, lo + CHUNK, AT_LAST_Z + lo // CHUNK)
-            if lo == CHUNK:
-                quantize("w3_1", AT_DEPOSIT + 2 * LAST)
-            if lo > 0:
-                finish(lo - CHUNK)
-        finish(M - CHUNK)
+        pick_hop(LAST, 0, CHUNK)
+        pick_hop(LAST, CHUNK, 2 * CHUNK)
+        for c in range(chunks):
+            staged["z_1", c] = larger(1, CHUNK * c, CHUNK * (c + 1), AT_LAST_Z + c)
+            if c == 0:
+                file_codes("w3_1", 0, quantize("w3_1", staged["w3_1"]))
+            if c == chunks - 1:
+                finish(c - 1)
+                finish(c)
+            elif c + 2 < chunks:
+                pick_hop(LAST, CHUNK * (c + 2), CHUNK * (c + 3))
+                finish(c)

@@ -170,14 +170,16 @@ def tile_list_layering_chain_features_kernel(
         def gpsimd_cast(out, in_):
             nc.gpsimd.tensor_scalar(out, in_, 1.0, 0.0, ALU.mult, ALU.add)
 
-        def cast_w2(copy, b, a, t0, t1, kib):
-            staged = place([P, (t1 - t0) * P * PACK], BF16, "w2_%d%d%d_bf" % (b, a, t0), kib)
-            piece = staged[:].rearrange("p (t c e i) -> p c t i e", e=4, i=PACK, t=t1 - t0)
+        def cast_w2(copy, b, a, t0, t1, staged):
+            piece = staged.rearrange("p (t c e i) -> p c t i e", e=4, i=PACK, t=t1 - t0)
             rows = raw["w2_%d%d" % (b, a)][:].rearrange("p i (c t e) -> p c t i e", t=PACK, e=4)[:, :, t0:t1]
             if t1 - t0 == 1:
                 piece, rows = piece[:, :, 0], rows[:, :, 0]
             copy(piece, rows)
-            return staged[:]
+            return staged
+
+        def stage_w2(name, tiles, kib):
+            return place([P, tiles * SPAN], BF16, name + "_bf", kib)[:]
 
         def cast_columns(copy, staged, lo, hi, rows):
             copy(
@@ -308,13 +310,15 @@ def tile_list_layering_chain_features_kernel(
             if (i, hi) == (0, S):
                 pick_deposit(0)
         pick_deposit(1)
-        file_codes("w2_00", 0, quantize("w2_00", cast_w2(nc.vector.tensor_copy, 0, 0, 0, PACK, AT_FIRST_CAST)))
+        file_codes("w2_00", 0, quantize("w2_00", cast_w2(nc.vector.tensor_copy, 0, 0, 0, PACK, stage_w2("w2_00", PACK, AT_FIRST_CAST))))
         load_rows("prior_1", prior[SPAN:, :], AT_PRIOR_1)
-        tile_0 = cast_w2(nc.vector.tensor_copy, 0, 1, 0, 1, AT_SECOND_CASTS[0])
-        tiles_1_2 = cast_w2(nc.vector.tensor_copy, 0, 1, 1, 3, AT_SECOND_CASTS[1])
+        tile_0 = cast_w2(nc.vector.tensor_copy, 0, 1, 0, 1, stage_w2("w2_01_0", 1, AT_SECOND_CASTS[0]))
+        tiles_1_2 = stage_w2("w2_01_1", 2, AT_SECOND_CASTS[1])
+        cast_w2(nc.vector.tensor_copy, 0, 1, 1, 2, tiles_1_2[:, :SPAN])
         file_codes("w2_01", 0, quantize("w2_01_0", tile_0))
-        tile_3 = cast_w2(gpsimd_cast, 0, 1, 3, PACK, AT_SECOND_CASTS[0])
+        cast_w2(nc.vector.tensor_copy, 0, 1, 2, 3, tiles_1_2[:, SPAN:])
         file_codes("w2_01", 1, quantize("w2_01_1", tiles_1_2))
+        tile_3 = cast_w2(gpsimd_cast, 0, 1, 3, PACK, stage_w2("w2_01_3", 1, AT_SECOND_CASTS[1]))
 
         vector_cast = nc.vector.tensor_copy
         for i in range(ROW_TILES):
@@ -339,18 +343,18 @@ def tile_list_layering_chain_features_kernel(
             elif i == 5:
                 file_codes("prior_1", 2, quantize("prior_1b", staged["prior_1"][:, 2 * M :], AT_GATE[5, 0]))
             elif i == 6:
-                file_codes("z_0", 0, quantize("z_0", staged["z_0"], AT_GATE[6, 0]))
+                file_codes("z_0", 0, quantize("z_0", staged["z_0"][:, : 2 * SPAN], AT_GATE[6, 0]))
             else:
                 file_codes("w3_0", 0, quantize("w3_0", staged["w3_0"], AT_GATE[7, 0]))
                 break
             pick_hop(i, 0, M)
             if i == 0:
-                staged["w2_10"] = cast_w2(vector_cast, 1, 0, 0, PACK, AT_GATE[0, 1])
+                staged["w2_10"] = cast_w2(vector_cast, 1, 0, 0, PACK, stage_w2("w2_10", PACK, AT_GATE[0, 1]))
                 cast_columns(gpsimd_cast, staged["prior_0"], 0, SHARE, raw["prior_0a"][:])
                 load_w3(1)
                 load_w3(0)
             elif i == 1:
-                staged["w2_11"] = cast_w2(vector_cast, 1, 1, 0, PACK, AT_GATE[1, 1])
+                staged["w2_11"] = cast_w2(vector_cast, 1, 1, 0, PACK, stage_w2("w2_11", PACK, AT_GATE[1, 1]))
                 cast_columns(gpsimd_cast, staged["prior_0"], SHARE, 2 * SHARE, raw["prior_0b"][:, :, :SHARE])
                 w4_w = place([P, PASSES, N], I32, "w4_w", AT_W4_WORDS)
                 nc.sync.dma_start(
@@ -397,9 +401,17 @@ def tile_list_layering_chain_features_kernel(
                 if weights == "w4_0":
                     y_ps[c, j0] = bank_tile([P, j1 - j0, CHUNK], "y_%d_%d" % (c, j0), bank)
                 for j in range(j0, j1):
-                    y_pass(y_ps[c, j0][:, j - j0, :], codes[weights, j], codes[moving, c], weights == "w4_0" and j == j0, False)
+                    if (moving, c) in codes:
+                        y_pass(y_ps[c, j0][:, j - j0, :], codes[weights, j], codes[moving, c], weights == "w4_0" and j == j0, False)
 
         def finish(chunk):
+            if ("z_0", chunk) not in codes:
+                part = staged["z_0"][:, SPAN * chunk : SPAN * (chunk + 1)]
+                file_codes("z_0", chunk, quantize("z_0_%d" % chunk, part, AT_LAST_Z + chunk - 1))
+                for c, j0, j1 in pieces:
+                    if c == chunk:
+                        for j in range(j0, j1):
+                            y_pass(y_ps[c, j0][:, j - j0, :], codes["w3_0", j], codes["z_0", c], False, False)
             file_codes("z_1", chunk, quantize("z_1_%d" % chunk, staged["z_1", chunk]))
             for c, j0, j1 in pieces:
                 if c == chunk:
@@ -416,9 +428,6 @@ def tile_list_layering_chain_features_kernel(
             staged["z_1", c] = larger(1, CHUNK * c, CHUNK * (c + 1), AT_LAST_Z + c)
             if c == 0:
                 file_codes("w3_1", 0, quantize("w3_1", staged["w3_1"]))
-            if c == chunks - 1:
-                finish(c - 1)
-                finish(c)
-            elif c + 2 < chunks:
+            if c + 2 < chunks:
                 pick_hop(LAST, CHUNK * (c + 2), CHUNK * (c + 3))
-                finish(c)
+            finish(c)

@@ -38,12 +38,13 @@ AT_W3 = (16, 24)
 AT_W4_WORDS, AT_W4_SCALES = 46, 50
 AT_SECOND_CASTS = (54, 55)
 AT_GATE = {
-    (0, 0): 57, (1, 0): 59, (2, 0): 62, (3, 0): 65, (5, 0): 67, (6, 0): 69, (7, 0): 71,
+    (0, 0): 57, (1, 0): 60, (2, 0): 63, (3, 0): 65, (5, 0): 67, (6, 0): 69, (7, 0): 71,
     (0, 1): 73, (1, 1): 77, (4, 1): 81, (5, 1): 83, (7, 1): 88,
 }
 AT_SQUARES = 91
 AT_X2 = 99
 AT_LAST_Z = 115
+WARM_PASSES = 6
 SHARE = 192
 
 
@@ -111,7 +112,7 @@ def tile_list_layering_chain_features_kernel(
             nc.gpsimd.dma_start(loaded_s[s:P:32, :, :], scale_rows(w1_scales)[s])
         v_s = keep.tile([P, PASSES, S], U8, name="v_s", align_bytes=64)
 
-        picked_s = keep.tile([P, PASSES, S], U8, name="picked_s")
+        picked_s = keep.tile([P, PASSES, S], U8, name="picked_s", align_bytes=64)
         for a in range(PASSES):
             nc.vector.tensor_copy(picked_s[:, a, :], tab_s[:, T * a : T * (a + 1)].indirect(idx[:]))
         for s in range(4):
@@ -135,6 +136,17 @@ def tile_list_layering_chain_features_kernel(
         halves = ((0, BANK), (BANK, S))
         quarters = ((0, BANK // 2), (BANK // 2, BANK))
         pick_words(0, halves)
+        idle = bank_tile([P, BANK], "idle", 7)
+        for step in range(WARM_PASSES):
+            nc.tensor.matmul_mx(
+                out=idle[:],
+                lhsT=w1_w[0][:, : P // 2].bitcast(FP4X4),
+                lhsT_scale=picked_s[:, 0, :P],
+                rhs=v_w[0][:, :BANK].bitcast(FP8X4),
+                rhs_scale=picked_s[:, 1, :BANK],
+                start=True,
+                stop=True,
+            )
 
         w1_s = place([P, PASSES * H // 4], I32, "w1_s", AT_W1_SCALES)
         nc.vector.tensor_copy(
@@ -163,9 +175,9 @@ def tile_list_layering_chain_features_kernel(
         pick_words(1, quarters + halves[1:])
         load_w2(1, 0)
         load_rows("prior_0a", prior[:SPAN, :SHARE], AT_PRIOR_0[0])
+        load_w1(1, place([P, PASSES, SPAN // 2], I32, "w1_raw1", AT_W1_LATE))
         load_w2(1, 1)
         load_rows("prior_0b", prior[:SPAN, SHARE:], AT_PRIOR_0[1])
-        load_w1(1, place([P, PASSES, SPAN // 2], I32, "w1_raw1", AT_W1_LATE))
 
         def gpsimd_cast(out, in_):
             nc.gpsimd.tensor_scalar(out, in_, 1.0, 0.0, ALU.mult, ALU.add)
@@ -332,10 +344,10 @@ def tile_list_layering_chain_features_kernel(
             if i == 0:
                 file_codes("w2_01", 3, quantize("w2_01_3", tile_3, AT_GATE[0, 0]))
             elif i == 1:
-                file_codes("w2_10", 0, quantize("w2_10", staged["w2_10"], AT_GATE[1, 0]))
+                file_codes("w2_10", 0, quantize("w2_10", staged["w2_10"], AT_GATE[1, 0] - 1))
+                order_w1(1, place([P, SPAN], I32, "w1_w1", AT_GATE[1, 0] + 1))
             elif i == 2:
-                file_codes("w2_11", 0, quantize("w2_11", staged["w2_11"], AT_GATE[2, 0] - 1))
-                order_w1(1, place([P, SPAN], I32, "w1_w1", AT_GATE[2, 0] + 1))
+                file_codes("w2_11", 0, quantize("w2_11", staged["w2_11"], AT_GATE[2, 0]))
             elif i == 3:
                 file_codes("prior_0", 0, quantize("prior_0", staged["prior_0"], AT_GATE[3, 0]))
             elif i == 4:

from contextlib import ExitStack

import concourse.mybir as mybir

K, H, N, T, S, M = 1024, 1024, 512, 4096, 1024, 512
FLOPS = 2 * (2 * K * H * S + 2 * H * N * M)

F32 = mybir.dt.float32
BF16 = mybir.dt.bfloat16
I32 = mybir.dt.int32
U32 = mybir.dt.uint32
U16 = mybir.dt.uint16
U8 = mybir.dt.uint8
FP8X4 = mybir.dt.float8_e4m3fn_x4
FP4X4 = mybir.dt.float4_e2m1fn_x4
ACT = mybir.ActivationFunctionType
ALU = mybir.AluOpType

P = 128
PACK = 4
PASSES = 2
SPAN = P * PACK
BANK = 512
ROW_TILES = PASSES * PACK
LAST = ROW_TILES - 1
CHUNK = 128
PAIRS = 4
Y_BANKS = (0, 1, 2, 3, 6)

AT_TABLE = (8, 31)
AT_W1_SCALES = 8
AT_W2 = ((0, 16), (24, 46))
AT_PRIOR_0 = (32, 35)
AT_W1_LATE = 40
AT_FIRST_CAST = 42
AT_PRIOR_1 = 0
AT_W3 = (16, 24)
AT_W4_WORDS, AT_W4_SCALES = 46, 50
AT_SECOND_CASTS = (54, 55)
AT_GATE = {
    (0, 0): 57, (1, 0): 60, (2, 0): 63, (3, 0): 65, (5, 0): 67, (6, 0): 69, (7, 0): 71,
    (0, 1): 73, (1, 1): 77, (4, 1): 81, (5, 1): 83, (7, 1): 88,
}
AT_SQUARES = 91
AT_X2 = 99
AT_LAST_Z = 115
WARM_PASSES = 6
SHARE = 192


def tile_list_layering_chain_features_kernel(
    tc, tab_words, tab_scales, offs, pos1, pos2, pos3, w1_words, w1_scales,
    w2, w3, w4_words, w4_scales, prior, out
):
    nc = tc.nc
    with ExitStack() as ctx:
        lists = ctx.enter_context(tc.tile_pool(name="lists", bufs=1))
        keep = ctx.enter_context(tc.tile_pool(name="keep", bufs=1))
        laid = ctx.enter_context(tc.tile_pool(name="laid", bufs=1))
        psum = ctx.enter_context(tc.psum_pool(name="psum", bufs=1))

        def place(shape, dtype, name, kib):
            return laid.tile(shape, dtype, name=name, align_bytes=64, offset=int(1024 * kib))

        def bank_tile(shape, name, bank):
            return psum.tile(shape, F32, name=name, offset=4 * BANK * bank)

        def scale_rows(scales):
            return scales.bitcast(I32).rearrange("a (q s) n -> s q a n", s=4)

        tab_s = place([P, PASSES * T], U8, "tab_s", AT_W2[0][0])
        loaded_s = keep.tile([P, PASSES, H // 4], I32, name="loaded_s", align_bytes=64)
        nc.vector.memset(tab_s[:, :T].bitcast(I32), 0)
        nc.gpsimd.memset(tab_s[:, T:].bitcast(I32), 0)
        nc.vector.memset(loaded_s[:], 0)

        warm = keep.tile([P, 2], F32, name="warm")
        nc.vector.memset(warm[:, 0:1], 0.0)
        nc.scalar.activation(warm[:, 1:2], warm[:, 0:1], ACT.Silu)

        idx = lists.tile([P, S // 16], U16, name="idx")
        p1 = lists.tile([P, M // 16], U16, name="p1")
        p2 = lists.tile([P, M // 16], U16, name="p2")
        p3 = lists.tile([P, M // 16], U16, name="p3")
        tab_w = [place([P, T], I32, "tab_w%d" % a, AT_TABLE[a]) for a in range(PASSES)]

        def load_table_words(a, lo, hi):
            cols = slice(lo, hi)
            nc.sync.dma_start(tab_w[a][:, cols], tab_words[a].rearrange("p t i -> p (t i)").bitcast(I32)[:, cols])

        nc.sync.dma_start(idx[:], offs)
        load_table_words(0, 0, T // 4)
        nc.sync.dma_start(
            tab_s[4:P:8, :].bitcast(I32).rearrange("m (a n) -> m a n", a=PASSES),
            tab_scales.bitcast(I32).rearrange("a m n -> m a n"),
        )
        w1_raw, w1_w = {}, {}

        def load_w1(b, tile):
            w1_raw[b] = tile
            words = w1_words.bitcast(I32).rearrange("a p c -> p a c")
            nc.sync.dma_start(tile[:], words[:, :, SPAN // 2 * b : SPAN // 2 * (b + 1)])

        load_w1(0, keep.tile([P, PASSES, SPAN // 2], I32, name="w1_raw0"))
        load_table_words(0, T // 4, T)
        nc.sync.dma_start(p1[:], pos1)
        nc.sync.dma_start(p2[:], pos2)
        load_table_words(1, 0, T // 2)
        load_table_words(1, T // 2, T)
        nc.sync.dma_start(p3[:], pos3)
        for s in range(4):
            nc.gpsimd.dma_start(loaded_s[s:P:32, :, :], scale_rows(w1_scales)[s])
        v_s = keep.tile([P, PASSES, S], U8, name="v_s", align_bytes=64)

        picked_s = keep.tile([P, PASSES, S], U8, name="picked_s", align_bytes=64)
        for a in range(PASSES):
            nc.vector.tensor_copy(picked_s[:, a, :], tab_s[:, T * a : T * (a + 1)].indirect(idx[:]))
        for s in range(4):
            nc.sync.dma_start(v_s[s:P:32, :, :].bitcast(I32), picked_s[8 * s + 4 : P : 32, :, :].bitcast(I32))

        def order_w1(b, tile):
            w1_w[b] = tile
            nc.vector.tensor_copy(
                tile[:].rearrange("p (a t c w) -> p a t c w", a=PASSES, t=PACK, w=2),
                w1_raw[b][:].rearrange("p a (c t w) -> p a t c w", t=PACK, w=2),
            )

        order_w1(0, keep.tile([P, SPAN], I32, name="w1_w0", align_bytes=64))
        v_w = {}

        def pick_words(a, cuts):
            v_w[a] = keep.tile([P, S], U32, name="v_w%d" % a, align_bytes=64)
            for lo, hi in cuts:
                nc.vector.tensor_copy(v_w[a][:, lo:hi], tab_w[a][:].bitcast(U32).indirect(idx[:, lo // 16 : hi // 16]))

        halves = ((0, BANK), (BANK, S))
        quarters = ((0, BANK // 2), (BANK // 2, BANK))
        pick_words(0, halves)
        idle = bank_tile([P, BANK], "idle", 7)
        for step in range(WARM_PASSES):
            nc.tensor.matmul_mx(
                out=idle[:],
                lhsT=w1_w[0][:, : P // 2].bitcast(FP4X4),
                lhsT_scale=picked_s[:, 0, :P],
                rhs=v_w[0][:, :BANK].bitcast(FP8X4),
                rhs_scale=picked_s[:, 1, :BANK],
                start=True,
                stop=True,
            )

        w1_s = place([P, PASSES * H // 4], I32, "w1_s", AT_W1_SCALES)
        nc.vector.tensor_copy(
            w1_s[:].rearrange("p (f t c) -> p f t c", f=4, t=PACK),
            loaded_s[:].rearrange("p a (b c t) -> p (a b) t c", b=PASSES, t=PACK),
        )

        raw = {}

        def load_rows(name, rows, kib):
            raw[name] = place([P, PACK, rows.shape[1]], F32, name + "_raw", kib)
            nc.sync.dma_start(raw[name][:], rows.rearrange("(p i) c -> p i c", i=PACK))

        def load_w2(b, a):
            load_rows("w2_%d%d" % (b, a), w2[SPAN * a : SPAN * (a + 1), SPAN * b : SPAN * (b + 1)], AT_W2[b][a])

        def load_w3(b):
            name = "w3_%d" % b
            raw[name] = place([P, PACK, N], F32, name + "_raw", AT_W3[b])
            by_slot = w3[SPAN * b : SPAN * (b + 1), :].rearrange("(c t e) n -> t c e n", t=PACK, e=4)
            for t in range(PACK):
                nc.sync.dma_start(raw[name][:, t, :], by_slot[t])

        load_w2(0, 0)
        load_w2(0, 1)
        pick_words(1, quarters + halves[1:])
        load_w2(1, 0)
        load_rows("prior_0a", prior[:SPAN, :SHARE], AT_PRIOR_0[0])
        load_w1(1, place([P, PASSES, SPAN // 2], I32, "w1_raw1", AT_W1_LATE))
        load_w2(1, 1)
        load_rows("prior_0b", prior[:SPAN, SHARE:], AT_PRIOR_0[1])

        def gpsimd_cast(out, in_):
            nc.gpsimd.tensor_scalar(out, in_, 1.0, 0.0, ALU.mult, ALU.add)

        def cast_w2(copy, b, a, t0, t1, staged):
            piece = staged.rearrange("p (t c e i) -> p c t i e", e=4, i=PACK, t=t1 - t0)
            rows = raw["w2_%d%d" % (b, a)][:].rearrange("p i (c t e) -> p c t i e", t=PACK, e=4)[:, :, t0:t1]
            if t1 - t0 == 1:
                piece, rows = piece[:, :, 0], rows[:, :, 0]
            copy(piece, rows)
            return staged

        def stage_w2(name, tiles, kib):
            return place([P, tiles * SPAN], BF16, name + "_bf", kib)[:]

        def cast_columns(copy, staged, lo, hi, rows):
            copy(
                staged[:, PACK * lo : PACK * hi].rearrange("p (c e t) -> p c t e", e=4, t=PACK),
                rows.rearrange("p t (c e) -> p c t e", e=4),
            )

        def quantize(name, staged, kib=None):
            columns = staged.shape[1] // PACK
            if kib is None:
                words = keep.tile([P, columns], U32, name=name + "_w", align_bytes=64)
            else:
                words = place([P, columns], U32, name + "_w", kib)
            scales = keep.tile([P, columns], U8, name=name + "_s", align_bytes=64)
            nc.vector.quantize_mx(out=words[:].bitcast(FP8X4), scales=scales[:], in_=staged)
            return words, scales

        codes = {}

        def file_codes(name, first, planes):
            words, scales = planes
            for j in range(scales[:].shape[1] // P):
                codes[name, first + j] = (words[:, P * j : P * (j + 1)].bitcast(FP8X4), scales[:, P * j : P * (j + 1)])

        gate, deposit_at, staged = {}, {}, {}
        for name, first, held_by in (("prior_0", 0, (2, 1)), ("prior_1", 2, (4, 0)), ("w3_0", 4, (6, 1))):
            tile = keep.tile([P, 3 * M], F32, name=name + "_stage", align_bytes=64)
            deposit_at[first], deposit_at[first + 1], gate[held_by] = tile[:, :M], tile[:, M : 2 * M], tile[:, 2 * M :]
            start = M - 2 * SHARE
            staged[name] = tile[:, start : start + 2 * N].bitcast(BF16)
        tile = keep.tile([P, 2 * (N - SHARE) + M], F32, name="w3_1_stage", align_bytes=64)
        gate[3, 1], deposit_at[6], staged["w3_1"] = tile[:, :BANK], tile[:, 2 * (N - SHARE) :], tile[:, : 2 * N].bitcast(BF16)
        deposit_at[LAST] = keep.tile([P, M], F32, name="last_deposit")[:]

        u_ps, squares, x2, product, withdrawal = {}, {}, {}, {}, {}

        def first_stage_product(name, bank, lo, hi, passes, stationary):
            sums = bank_tile([P, hi - lo], name, bank)
            for a in passes:
                words, scales = stationary(a)
                nc.tensor.matmul_mx(
                    out=sums[:],
                    lhsT=words,
                    lhsT_scale=scales,
                    rhs=v_w[a][:, lo:hi].bitcast(FP8X4),
                    rhs_scale=v_s[:, a, lo:hi],
                    start=(a == passes[0]),
                    stop=(a == passes[-1]),
                )
            return sums

        def u_product(i):
            b, t = divmod(i, PACK)
            passes = (0, 1) if i == 0 else (1, 0)
            u_ps[i] = [
                first_stage_product(
                    "u_%d_%d" % (i, h), 2 * ((i - 1) % PAIRS) + h, lo, hi, passes, lambda a: codes["w2_%d%d" % (b, a), t]
                )
                for h, (lo, hi) in enumerate(halves)
            ]

        def w1_codes(i, a):
            at = PACK * a + i % PACK
            words = w1_w[i // PACK][:, P // 2 * at : P // 2 * (at + 1)].bitcast(FP4X4)
            at = ROW_TILES * a + i
            return words, w1_s[:, P // 4 * at : P // 4 * (at + 1)].bitcast(U8)

        def x1_product(i, lo, hi, bank, passes):
            return first_stage_product("x1_%d_%d" % (i, lo), bank, lo, hi, passes, lambda a: w1_codes(i, a))

        def out_of_x1(func, i, lo, hi, sums):
            h = lo // BANK
            if func == ACT.Tanh:
                if (i, h) not in gate:
                    gate[i, h] = place([P, BANK], F32, "gate%d%d" % (i, h), AT_GATE[i, h])[:]
                nc.scalar.activation(gate[i, h][:, lo - BANK * h : hi - BANK * h], sums[:], func, scale=0.5)
            else:
                if i not in squares:
                    squares[i] = place([P, S], F32, "squares%d" % i, AT_SQUARES + 4 * (i % 2))
                nc.scalar.activation(squares[i][:, lo:hi], sums[:], func)

        def from_x1(i):
            sums = [x1_product(i, lo, hi, 2 * (i % PAIRS) + h, (1, 0)) for h, (lo, hi) in enumerate(halves)]
            for func in (ACT.Tanh, ACT.Square):
                for h, (lo, hi) in enumerate(halves):
                    out_of_x1(func, i, lo, hi, sums[h])

        def pick_deposit(i):
            nc.scalar.activation(deposit_at[i], squares[i][:].indirect(p1[:]), ACT.Copy, scale=0.5)

        def make_x2(i):
            x2[i] = place([P, S], F32, "x2_%d" % i, AT_X2 + 4 * (i % PACK))
            for h in range(2):
                nc.vector.scalar_tensor_tensor(
                    x2[i][:, BANK * h : BANK * (h + 1)], gate[i, h], 1.0, u_ps[i][h][:], ALU.add, ALU.mult
                )

        withdrawal[0, 0] = keep.tile([P, PACK, M], F32, name="withdrawal0")
        withdrawal[1, 0] = keep.tile([P, PACK, M // 2], F32, name="withdrawal1")

        def pick_withdrawal(i, lo, hi):
            b, t = divmod(i, PACK)
            nc.scalar.activation(withdrawal[b, lo][:, t, :], x2[i][:].indirect(p3[:, lo // 16 : hi // 16]), ACT.Copy, scale=0.5)

        def pick_hop(i, lo, hi):
            b, t = divmod(i, PACK)
            if b not in product:
                product[b] = keep.tile([P, PACK, M], F32, name="product%d" % b)
            picked = x2[i][:].indirect(p2[:, lo // 16 : hi // 16])
            nc.vector.tensor_tensor(product[b][:, t, lo:hi], picked, deposit_at[i][:, lo:hi], ALU.mult)

        def larger(b, lo, hi, kib):
            first = max(start for (c, start) in withdrawal if c == b and start <= lo)
            z = place([P, (hi - lo) * PACK], BF16, "z_%d_%d" % (b, lo), kib)
            nc.vector.tensor_tensor(
                z[:].rearrange("p (c e t) -> p c t e", e=2, t=PACK),
                product[b][:, :, lo:hi].rearrange("p t (c e) -> p c t e", e=2),
                withdrawal[b, first][:, :, lo - first : hi - first].rearrange("p t (c e) -> p c t e", e=2),
                ALU.max,
            )
            return z[:]

        first_steps = [(0, quarters[0], 0), (0, quarters[1], 4), (1, halves[0], 2), (0, halves[1], 1), (1, halves[1], 3)]
        for step, (i, (lo, hi), bank) in enumerate(first_steps):
            sums = x1_product(i, lo, hi, bank, (0, 1) if step < 4 else (1, 0))
            out_of_x1(ACT.Tanh, i, lo, hi, sums)
            out_of_x1(ACT.Square, i, lo, hi, sums)
            if (i, hi) == (0, S):
                pick_deposit(0)
        pick_deposit(1)
        file_codes("w2_00", 0, quantize("w2_00", cast_w2(nc.vector.tensor_copy, 0, 0, 0, PACK, stage_w2("w2_00", PACK, AT_FIRST_CAST))))
        load_rows("prior_1", prior[SPAN:, :], AT_PRIOR_1)
        tile_0 = cast_w2(nc.vector.tensor_copy, 0, 1, 0, 1, stage_w2("w2_01_0", 1, AT_SECOND_CASTS[0]))
        tiles_1_2 = stage_w2("w2_01_1", 2, AT_SECOND_CASTS[1])
        cast_w2(nc.vector.tensor_copy, 0, 1, 1, 2, tiles_1_2[:, :SPAN])
        file_codes("w2_01", 0, quantize("w2_01_0", tile_0))
        cast_w2(nc.vector.tensor_copy, 0, 1, 2, 3, tiles_1_2[:, SPAN:])
        file_codes("w2_01", 1, quantize("w2_01_1", tiles_1_2))
        tile_3 = cast_w2(gpsimd_cast, 0, 1, 3, PACK, stage_w2("w2_01_3", 1, AT_SECOND_CASTS[1]))

        vector_cast = nc.vector.tensor_copy
        for i in range(ROW_TILES):
            u_product(i)
            if 0 < i < LAST:
                from_x1(i + 1)
                pick_deposit(i + 1)
            if i > 0:
                pick_withdrawal(i - 1, 0, M if i <= PACK else M // 2)
            make_x2(i)
            if i == 0:
                file_codes("w2_01", 3, quantize("w2_01_3", tile_3, AT_GATE[0, 0]))
            elif i == 1:
                file_codes("w2_10", 0, quantize("w2_10", staged["w2_10"], AT_GATE[1, 0] - 1))
                order_w1(1, place([P, SPAN], I32, "w1_w1", AT_GATE[1, 0] + 1))
            elif i == 2:
                file_codes("w2_11", 0, quantize("w2_11", staged["w2_11"], AT_GATE[2, 0]))
            elif i == 3:
                file_codes("prior_0", 0, quantize("prior_0", staged["prior_0"], AT_GATE[3, 0]))
            elif i == 4:
                cast_columns(vector_cast, staged["prior_1"], 2 * SHARE, M, raw["prior_1"][:, :, 2 * SHARE :])
            elif i == 5:
                file_codes("prior_1", 2, quantize("prior_1b", staged["prior_1"][:, 2 * M :], AT_GATE[5, 0]))
            elif i == 6:
                file_codes("z_0", 0, quantize("z_0", staged["z_0"][:, : 2 * SPAN], AT_GATE[6, 0]))
            else:
                file_codes("w3_0", 0, quantize("w3_0", staged["w3_0"], AT_GATE[7, 0]))
                break
            pick_hop(i, 0, M)
            if i == 0:
                staged["w2_10"] = cast_w2(vector_cast, 1, 0, 0, PACK, stage_w2("w2_10", PACK, AT_GATE[0, 1]))
                cast_columns(gpsimd_cast, staged["prior_0"], 0, SHARE, raw["prior_0a"][:])
                load_w3(1)
                load_w3(0)
            elif i == 1:
                staged["w2_11"] = cast_w2(vector_cast, 1, 1, 0, PACK, stage_w2("w2_11", PACK, AT_GATE[1, 1]))
                cast_columns(gpsimd_cast, staged["prior_0"], SHARE, 2 * SHARE, raw["prior_0b"][:, :, :SHARE])
                w4_w = place([P, PASSES, N], I32, "w4_w", AT_W4_WORDS)
                nc.sync.dma_start(
                    w4_w[:], w4_words.rearrange("a p c i -> a p (c i)").bitcast(I32).rearrange("a p c -> p a c")
                )
                w4_s = place([P, PASSES, N // 4], I32, "w4_s", AT_W4_SCALES)
                for s in range(4):
                    nc.sync.dma_start(w4_s[s:P:32, :, :], scale_rows(w4_scales)[s])
            elif i == 2:
                cast_columns(vector_cast, staged["prior_0"], 2 * SHARE, M, raw["prior_0b"][:, :, SHARE:])
                cast_columns(gpsimd_cast, staged["prior_1"], 0, SHARE, raw["prior_1"][:, :, :SHARE])
            elif i == 3:
                cast_columns(vector_cast, staged["w3_1"], 0, N - SHARE, raw["w3_1"][:, :, : N - SHARE])
                cast_columns(gpsimd_cast, staged["prior_1"], SHARE, 2 * SHARE, raw["prior_1"][:, :, SHARE : 2 * SHARE])
            elif i == 4:
                file_codes("prior_1", 0, quantize("prior_1a", staged["prior_1"][:, : 2 * M], AT_GATE[4, 1]))
                cast_columns(gpsimd_cast, staged["w3_0"], 0, SHARE, raw["w3_0"][:, :, :SHARE])
            elif i == 5:
                staged["z_0"] = larger(0, 0, M, AT_GATE[5, 1])
                cast_columns(gpsimd_cast, staged["w3_0"], SHARE, 2 * SHARE, raw["w3_0"][:, :, SHARE : 2 * SHARE])
            else:
                cast_columns(vector_cast, staged["w3_0"], 2 * SHARE, N, raw["w3_0"][:, :, 2 * SHARE :])
                cast_columns(gpsimd_cast, staged["w3_1"], N - SHARE, N, raw["w3_1"][:, :, N - SHARE :])

        pick_withdrawal(LAST, 0, M // 2)
        for lo, kib in zip(range(M // 2, M, CHUNK), (AT_GATE[7, 1] - 1, AT_GATE[7, 1] + 1)):
            withdrawal[1, lo] = place([P, PACK, CHUNK], F32, "withdrawal_%d" % lo, kib)
            for i in range(PACK, ROW_TILES):
                pick_withdrawal(i, lo, lo + CHUNK)

        def y_pass(bank, weights, moving, start, stop):
            nc.tensor.matmul_mx(
                out=bank, lhsT=weights[0], lhsT_scale=weights[1], rhs=moving[0], rhs_scale=moving[1], start=start, stop=stop
            )

        for b in range(PASSES):
            file_codes("w4_%d" % b, 0, (w4_w[:, b, :], w4_s[:, b, :].bitcast(U8)))
        chunks = M // CHUNK
        tiles = N // P
        pieces = [(c, 0, tiles) for c in range(chunks - 1)] + [(chunks - 1, 0, tiles // 2), (chunks - 1, tiles // 2, tiles)]
        y_ps = {}
        for weights, moving in (("w4_0", "prior_0"), ("w4_1", "prior_1"), ("w3_0", "z_0")):
            for (c, j0, j1), bank in zip(pieces, Y_BANKS):
                if weights == "w4_0":
                    y_ps[c, j0] = bank_tile([P, j1 - j0, CHUNK], "y_%d_%d" % (c, j0), bank)
                for j in range(j0, j1):
                    if (moving, c) in codes:
                        y_pass(y_ps[c, j0][:, j - j0, :], codes[weights, j], codes[moving, c], weights == "w4_0" and j == j0, False)

        def finish(chunk):
            if ("z_0", chunk) not in codes:
                part = staged["z_0"][:, SPAN * chunk : SPAN * (chunk + 1)]
                file_codes("z_0", chunk, quantize("z_0_%d" % chunk, part, AT_LAST_Z + chunk - 1))
                for c, j0, j1 in pieces:
                    if c == chunk:
                        for j in range(j0, j1):
                            y_pass(y_ps[c, j0][:, j - j0, :], codes["w3_0", j], codes["z_0", c], False, False)
            file_codes("z_1", chunk, quantize("z_1_%d" % chunk, staged["z_1", chunk]))
            for c, j0, j1 in pieces:
                if c == chunk:
                    for j in range(j0, j1):
                        y_pass(y_ps[c, j0][:, j - j0, :], codes["w3_1", j], codes["z_1", c], False, j == j1 - 1)
                    result = keep.tile([P, j1 - j0, CHUNK], F32, name="result_%d_%d" % (c, j0))
                    nc.scalar.activation(result[:], y_ps[c, j0][:], ACT.Sin)
                    rows = out[P * j0 : P * j1, CHUNK * c : CHUNK * (c + 1)]
                    nc.sync.dma_start(rows.rearrange("(j p) m -> p j m", p=P), result[:])

        pick_hop(LAST, 0, CHUNK)
        pick_hop(LAST, CHUNK, 2 * CHUNK)
        for c in range(chunks):
            staged["z_1", c] = larger(1, CHUNK * c, CHUNK * (c + 1), AT_LAST_Z + c)
            if c == 0:
                file_codes("w3_1", 0, quantize("w3_1", staged["w3_1"]))
            if c + 2 < chunks:
                pick_hop(LAST, CHUNK * (c + 2), CHUNK * (c + 3))
            finish(c)
